import numpy as np
import ml_dtypes


def mxq(x, axis, fmt="e4m3"):
    dtype, down = {"e4m3": (ml_dtypes.float8_e4m3fn, 7), "e5m2": (ml_dtypes.float8_e5m2, 14)}[fmt]
    v = np.moveaxis(np.asarray(x, np.float32).astype(ml_dtypes.bfloat16).astype(np.float64), axis, -1)
    blocks = v.reshape(v.shape[:-1] + (-1, 32))
    amax = np.abs(blocks).max(-1, keepdims=True)
    byte = np.maximum(np.where(amax > 0, np.frexp(amax)[1] - 1 + 127, 0) - down, 1)
    scale = np.exp2(byte - 127.0)
    codes = (blocks / scale).astype(np.float32).astype(dtype).astype(np.float64)
    return np.moveaxis((codes * scale).reshape(v.shape), -1, axis)


WIDE = False


def mx_kscale(k):
    if not WIDE:
        return np.ones(k)
    levels = np.array([10, -10, 5, -5, 0])
    if k % 512:
        return np.exp2(np.random.permutation(np.resize(levels, k // 32))).repeat(32)
    a = np.empty((k // 512, 16))
    for p in range(k // 512):
        a[p, :8] = np.random.permutation(np.resize(levels, 8))
        for g in range(8):
            far = levels[np.abs(levels - a[p, g]) >= 10]
            a[p, g + 8] = far[np.random.randint(len(far))]
    return np.exp2(a.ravel()).repeat(32)


def f64(x):
    return np.asarray(x).astype(np.float64)


def striped(idx):
    return np.tile(idx.reshape(-1, 16).T, (8, 1)).astype(np.uint16)


def unstriped(offs):
    return offs[:16].T.reshape(-1).astype(np.int64)


def relu(v):
    return np.maximum(v, 0.0)


K, T, D, V, H, N = 1536, 512, 6, 256, 512, 256
P = 2 ** 7


def setup_inputs():
    n = np.random.standard_normal
    s = mx_kscale(K)[:, None]
    u = mx_kscale(H)
    return {
        "xT": (n((K, T)) * s).astype(np.float32),
        "w1": (n((K, H)) / np.sqrt(K) / s * u).astype(np.float32),
        "w2": (n((H, N)) / np.sqrt(H) / u[:, None]).astype(np.float32),
        "gate": np.tile(np.random.uniform(0.2, 1.0, (D, 1, V)) / np.sqrt(D), (1, P, 1)).astype(np.float32),
        "pos1": striped(np.random.permutation(T)[:V]),
        "pos2": striped(np.random.permutation(T)[:V]),
        "pos3": striped(np.random.permutation(T)[:V]),
        "pos4": striped(np.random.permutation(T)[:V]),
        "pos5": striped(np.random.permutation(T)[:V]),
        "pos6": striped(np.random.permutation(T)[:V]),
    }


def reference(xT, w1, w2, gate, pos1, pos2, pos3, pos4, pos5, pos6):
    h = relu(mxq(f64(w1), 0, "e4m3").T @ mxq(f64(xT), 0, "e4m3"))
    z = sum(f64(gate)[d, :1] * h[:, unstriped(p)] for d, p in enumerate((pos1, pos2, pos3, pos4, pos5, pos6)))
    return mxq(f64(w2), 0, "e4m3").T @ mxq(z, 0, "e4m3")

@@ -1,0 +1,237 @@
+from contextlib import ExitStack
+
+import concourse.mybir as mybir
+from concourse.masks import make_identity
+
+K, T, D, V, H, N = 1536, 512, 6, 256, 512, 256
+FLOPS = 2 * K * H * T + 2 * H * N * V
+
+F32 = mybir.dt.float32
+BF16 = mybir.dt.bfloat16
+U32 = mybir.dt.uint32
+U16 = mybir.dt.uint16
+U8 = mybir.dt.uint8
+FP8X4 = mybir.dt.float8_e4m3fn_x4
+RELU = mybir.ActivationFunctionType.Relu
+MULT = mybir.AluOpType.mult
+
+P = 128
+J = 4
+KP = P * J
+PASSES = K // KP
+CB = H // P
+VH = V // P
+
+
+def interleave(copy, grouped, raw):
+    copy(
+        out=grouped.rearrange("p (c i) j -> p c j i", i=4),
+        in_=raw.rearrange("p j (c i) -> p c j i", i=4),
+    )
+
+
+def quantize(nc, codes, scales, grouped):
+    nc.vector.quantize_mx(
+        out=codes.bitcast(FP8X4), scales=scales, in_=grouped.rearrange("p c j -> p (c j)")
+    )
+
+
+def tile_picked_gcn_mlp_relu_sub_l_kernel(
+    tc, xT, w1, w2, gate, pos1, pos2, pos3, pos4, pos5, pos6, out
+):
+    nc = tc.nc
+    with ExitStack() as ctx:
+        keep = ctx.enter_context(tc.tile_pool(name="keep", bufs=1))
+        prods = ctx.enter_context(tc.tile_pool(name="prods", bufs=12))
+        psum_h = ctx.enter_context(tc.psum_pool(name="psum_h", bufs=2))
+        psum_z = ctx.enter_context(tc.psum_pool(name="psum_z", bufs=4))
+        psum_m = ctx.enter_context(tc.psum_pool(name="psum_m", bufs=2))
+
+        gate_all = []
+
+        def load_gate(first, last):
+            t = keep.tile([P, last - first, V], F32, name=f"gate{first}")
+            nc.sync.dma_start(out=t[:], in_=gate[first:last].rearrange("d p v -> p d v"))
+            for i in range(last - first):
+                gate_all.append(t[:, i, :])
+
+        w1_raw = [[], [], [], []]
+
+        def load_w1(b, g):
+            t = keep.tile([P, J, P], F32, name=f"w1_raw{b}_{g}")
+            nc.sync.dma_start(out=t[:], in_=w1[g * KP : (g + 1) * KP, b * P : (b + 1) * P].rearrange("(p j) c -> p j c", j=J))
+            w1_raw[b].append(t)
+
+        x_raw = []
+
+        def load_x(g):
+            t = keep.tile([P, J, T], F32, name=f"x_raw{g}")
+            nc.sync.dma_start(out=t[:], in_=xT[g * KP : (g + 1) * KP, :].rearrange("(p j) t -> p j t", j=J))
+            x_raw.append(t)
+
+        lists = []
+
+        def load_list():
+            d = len(lists)
+            t = keep.tile([P, V // 16], U16, name=f"list{d}")
+            nc.sync.dma_start(t[:], (pos1, pos2, pos3, pos4, pos5, pos6)[d])
+            lists.append(t)
+
+        for g in range(PASSES):
+            load_w1(0, g)
+        load_list()
+        load_list()
+        for g in range(PASSES):
+            load_x(g)
+        for d in range(4):
+            load_list()
+        load_gate(0, 4)
+        for g in range(PASSES):
+            load_w1(1, g)
+        load_gate(4, 6)
+        for b in (2, 3):
+            for g in range(PASSES):
+                load_w1(b, g)
+        w2_raw = keep.tile([P, J, N], F32)
+        nc.sync.dma_start(out=w2_raw[:], in_=w2.rearrange("(p j) m -> p j m", j=J))
+
+        ident = keep.tile([P, P], F32)
+        make_identity(nc, ident[:])
+
+        def prepare_w1(c, copies):
+            codes = keep.tile([P, PASSES, P], U32, align_bytes=64, name=f"w1_codes{c}")
+            scales = keep.tile([P, PASSES, P], U8, align_bytes=64, name=f"w1_scales{c}")
+            grouped = keep.tile([P, PASSES, P, J], BF16, align_bytes=64, name=f"w1_grouped{c}")
+            for g in range(PASSES):
+                interleave(copies[g], grouped[:, g], w1_raw[c][g][:])
+            for lo, hi in ((0, 2), (2, 3)):
+                nc.vector.quantize_mx(
+                    out=codes[:, lo:hi, :].rearrange("p g c -> p (g c)").bitcast(FP8X4),
+                    scales=scales[:, lo:hi, :].rearrange("p g c -> p (g c)"),
+                    in_=grouped[:, lo:hi].rearrange("p g c j -> p (g c j)"),
+                )
+            return codes, scales
+
+        def project(c, codes, scales, widths):
+            h = keep.tile([P, T], F32, name=f"h{c}")
+            parts, lo = [], 0
+            for n in widths:
+                hp = psum_h.tile([P, T], F32, name="hp", tag="hp")
+                parts.append((hp, n, slice(lo, lo + n)))
+                lo += n
+            for g in range(PASSES):
+                for hp, n, cols in parts:
+                    nc.tensor.matmul_mx(
+                        out=hp[:, :n],
+                        lhsT=codes[:, g, :].bitcast(FP8X4),
+                        lhsT_scale=scales[:, g, :],
+                        rhs=x_codes[g][:, cols].bitcast(FP8X4),
+                        rhs_scale=x_scales[g][:, cols],
+                        start=(g == 0),
+                        stop=(g == PASSES - 1),
+                    )
+            for i, (hp, n, cols) in enumerate(parts):
+                if i == 0:
+                    nc.scalar.activation(out=h[:, cols], in_=hp[:, :n], func=RELU)
+                else:
+                    nc.vector.tensor_relu(out=h[:, cols], in_=hp[:, :n])
+            return h
+
+        zt = []
+        for vh in range(VH):
+            t = keep.tile([P, 2, P, 2], BF16, align_bytes=64, name=f"zt{vh}")
+            zt.append(t)
+
+        def gather_sum(c, h, last_halves):
+            zps = []
+            for vh in range(VH):
+                t = psum_z.tile([P, P], F32, name="zps", tag="zps")
+                zps.append(t)
+            for d in range(D):
+                halves = ((0, 1), (1, 1)) if last_halves and d == D - 1 else ((0, 2),)
+                for first, count in halves:
+                    prod = prods.tile([P, V], F32, name="prod", tag="prod")
+                    nc.vector.tensor_tensor(
+                        prod[:, : count * P],
+                        h[:].indirect(lists[d][:, first * 8 : (first + count) * 8]),
+                        gate_all[d][:, first * P : (first + count) * P],
+                        MULT,
+                    )
+                    for i in range(count):
+                        nc.tensor.matmul(
+                            zps[first + i][:], prod[:, i * P : (i + 1) * P], ident[:],
+                            start=(d == 0), stop=(d == D - 1), is_transpose=True,
+                        )
+            for vh in range(VH):
+                copy = nc.vector.tensor_copy if last_halves and vh == 1 else nc.scalar.copy
+                copy(
+                    out=zt[vh][:, :, 32 * c : 32 * c + 32, :],
+                    in_=zps[vh][:].rearrange("v (p u e) -> v u p e", u=2, e=2),
+                )
+
+        w2_grouped = keep.tile([P, N, J], BF16, align_bytes=64)
+        w2_codes = keep.tile([P, N], U32, align_bytes=64)
+        w2_scales = keep.tile([P, N], U8, align_bytes=64)
+        z_codes = keep.tile([P, V], U32, align_bytes=64)
+        z_scales = keep.tile([P, V], U8, align_bytes=64)
+
+        def finish(vh):
+            cols = slice(vh * P, (vh + 1) * P)
+            words = zt[vh][:].rearrange("v u p e -> v (u p e)").bitcast(F32)
+            back = psum_m.tile([P, 2, P], F32, name="back", tag="m")
+            for u in range(2):
+                nc.tensor.transpose(back[:, u, :], words[:, u * P : (u + 1) * P], ident[:])
+            grouped = keep.tile([P, P, J], BF16, align_bytes=64, name=f"z_grouped{vh}")
+            copy = (nc.scalar.copy, nc.vector.tensor_copy)[vh]
+            copy(
+                out=grouped[:].rearrange("p v j -> p (v j)").bitcast(F32).rearrange("p (v u) -> p v u", u=2),
+                in_=back[:].rearrange("p u v -> p v u"),
+            )
+            quantize(nc, z_codes[:, cols], z_scales[:, cols], grouped[:])
+            res = keep.tile([P, 2, P], F32, name=f"res{vh}")
+            ops = psum_h.tile([P, 2, P], F32, name="ops", tag="hp")
+            for mb in range(N // P):
+                nc.tensor.matmul_mx(
+                    out=ops[:, mb, :],
+                    lhsT=w2_codes[:, mb * P : (mb + 1) * P].bitcast(FP8X4),
+                    lhsT_scale=w2_scales[:, mb * P : (mb + 1) * P],
+                    rhs=z_codes[:, cols].bitcast(FP8X4),
+                    rhs_scale=z_scales[:, cols],
+                    start=True,
+                    stop=True,
+                )
+            copy(out=res[:], in_=ops[:])
+            nc.sync.dma_start(out=out[:, cols].rearrange("(b p) v -> p b v", p=P), in_=res[:])
+
+        x_codes, x_scales = [], []
+        for g in range(PASSES):
+            t = keep.tile([P, T], U32, align_bytes=64, name=f"x_codes{g}")
+            x_codes.append(t)
+            t = keep.tile([P, T], U8, align_bytes=64, name=f"x_scales{g}")
+            x_scales.append(t)
+
+        def prepare_x(g, vector_cols):
+            grouped = keep.tile([P, T, J], BF16, align_bytes=64, name=f"x_grouped{g}")
+            for lo in range(0, vector_cols, 256):
+                hi = min(lo + 256, vector_cols)
+                interleave(nc.vector.tensor_copy, grouped[:, lo:hi, :], x_raw[g][:, :, lo:hi])
+            interleave(nc.scalar.copy, grouped[:, vector_cols:, :], x_raw[g][:, :, vector_cols:])
+            for lo in (0, 256):
+                cols = slice(lo, lo + 256)
+                quantize(nc, x_codes[g][:, cols], x_scales[g][:, cols], grouped[:, cols, :])
+
+        sc, ve = nc.scalar.copy, nc.vector.tensor_copy
+        codes, scales = prepare_w1(0, (ve, sc, ve))
+        for g, vector_cols in enumerate((256, 256, 352)):
+            prepare_x(g, vector_cols)
+        hs = [project(0, codes, scales, (256, 256))]
+        for c in range(CB):
+            if c + 1 < CB:
+                codes, scales = prepare_w1(c + 1, (sc, sc, sc))
+                hs.append(project(c + 1, codes, scales, (T,)))
+            else:
+                interleave(sc, w2_grouped[:], w2_raw[:])
+                quantize(nc, w2_codes[:], w2_scales[:], w2_grouped[:])
+            gather_sum(c, hs[c], c == CB - 1)
+        for vh in range(VH):
+            finish(vh)

@@ -21,6 +21,7 @@ KP = P * J
 PASSES = K // KP
 CB = H // P
 VH = V // P
+NODE_PARTS = ((0, 256), (256, 384), (384, 512))
 
 
 def interleave(copy, grouped, raw):
@@ -42,147 +43,200 @@ def tile_picked_gcn_mlp_relu_sub_l_kernel(
     nc = tc.nc
     with ExitStack() as ctx:
         keep = ctx.enter_context(tc.tile_pool(name="keep", bufs=1))
-        prods = ctx.enter_context(tc.tile_pool(name="prods", bufs=12))
         psum_h = ctx.enter_context(tc.psum_pool(name="psum_h", bufs=2))
-        psum_z = ctx.enter_context(tc.psum_pool(name="psum_z", bufs=4))
+        psum_z = ctx.enter_context(tc.psum_pool(name="psum_z", bufs=1))
         psum_m = ctx.enter_context(tc.psum_pool(name="psum_m", bufs=2))
+        sc, ve = nc.scalar.copy, nc.vector.tensor_copy
 
-        gate_all = []
+        x_raw, w1_raw, lists, gates = {}, {}, [], []
 
-        def load_gate(first, last):
-            t = keep.tile([P, last - first, V], F32, name=f"gate{first}")
-            nc.sync.dma_start(out=t[:], in_=gate[first:last].rearrange("d p v -> p d v"))
-            for i in range(last - first):
-                gate_all.append(t[:, i, :])
+        def load_x(g, lo, hi):
+            t = keep.tile([P, J, hi - lo], F32, name=f"x_raw{g}_{lo}")
+            nc.sync.dma_start(out=t[:], in_=xT[g * KP : (g + 1) * KP, lo:hi].rearrange("(p j) t -> p j t", j=J))
+            x_raw[g, lo] = t
 
-        w1_raw = [[], [], [], []]
+        def load_w1(c, g):
+            t = keep.tile([P, J, P], F32, name=f"w1_raw{c}_{g}")
+            nc.sync.dma_start(out=t[:], in_=w1[g * KP : (g + 1) * KP, c * P : (c + 1) * P].rearrange("(p j) c -> p j c", j=J))
+            w1_raw[c, g] = t
 
-        def load_w1(b, g):
-            t = keep.tile([P, J, P], F32, name=f"w1_raw{b}_{g}")
-            nc.sync.dma_start(out=t[:], in_=w1[g * KP : (g + 1) * KP, b * P : (b + 1) * P].rearrange("(p j) c -> p j c", j=J))
-            w1_raw[b].append(t)
-
-        x_raw = []
-
-        def load_x(g):
-            t = keep.tile([P, J, T], F32, name=f"x_raw{g}")
-            nc.sync.dma_start(out=t[:], in_=xT[g * KP : (g + 1) * KP, :].rearrange("(p j) t -> p j t", j=J))
-            x_raw.append(t)
-
-        lists = []
-
-        def load_list():
-            d = len(lists)
+        def load_list(d):
             t = keep.tile([P, V // 16], U16, name=f"list{d}")
             nc.sync.dma_start(t[:], (pos1, pos2, pos3, pos4, pos5, pos6)[d])
             lists.append(t)
 
-        for g in range(PASSES):
+        def load_gates(first):
+            t = keep.tile([P, 2, V], F32, name=f"gate{first}")
+            nc.sync.dma_start(out=t[:], in_=gate[first : first + 2].rearrange("d p v -> p d v"))
+            gates.extend([t[:, 0, :], t[:, 1, :]])
+
+        for g in range(PASSES - 1):
+            load_x(g, 0, T)
+            for d in range(3 * g, 3 * g + 3):
+                load_list(d)
             load_w1(0, g)
-        load_list()
-        load_list()
-        for g in range(PASSES):
-            load_x(g)
-        for d in range(4):
-            load_list()
-        load_gate(0, 4)
+        load_w1(0, PASSES - 1)
+        for lo, hi in NODE_PARTS:
+            load_x(PASSES - 1, lo, hi)
+        load_gates(0)
         for g in range(PASSES):
             load_w1(1, g)
-        load_gate(4, 6)
-        for b in (2, 3):
+        load_gates(2)
+        load_gates(4)
+        for c in range(2, CB):
             for g in range(PASSES):
-                load_w1(b, g)
+                load_w1(c, g)
         w2_raw = keep.tile([P, J, N], F32)
         nc.sync.dma_start(out=w2_raw[:], in_=w2.rearrange("(p j) m -> p j m", j=J))
 
         ident = keep.tile([P, P], F32)
         make_identity(nc, ident[:])
 
-        def prepare_w1(c, copies):
-            codes = keep.tile([P, PASSES, P], U32, align_bytes=64, name=f"w1_codes{c}")
-            scales = keep.tile([P, PASSES, P], U8, align_bytes=64, name=f"w1_scales{c}")
-            grouped = keep.tile([P, PASSES, P, J], BF16, align_bytes=64, name=f"w1_grouped{c}")
-            for g in range(PASSES):
-                interleave(copies[g], grouped[:, g], w1_raw[c][g][:])
-            for lo, hi in ((0, 2), (2, 3)):
-                nc.vector.quantize_mx(
-                    out=codes[:, lo:hi, :].rearrange("p g c -> p (g c)").bitcast(FP8X4),
-                    scales=scales[:, lo:hi, :].rearrange("p g c -> p (g c)"),
-                    in_=grouped[:, lo:hi].rearrange("p g c j -> p (g c j)"),
-                )
-            return codes, scales
+        prods, stage_first, stage_rest = {}, {}, {}
+        for c in range(CB - 1):
+            for d in range(2):
+                prods[c, d] = keep.tile([P, V], F32, align_bytes=64, name=f"prod{c}_{d}")[:]
+            wide = keep.tile([P, 3 * V], F32, align_bytes=64, name=f"prod{c}_rest")
+            for d in range(2, D):
+                slot = (d - 2) % 3
+                prods[c, d] = wide[:, slot * V : (slot + 1) * V]
+            stage_first[c + 1] = prods[c, 1]
+            stage_rest[c + 1] = wide[:, V // 2 : V // 2 + 2 * V]
+        last_prods = keep.tile([P, D * V], F32, align_bytes=64)
 
-        def project(c, codes, scales, widths):
-            h = keep.tile([P, T], F32, name=f"h{c}")
-            parts, lo = [], 0
-            for n in widths:
-                hp = psum_h.tile([P, T], F32, name="hp", tag="hp")
-                parts.append((hp, n, slice(lo, lo + n)))
-                lo += n
-            for g in range(PASSES):
-                for hp, n, cols in parts:
-                    nc.tensor.matmul_mx(
-                        out=hp[:, :n],
-                        lhsT=codes[:, g, :].bitcast(FP8X4),
-                        lhsT_scale=scales[:, g, :],
-                        rhs=x_codes[g][:, cols].bitcast(FP8X4),
-                        rhs_scale=x_scales[g][:, cols],
-                        start=(g == 0),
-                        stop=(g == PASSES - 1),
-                    )
-            for i, (hp, n, cols) in enumerate(parts):
-                if i == 0:
-                    nc.scalar.activation(out=h[:, cols], in_=hp[:, :n], func=RELU)
-                else:
-                    nc.vector.tensor_relu(out=h[:, cols], in_=hp[:, :n])
+        def as_grouped(ap):
+            return ap.bitcast(BF16).rearrange("p (c j) -> p c j", j=J)
+
+        x_codes, x_scales = [], []
+
+        x_grouped = []
+        for g in range(PASSES):
+            x_codes.append(keep.tile([P, T], U32, align_bytes=64, name=f"x_codes{g}"))
+            x_scales.append(keep.tile([P, T], U8, align_bytes=64, name=f"x_scales{g}"))
+            x_grouped.append(keep.tile([P, T, J], BF16, align_bytes=64, name=f"x_grouped{g}"))
+
+        def prepare_x(g, lo, hi, vector_cols, width):
+            raw, grouped = x_raw[g, lo], x_grouped[g]
+            interleave(ve, grouped[:, lo : lo + vector_cols, :], raw[:, :, :vector_cols])
+            if lo + vector_cols < hi:
+                interleave(sc, grouped[:, lo + vector_cols : hi, :], raw[:, :, vector_cols:])
+            for a in range(lo, hi, width):
+                cols = slice(a, a + width)
+                quantize(nc, x_codes[g][:, cols], x_scales[g][:, cols], grouped[:, cols, :])
+
+        def prepare_w1(c, g, copy):
+            codes = keep.tile([P, P], U32, align_bytes=64, name=f"w1_codes{c}_{g}")
+            scales = keep.tile([P, P], U8, align_bytes=64, name=f"w1_scales{c}_{g}")
+            if c == 0:
+                stage = keep.tile([P, V], F32, align_bytes=64, name=f"w1_stage{g}")[:]
+            else:
+                stage = stage_first[c]
+            grouped = as_grouped(stage)
+            interleave(copy, grouped, w1_raw[c, g][:])
+            quantize(nc, codes[:], scales[:], grouped)
+            return codes[:], scales[:]
+
+        def product(acc, g, codes, scales, cols):
+            nc.tensor.matmul_mx(
+                out=acc,
+                lhsT=codes.bitcast(FP8X4),
+                lhsT_scale=scales,
+                rhs=x_codes[g][:, cols].bitcast(FP8X4),
+                rhs_scale=x_scales[g][:, cols],
+                start=(g == 0),
+                stop=(g == PASSES - 1),
+            )
+
+        def project_first():
+            h = keep.tile([P, T], F32, name="h0")
+            banks = [
+                psum_h.tile([P, T], F32, name="hp", tag="hp"),
+                psum_h.tile([P, T], F32, name="hp", tag="hp"),
+                psum_m.tile([P, T], F32, name="hm", tag="m"),
+            ]
+            for g in range(PASSES - 1):
+                prepare_x(g, 0, T, 256, 256)
+                codes, scales = prepare_w1(0, g, sc)
+                for bank, (lo, hi) in zip(banks, NODE_PARTS):
+                    product(bank[:, : hi - lo], g, codes, scales, slice(lo, hi))
+            g = PASSES - 1
+            codes, scales = prepare_w1(0, g, sc)
+            for bank, (lo, hi) in zip(banks, NODE_PARTS):
+                prepare_x(g, lo, hi, (hi - lo) * 5 // 8 if hi < T else hi - lo, hi - lo)
+                product(bank[:, : hi - lo], g, codes, scales, slice(lo, hi))
+                relu = relu_scalar if hi < T else relu_vector
+                relu(h[:, lo:hi], bank[:, : hi - lo])
             return h
 
-        zt = []
+        def project(c):
+            h = keep.tile([P, T], F32, name=f"h{c}")
+            hp = psum_h.tile([P, T], F32, name="hp", tag="hp")
+            codes, scales = prepare_w1(c, 0, sc)
+            product(hp[:], 0, codes, scales, slice(0, T))
+            codes = keep.tile([P, 2 * P], U32, align_bytes=64, name=f"w1_codes{c}_rest")
+            scales = keep.tile([P, 2 * P], U8, align_bytes=64, name=f"w1_scales{c}_rest")
+            grouped = as_grouped(stage_rest[c])
+            for i in range(2):
+                interleave(sc, grouped[:, i * P : (i + 1) * P, :], w1_raw[c, 1 + i][:])
+            quantize(nc, codes[:], scales[:], grouped)
+            for i in range(2):
+                product(hp[:], 1 + i, codes[:, i * P : (i + 1) * P], scales[:, i * P : (i + 1) * P], slice(0, T))
+            relu_scalar(h[:], hp[:])
+            return h
+
+        def relu_scalar(o, i):
+            nc.scalar.activation(out=o, in_=i, func=RELU)
+
+        def relu_vector(o, i):
+            nc.vector.tensor_relu(out=o, in_=i)
+
+        zt_words, zt, early, late = [], [], [], []
         for vh in range(VH):
-            t = keep.tile([P, 2, P, 2], BF16, align_bytes=64, name=f"zt{vh}")
-            zt.append(t)
+            zt_words.append(keep.tile([P, 2 * P], F32, align_bytes=64, name=f"zt{vh}"))
+            zt.append(zt_words[vh][:].bitcast(BF16).rearrange("v (u p e) -> v u p e", u=2, e=2))
+            early.append(psum_z.tile([P, (CB - 1) * P], F32, name=f"early{vh}"))
+            late.append(psum_z.tile([P, P], F32, name=f"late{vh}"))
 
-        def gather_sum(c, h, last_halves):
-            zps = []
-            for vh in range(VH):
-                t = psum_z.tile([P, P], F32, name="zps", tag="zps")
-                zps.append(t)
+        def add_transposed(acc, prod, d):
+            nc.tensor.matmul(acc, prod, ident[:], start=(d == 0), stop=(d == D - 1), is_transpose=True)
+
+        def gather_block(c, h):
             for d in range(D):
-                halves = ((0, 1), (1, 1)) if last_halves and d == D - 1 else ((0, 2),)
-                for first, count in halves:
-                    prod = prods.tile([P, V], F32, name="prod", tag="prod")
-                    nc.vector.tensor_tensor(
-                        prod[:, : count * P],
-                        h[:].indirect(lists[d][:, first * 8 : (first + count) * 8]),
-                        gate_all[d][:, first * P : (first + count) * P],
-                        MULT,
-                    )
-                    for i in range(count):
-                        nc.tensor.matmul(
-                            zps[first + i][:], prod[:, i * P : (i + 1) * P], ident[:],
-                            start=(d == 0), stop=(d == D - 1), is_transpose=True,
-                        )
-            for vh in range(VH):
-                copy = nc.vector.tensor_copy if last_halves and vh == 1 else nc.scalar.copy
-                copy(
-                    out=zt[vh][:, :, 32 * c : 32 * c + 32, :],
-                    in_=zps[vh][:].rearrange("v (p u e) -> v u p e", u=2, e=2),
-                )
+                prod = prods[c, d]
+                nc.vector.tensor_tensor(prod, h[:].indirect(lists[d][:]), gates[d], MULT)
+                for vh in range(VH):
+                    add_transposed(early[vh][:, c * P : (c + 1) * P], prod[:, vh * P : (vh + 1) * P], d)
 
-        w2_grouped = keep.tile([P, N, J], BF16, align_bytes=64)
+        def gather_half(vh, h):
+            for d in range(D):
+                prod = last_prods[:, (vh * D + d) * P : (vh * D + d + 1) * P]
+                if vh == 0 and d < VH:
+                    prod = zt_words[d][:, :P]
+                nc.vector.tensor_tensor(
+                    prod, h[:].indirect(lists[d][:, vh * 8 : (vh + 1) * 8]), gates[d][:, vh * P : (vh + 1) * P], MULT
+                )
+                add_transposed(late[vh][:], prod, d)
+
+        def round_sums(copy, vh, acc, first, count):
+            copy(
+                out=zt[vh][:, :, 32 * first : 32 * (first + count), :],
+                in_=acc.rearrange("v (p u e) -> v u p e", u=2, e=2),
+            )
+
         w2_codes = keep.tile([P, N], U32, align_bytes=64)
         w2_scales = keep.tile([P, N], U8, align_bytes=64)
         z_codes = keep.tile([P, V], U32, align_bytes=64)
         z_scales = keep.tile([P, V], U8, align_bytes=64)
 
         def finish(vh):
+            copy = (sc, ve)[vh]
+            round_sums(copy, vh, late[vh][:], CB - 1, 1)
             cols = slice(vh * P, (vh + 1) * P)
-            words = zt[vh][:].rearrange("v u p e -> v (u p e)").bitcast(F32)
+            words = zt_words[vh]
             back = psum_m.tile([P, 2, P], F32, name="back", tag="m")
             for u in range(2):
                 nc.tensor.transpose(back[:, u, :], words[:, u * P : (u + 1) * P], ident[:])
             grouped = keep.tile([P, P, J], BF16, align_bytes=64, name=f"z_grouped{vh}")
-            copy = (nc.scalar.copy, nc.vector.tensor_copy)[vh]
             copy(
                 out=grouped[:].rearrange("p v j -> p (v j)").bitcast(F32).rearrange("p (v u) -> p v u", u=2),
                 in_=back[:].rearrange("p u v -> p v u"),
@@ -203,35 +257,17 @@ def tile_picked_gcn_mlp_relu_sub_l_kernel(
             copy(out=res[:], in_=ops[:])
             nc.sync.dma_start(out=out[:, cols].rearrange("(b p) v -> p b v", p=P), in_=res[:])
 
-        x_codes, x_scales = [], []
-        for g in range(PASSES):
-            t = keep.tile([P, T], U32, align_bytes=64, name=f"x_codes{g}")
-            x_codes.append(t)
-            t = keep.tile([P, T], U8, align_bytes=64, name=f"x_scales{g}")
-            x_scales.append(t)
-
-        def prepare_x(g, vector_cols):
-            grouped = keep.tile([P, T, J], BF16, align_bytes=64, name=f"x_grouped{g}")
-            for lo in range(0, vector_cols, 256):
-                hi = min(lo + 256, vector_cols)
-                interleave(nc.vector.tensor_copy, grouped[:, lo:hi, :], x_raw[g][:, :, lo:hi])
-            interleave(nc.scalar.copy, grouped[:, vector_cols:, :], x_raw[g][:, :, vector_cols:])
-            for lo in (0, 256):
-                cols = slice(lo, lo + 256)
-                quantize(nc, x_codes[g][:, cols], x_scales[g][:, cols], grouped[:, cols, :])
-
-        sc, ve = nc.scalar.copy, nc.vector.tensor_copy
-        codes, scales = prepare_w1(0, (ve, sc, ve))
-        for g, vector_cols in enumerate((256, 256, 352)):
-            prepare_x(g, vector_cols)
-        hs = [project(0, codes, scales, (256, 256))]
-        for c in range(CB):
-            if c + 1 < CB:
-                codes, scales = prepare_w1(c + 1, (sc, sc, sc))
-                hs.append(project(c + 1, codes, scales, (T,)))
-            else:
-                interleave(sc, w2_grouped[:], w2_raw[:])
-                quantize(nc, w2_codes[:], w2_scales[:], w2_grouped[:])
-            gather_sum(c, hs[c], c == CB - 1)
+        h = project_first()
+        for c in range(CB - 1):
+            h_next = project(c + 1)
+            gather_block(c, h)
+            h = h_next
+        w2_grouped = as_grouped(last_prods[:, 2 * P : 2 * P + 2 * N])
+        interleave(sc, w2_grouped, w2_raw[:])
+        quantize(nc, w2_codes[:], w2_scales[:], w2_grouped)
+        gather_half(0, h)
+        for vh in range(VH):
+            round_sums(sc, vh, early[vh][:], 0, CB - 1)
+        gather_half(1, h)
         for vh in range(VH):
             finish(vh)

@@ -21,7 +21,7 @@ KP = P * J
 PASSES = K // KP
 CB = H // P
 VH = V // P
-NODE_PARTS = ((0, 256), (256, 384), (384, 512))
+HALF = T // 2
 
 
 def interleave(copy, grouped, raw):
@@ -50,10 +50,10 @@ def tile_picked_gcn_mlp_relu_sub_l_kernel(
 
         x_raw, w1_raw, lists, gates = {}, {}, [], []
 
-        def load_x(g, lo, hi):
-            t = keep.tile([P, J, hi - lo], F32, name=f"x_raw{g}_{lo}")
-            nc.sync.dma_start(out=t[:], in_=xT[g * KP : (g + 1) * KP, lo:hi].rearrange("(p j) t -> p j t", j=J))
-            x_raw[g, lo] = t
+        def load_x(g):
+            t = keep.tile([P, J, T], F32, name=f"x_raw{g}")
+            nc.sync.dma_start(out=t[:], in_=xT[g * KP : (g + 1) * KP, :].rearrange("(p j) t -> p j t", j=J))
+            x_raw[g] = t
 
         def load_w1(c, g):
             t = keep.tile([P, J, P], F32, name=f"w1_raw{c}_{g}")
@@ -70,17 +70,20 @@ def tile_picked_gcn_mlp_relu_sub_l_kernel(
             nc.sync.dma_start(out=t[:], in_=gate[first : first + 2].rearrange("d p v -> p d v"))
             gates.extend([t[:, 0, :], t[:, 1, :]])
 
-        for g in range(PASSES - 1):
-            load_x(g, 0, T)
-            for d in range(3 * g, 3 * g + 3):
-                load_list(d)
-            load_w1(0, g)
-        load_w1(0, PASSES - 1)
-        for lo, hi in NODE_PARTS:
-            load_x(PASSES - 1, lo, hi)
+        load_x(0)
+        load_w1(0, 0)
+        load_x(1)
+        load_w1(0, 1)
+        load_x(2)
+        load_w1(0, 2)
+        load_list(0)
         load_gates(0)
+        for d in range(1, 4):
+            load_list(d)
         for g in range(PASSES):
             load_w1(1, g)
+        load_list(4)
+        load_list(5)
         load_gates(2)
         load_gates(4)
         for c in range(2, CB):
@@ -97,9 +100,9 @@ def tile_picked_gcn_mlp_relu_sub_l_kernel(
             for d in range(2):
                 prods[c, d] = keep.tile([P, V], F32, align_bytes=64, name=f"prod{c}_{d}")[:]
             wide = keep.tile([P, 3 * V], F32, align_bytes=64, name=f"prod{c}_rest")
-            for d in range(2, D):
-                slot = (d - 2) % 3
-                prods[c, d] = wide[:, slot * V : (slot + 1) * V]
+            for d in range(2, D - 1):
+                prods[c, d] = wide[:, (d - 2) * V : (d - 1) * V]
+            prods[c, D - 1] = w1_raw[c + 1, PASSES - 1][:].rearrange("p j c -> p (j c)")[:, :V]
             stage_first[c + 1] = prods[c, 1]
             stage_rest[c + 1] = wide[:, V // 2 : V // 2 + 2 * V]
         last_prods = keep.tile([P, D * V], F32, align_bytes=64)
@@ -115,14 +118,18 @@ def tile_picked_gcn_mlp_relu_sub_l_kernel(
             x_scales.append(keep.tile([P, T], U8, align_bytes=64, name=f"x_scales{g}"))
             x_grouped.append(keep.tile([P, T, J], BF16, align_bytes=64, name=f"x_grouped{g}"))
 
-        def prepare_x(g, lo, hi, vector_cols, width):
-            raw, grouped = x_raw[g, lo], x_grouped[g]
-            interleave(ve, grouped[:, lo : lo + vector_cols, :], raw[:, :, :vector_cols])
-            if lo + vector_cols < hi:
-                interleave(sc, grouped[:, lo + vector_cols : hi, :], raw[:, :, vector_cols:])
-            for a in range(lo, hi, width):
-                cols = slice(a, a + width)
-                quantize(nc, x_codes[g][:, cols], x_scales[g][:, cols], grouped[:, cols, :])
+        def prepare_x(g, vector_cols):
+            raw, grouped = x_raw[g], x_grouped[g]
+            interleave(ve, grouped[:, :vector_cols, :], raw[:, :, :vector_cols])
+            if vector_cols < HALF:
+                interleave(sc, grouped[:, vector_cols:HALF, :], raw[:, :, vector_cols:HALF])
+            interleave(sc, grouped[:, HALF:, :], raw[:, :, HALF:])
+
+        def quantize_x(g, cols):
+            quantize(nc, x_codes[g][:, cols], x_scales[g][:, cols], grouped_x(g, cols))
+
+        def grouped_x(g, cols):
+            return x_grouped[g][:, cols, :]
 
         def prepare_w1(c, g, copy):
             codes = keep.tile([P, P], U32, align_bytes=64, name=f"w1_codes{c}_{g}")
@@ -149,23 +156,18 @@ def tile_picked_gcn_mlp_relu_sub_l_kernel(
 
         def project_first():
             h = keep.tile([P, T], F32, name="h0")
-            banks = [
-                psum_h.tile([P, T], F32, name="hp", tag="hp"),
-                psum_h.tile([P, T], F32, name="hp", tag="hp"),
-                psum_m.tile([P, T], F32, name="hm", tag="m"),
-            ]
-            for g in range(PASSES - 1):
-                prepare_x(g, 0, T, 256, 256)
-                codes, scales = prepare_w1(0, g, sc)
-                for bank, (lo, hi) in zip(banks, NODE_PARTS):
-                    product(bank[:, : hi - lo], g, codes, scales, slice(lo, hi))
-            g = PASSES - 1
-            codes, scales = prepare_w1(0, g, sc)
-            for bank, (lo, hi) in zip(banks, NODE_PARTS):
-                prepare_x(g, lo, hi, (hi - lo) * 5 // 8 if hi < T else hi - lo, hi - lo)
-                product(bank[:, : hi - lo], g, codes, scales, slice(lo, hi))
-                relu = relu_scalar if hi < T else relu_vector
-                relu(h[:, lo:hi], bank[:, : hi - lo])
+            banks = [psum_h.tile([P, T], F32, name="hp", tag="hp") for i in range(2)]
+            halves = [slice(0, HALF), slice(HALF, T)]
+            for g in range(PASSES):
+                last = g == PASSES - 1
+                prepare_x(g, 176 if last else HALF)
+                quantize_x(g, halves[0])
+                codes, scales = prepare_w1(0, g, ve if last else sc)
+                product(banks[0][:, :HALF], g, codes, scales, halves[0])
+                quantize_x(g, halves[1])
+                product(banks[1][:, :HALF], g, codes, scales, halves[1])
+            for bank, cols in zip(banks, halves):
+                relu_vector(h[:, cols], bank[:, :HALF])
             return h
 
         def project(c):

@@ -51,7 +51,7 @@ def tile_picked_gcn_mlp_relu_sub_l_kernel(
         x_raw, w1_raw, lists, gates = {}, {}, [], []
 
         def load_x(g):
-            t = keep.tile([P, J, T], F32, name=f"x_raw{g}")
+            t = keep.tile([P, J, T], F32, align_bytes=64, name=f"x_raw{g}")
             nc.sync.dma_start(out=t[:], in_=xT[g * KP : (g + 1) * KP, :].rearrange("(p j) t -> p j t", j=J))
             x_raw[g] = t
 
@@ -65,27 +65,26 @@ def tile_picked_gcn_mlp_relu_sub_l_kernel(
             nc.sync.dma_start(t[:], (pos1, pos2, pos3, pos4, pos5, pos6)[d])
             lists.append(t)
 
-        def load_gates(first):
-            t = keep.tile([P, 2, V], F32, name=f"gate{first}")
-            nc.sync.dma_start(out=t[:], in_=gate[first : first + 2].rearrange("d p v -> p d v"))
-            gates.extend([t[:, 0, :], t[:, 1, :]])
+        gate_raw = keep.tile([D, V], F32)
+        gate_rows = keep.tile([P, V], F32)
+        nc.vector.memset(gate_rows[:], 0.0)
 
+        for rows in (slice(0, 4), slice(4, D)):
+            nc.sync.dma_start(out=gate_raw[rows, :], in_=gate[rows, 0, :])
         load_x(0)
         load_w1(0, 0)
-        load_x(1)
         load_w1(0, 1)
+        load_x(1)
         load_x(2)
         load_w1(0, 2)
-        load_list(0)
-        load_gates(0)
-        for d in range(1, 4):
+        for d in range(3):
             load_list(d)
-        for g in range(PASSES):
-            load_w1(1, g)
+        load_w1(1, 0)
+        load_w1(1, 1)
+        load_list(3)
+        load_w1(1, 2)
         load_list(4)
         load_list(5)
-        load_gates(2)
-        load_gates(4)
         for c in range(2, CB):
             for g in range(PASSES):
                 load_w1(c, g)
@@ -97,14 +96,21 @@ def tile_picked_gcn_mlp_relu_sub_l_kernel(
 
         prods, stage_first, stage_rest = {}, {}, {}
         for c in range(CB - 1):
-            for d in range(2):
-                prods[c, d] = keep.tile([P, V], F32, align_bytes=64, name=f"prod{c}_{d}")[:]
-            wide = keep.tile([P, 3 * V], F32, align_bytes=64, name=f"prod{c}_rest")
-            for d in range(2, D - 1):
-                prods[c, d] = wide[:, (d - 2) * V : (d - 1) * V]
-            prods[c, D - 1] = w1_raw[c + 1, PASSES - 1][:].rearrange("p j c -> p (j c)")[:, :V]
-            stage_first[c + 1] = prods[c, 1]
-            stage_rest[c + 1] = wide[:, V // 2 : V // 2 + 2 * V]
+            if c == 0:
+                prods[c, 0] = keep.tile([P, V], F32, align_bytes=64, name="prod_first")[:]
+            else:
+                prods[c, 0] = prods[c - 1, 2]
+            if c == 0:
+                wide = x_raw[PASSES - 1][:].rearrange("p j t -> p (j t)")[:, HALF : HALF + 7 * P]
+            else:
+                wide = keep.tile([P, 7 * P], F32, align_bytes=64, name=f"prod{c}_rest")[:]
+            for d in range(1, 4):
+                prods[c, d] = wide[:, (2 * d - 1) * P : (2 * d + 1) * P]
+            raw = w1_raw[c + 1, PASSES - 1][:].rearrange("p j c -> p (j c)")
+            for d in range(4, D):
+                prods[c, d] = raw[:, (d - 4) * V : (d - 3) * V]
+            stage_first[c + 1] = wide[:, : 2 * P]
+            stage_rest[c + 1] = wide[:, 2 * P : 6 * P]
         last_prods = keep.tile([P, D * V], F32, align_bytes=64)
 
         def as_grouped(ap):
@@ -112,24 +118,19 @@ def tile_picked_gcn_mlp_relu_sub_l_kernel(
 
         x_codes, x_scales = [], []
 
-        x_grouped = []
+        x_stage = [keep.tile([P, HALF, J], BF16, align_bytes=64, name=f"x_stage{i}")[:] for i in range(2)]
         for g in range(PASSES):
             x_codes.append(keep.tile([P, T], U32, align_bytes=64, name=f"x_codes{g}"))
             x_scales.append(keep.tile([P, T], U8, align_bytes=64, name=f"x_scales{g}"))
-            x_grouped.append(keep.tile([P, T, J], BF16, align_bytes=64, name=f"x_grouped{g}"))
 
-        def prepare_x(g, vector_cols):
-            raw, grouped = x_raw[g], x_grouped[g]
-            interleave(ve, grouped[:, :vector_cols, :], raw[:, :, :vector_cols])
-            if vector_cols < HALF:
-                interleave(sc, grouped[:, vector_cols:HALF, :], raw[:, :, vector_cols:HALF])
-            interleave(sc, grouped[:, HALF:, :], raw[:, :, HALF:])
+        def prepare_x(g):
+            raw = x_raw[g]
+            interleave(ve, x_stage[g % 2], raw[:, :, :HALF])
+            interleave(sc, x_stage[1 - g % 2], raw[:, :, HALF:])
 
-        def quantize_x(g, cols):
-            quantize(nc, x_codes[g][:, cols], x_scales[g][:, cols], grouped_x(g, cols))
-
-        def grouped_x(g, cols):
-            return x_grouped[g][:, cols, :]
+        def quantize_x(g, half):
+            cols = slice(half * HALF, (half + 1) * HALF)
+            quantize(nc, x_codes[g][:, cols], x_scales[g][:, cols], x_stage[(g + half) % 2])
 
         def prepare_w1(c, g, copy):
             codes = keep.tile([P, P], U32, align_bytes=64, name=f"w1_codes{c}_{g}")
@@ -154,17 +155,39 @@ def tile_picked_gcn_mlp_relu_sub_l_kernel(
                 stop=(g == PASSES - 1),
             )
 
+        def spread_gates():
+            ve(out=gate_rows[:D, :], in_=gate_raw[:])
+            turned = psum_m.tile([P, VH, P], F32, name="turned", tag="m")
+            for vh in range(VH):
+                nc.tensor.transpose(turned[:, vh, :], gate_rows[:, vh * P : (vh + 1) * P], ident[:])
+            columns = keep.tile([P, VH, D], F32, name="gate_columns")
+            ve(out=columns[:], in_=turned[:, :, :D])
+            for pair, (tag, copy) in enumerate((("late0", ve), ("late1", sc), ("early0", sc))):
+                bank = psum_z.tile([P, 2, V], F32, name="spread", tag=tag)
+                for i in range(2):
+                    for vh in range(VH):
+                        d = 2 * pair + i
+                        nc.tensor.transpose(
+                            bank[:, i, vh * P : (vh + 1) * P], columns[:, vh, d : d + 1].to_broadcast([P, P]), ident[:]
+                        )
+                t = keep.tile([P, 2, V], F32, name=f"gate{pair}")
+                copy(out=t[:], in_=bank[:])
+                gates.extend([t[:, 0, :], t[:, 1, :]])
+
         def project_first():
             h = keep.tile([P, T], F32, name="h0")
             banks = [psum_h.tile([P, T], F32, name="hp", tag="hp") for i in range(2)]
             halves = [slice(0, HALF), slice(HALF, T)]
             for g in range(PASSES):
                 last = g == PASSES - 1
-                prepare_x(g, 176 if last else HALF)
-                quantize_x(g, halves[0])
-                codes, scales = prepare_w1(0, g, ve if last else sc)
+                if g == 1:
+                    codes, scales = prepare_w1(0, g, sc)
+                prepare_x(g)
+                quantize_x(g, 0)
+                if g != 1:
+                    codes, scales = prepare_w1(0, g, ve if last else sc)
                 product(banks[0][:, :HALF], g, codes, scales, halves[0])
-                quantize_x(g, halves[1])
+                quantize_x(g, 1)
                 product(banks[1][:, :HALF], g, codes, scales, halves[1])
             for bank, cols in zip(banks, halves):
                 relu_vector(h[:, cols], bank[:, :HALF])
@@ -191,13 +214,6 @@ def tile_picked_gcn_mlp_relu_sub_l_kernel(
 
         def relu_vector(o, i):
             nc.vector.tensor_relu(out=o, in_=i)
-
-        zt_words, zt, early, late = [], [], [], []
-        for vh in range(VH):
-            zt_words.append(keep.tile([P, 2 * P], F32, align_bytes=64, name=f"zt{vh}"))
-            zt.append(zt_words[vh][:].bitcast(BF16).rearrange("v (u p e) -> v u p e", u=2, e=2))
-            early.append(psum_z.tile([P, (CB - 1) * P], F32, name=f"early{vh}"))
-            late.append(psum_z.tile([P, P], F32, name=f"late{vh}"))
 
         def add_transposed(acc, prod, d):
             nc.tensor.matmul(acc, prod, ident[:], start=(d == 0), stop=(d == D - 1), is_transpose=True)
@@ -259,7 +275,15 @@ def tile_picked_gcn_mlp_relu_sub_l_kernel(
             copy(out=res[:], in_=ops[:])
             nc.sync.dma_start(out=out[:, cols].rearrange("(b p) v -> p b v", p=P), in_=res[:])
 
+        spread_gates()
         h = project_first()
+        zt_words, zt, early, late = [], [], [], []
+        for vh in range(VH):
+            zt_words.append(keep.tile([P, 2 * P], F32, align_bytes=64, name=f"zt{vh}"))
+            zt.append(zt_words[vh][:].bitcast(BF16).rearrange("v (u p e) -> v u p e", u=2, e=2))
+            early.append(psum_z.tile([P, (CB - 1) * P], F32, name=f"early{vh}", tag=f"early{vh}"))
+            late.append(psum_z.tile([P, P], F32, name=f"late{vh}", tag=f"late{vh}"))
+
         for c in range(CB - 1):
             h_next = project(c + 1)
             gather_block(c, h)

@@ -195,18 +195,21 @@ def tile_picked_gcn_mlp_relu_sub_l_kernel(
 
         def project(c):
             h = keep.tile([P, T], F32, name=f"h{c}")
-            hp = psum_h.tile([P, T], F32, name="hp", tag="hp")
+            banks = [psum_h.tile([P, HALF], F32, name="hp", tag="hp") for i in range(2)]
+            halves = [slice(0, HALF), slice(HALF, T)]
             codes, scales = prepare_w1(c, 0, sc)
-            product(hp[:], 0, codes, scales, slice(0, T))
+            for bank, cols in zip(banks, halves):
+                product(bank[:], 0, codes, scales, cols)
             codes = keep.tile([P, 2 * P], U32, align_bytes=64, name=f"w1_codes{c}_rest")
             scales = keep.tile([P, 2 * P], U8, align_bytes=64, name=f"w1_scales{c}_rest")
             grouped = as_grouped(stage_rest[c])
             for i in range(2):
                 interleave(sc, grouped[:, i * P : (i + 1) * P, :], w1_raw[c, 1 + i][:])
             quantize(nc, codes[:], scales[:], grouped)
-            for i in range(2):
-                product(hp[:], 1 + i, codes[:, i * P : (i + 1) * P], scales[:, i * P : (i + 1) * P], slice(0, T))
-            relu_scalar(h[:], hp[:])
+            for bank, cols in zip(banks, halves):
+                for i in range(2):
+                    product(bank[:], 1 + i, codes[:, i * P : (i + 1) * P], scales[:, i * P : (i + 1) * P], cols)
+                relu_scalar(h[:, cols], bank[:])
             return h
 
         def relu_scalar(o, i):
@@ -230,6 +233,8 @@ def tile_picked_gcn_mlp_relu_sub_l_kernel(
                 prod = last_prods[:, (vh * D + d) * P : (vh * D + d + 1) * P]
                 if vh == 0 and d < VH:
                     prod = zt_words[d][:, :P]
+                if vh == 0 and d == VH:
+                    prod = w2_stage[:, :P]
                 nc.vector.tensor_tensor(
                     prod, h[:].indirect(lists[d][:, vh * 8 : (vh + 1) * 8]), gates[d][:, vh * P : (vh + 1) * P], MULT
                 )
@@ -241,6 +246,7 @@ def tile_picked_gcn_mlp_relu_sub_l_kernel(
                 in_=acc.rearrange("v (p u e) -> v u p e", u=2, e=2),
             )
 
+        w2_stage = keep.tile([P, 2 * N], F32, align_bytes=64)
         w2_codes = keep.tile([P, N], U32, align_bytes=64)
         w2_scales = keep.tile([P, N], U8, align_bytes=64)
         z_codes = keep.tile([P, V], U32, align_bytes=64)
@@ -260,11 +266,14 @@ def tile_picked_gcn_mlp_relu_sub_l_kernel(
                 in_=back[:].rearrange("p u v -> p v u"),
             )
             quantize(nc, z_codes[:, cols], z_scales[:, cols], grouped[:])
-            res = keep.tile([P, 2, P], F32, name=f"res{vh}")
-            ops = psum_h.tile([P, 2, P], F32, name="ops", tag="hp")
             for mb in range(N // P):
+                res = keep.tile([P, P], F32, name=f"res{vh}_{mb}")
+                if vh == 0:
+                    ops = psum_h.tile([P, P], F32, name="ops", tag="hp")
+                else:
+                    ops = psum_z.tile([P, P], F32, name="ops", tag=f"early{mb}")
                 nc.tensor.matmul_mx(
-                    out=ops[:, mb, :],
+                    out=ops[:],
                     lhsT=w2_codes[:, mb * P : (mb + 1) * P].bitcast(FP8X4),
                     lhsT_scale=w2_scales[:, mb * P : (mb + 1) * P],
                     rhs=z_codes[:, cols].bitcast(FP8X4),
@@ -272,8 +281,8 @@ def tile_picked_gcn_mlp_relu_sub_l_kernel(
                     start=True,
                     stop=True,
                 )
-            copy(out=res[:], in_=ops[:])
-            nc.sync.dma_start(out=out[:, cols].rearrange("(b p) v -> p b v", p=P), in_=res[:])
+                (sc, copy)[mb](out=res[:], in_=ops[:])
+                nc.sync.dma_start(out=out[mb * P : (mb + 1) * P, cols], in_=res[:])
 
         spread_gates()
         h = project_first()
@@ -288,12 +297,12 @@ def tile_picked_gcn_mlp_relu_sub_l_kernel(
             h_next = project(c + 1)
             gather_block(c, h)
             h = h_next
-        w2_grouped = as_grouped(last_prods[:, 2 * P : 2 * P + 2 * N])
-        interleave(sc, w2_grouped, w2_raw[:])
-        quantize(nc, w2_codes[:], w2_scales[:], w2_grouped)
         gather_half(0, h)
         for vh in range(VH):
             round_sums(sc, vh, early[vh][:], 0, CB - 1)
+        w2_grouped = as_grouped(w2_stage[:])
+        interleave(sc, w2_grouped, w2_raw[:])
         gather_half(1, h)
+        quantize(nc, w2_codes[:], w2_scales[:], w2_grouped)
         for vh in range(VH):
             finish(vh)

@@ -19,9 +19,12 @@ P = 128
 J = 4
 KP = P * J
 PASSES = K // KP
-CB = H // P
-VH = V // P
+GROUPS = H // P
+TARGET_HALVES = V // P
 HALF = T // 2
+NODE_HALVES = (slice(0, HALF), slice(HALF, T))
+LIST_COLUMNS = P // 16
+GROUP_PARTITIONS = P // J
 
 
 def interleave(copy, grouped, raw):
@@ -32,9 +35,11 @@ def interleave(copy, grouped, raw):
 
 
 def quantize(nc, codes, scales, grouped):
-    nc.vector.quantize_mx(
-        out=codes.bitcast(FP8X4), scales=scales, in_=grouped.rearrange("p c j -> p (c j)")
-    )
+    nc.vector.quantize_mx(out=codes.bitcast(FP8X4), scales=scales, in_=grouped.rearrange("p c j -> p (c j)"))
+
+
+def as_grouped(words):
+    return words.bitcast(BF16).rearrange("p (c j) -> p c j", j=J)
 
 
 def tile_picked_gcn_mlp_relu_sub_l_kernel(
@@ -46,9 +51,9 @@ def tile_picked_gcn_mlp_relu_sub_l_kernel(
         psum_h = ctx.enter_context(tc.psum_pool(name="psum_h", bufs=2))
         psum_z = ctx.enter_context(tc.psum_pool(name="psum_z", bufs=1))
         psum_m = ctx.enter_context(tc.psum_pool(name="psum_m", bufs=2))
-        sc, ve = nc.scalar.copy, nc.vector.tensor_copy
+        on_scalar, on_vector = nc.scalar.copy, nc.vector.tensor_copy
 
-        x_raw, w1_raw, lists, gates = {}, {}, [], []
+        x_raw, w1_raw, lists = {}, {}, []
 
         def load_x(g):
             t = keep.tile([P, J, T], F32, align_bytes=64, name=f"x_raw{g}")
@@ -57,7 +62,8 @@ def tile_picked_gcn_mlp_relu_sub_l_kernel(
 
         def load_w1(c, g):
             t = keep.tile([P, J, P], F32, name=f"w1_raw{c}_{g}")
-            nc.sync.dma_start(out=t[:], in_=w1[g * KP : (g + 1) * KP, c * P : (c + 1) * P].rearrange("(p j) c -> p j c", j=J))
+            rows = w1[g * KP : (g + 1) * KP, c * P : (c + 1) * P]
+            nc.sync.dma_start(out=t[:], in_=rows.rearrange("(p j) c -> p j c", j=J))
             w1_raw[c, g] = t
 
         def load_list(d):
@@ -68,7 +74,6 @@ def tile_picked_gcn_mlp_relu_sub_l_kernel(
         gate_raw = keep.tile([D, V], F32)
         gate_rows = keep.tile([P, V], F32)
         nc.vector.memset(gate_rows[:], 0.0)
-
         for rows in (slice(0, 4), slice(4, D)):
             nc.sync.dma_start(out=gate_raw[rows, :], in_=gate[rows, 0, :])
         load_x(0)
@@ -85,7 +90,7 @@ def tile_picked_gcn_mlp_relu_sub_l_kernel(
         load_w1(1, 2)
         load_list(4)
         load_list(5)
-        for c in range(2, CB):
+        for c in range(2, GROUPS):
             for g in range(PASSES):
                 load_w1(c, g)
         w2_raw = keep.tile([P, J, N], F32)
@@ -95,214 +100,187 @@ def tile_picked_gcn_mlp_relu_sub_l_kernel(
         make_identity(nc, ident[:])
 
         prods, stage_first, stage_rest = {}, {}, {}
-        for c in range(CB - 1):
+        for c in range(GROUPS - 1):
             if c == 0:
                 prods[c, 0] = keep.tile([P, V], F32, align_bytes=64, name="prod_first")[:]
+                shared = x_raw[PASSES - 1][:].rearrange("p j t -> p (j t)")[:, HALF : HALF + 7 * P]
             else:
-                prods[c, 0] = prods[c - 1, 2]
-            if c == 0:
-                wide = x_raw[PASSES - 1][:].rearrange("p j t -> p (j t)")[:, HALF : HALF + 7 * P]
-            else:
-                wide = keep.tile([P, 7 * P], F32, align_bytes=64, name=f"prod{c}_rest")[:]
+                prods[c, 0] = prods[c - 1, 1]
+                shared = keep.tile([P, 7 * P], F32, align_bytes=64, name=f"shared{c}")[:]
             for d in range(1, 4):
-                prods[c, d] = wide[:, (2 * d - 1) * P : (2 * d + 1) * P]
+                prods[c, d] = shared[:, (2 * d - 1) * P : (2 * d + 1) * P]
             raw = w1_raw[c + 1, PASSES - 1][:].rearrange("p j c -> p (j c)")
             for d in range(4, D):
                 prods[c, d] = raw[:, (d - 4) * V : (d - 3) * V]
-            stage_first[c + 1] = wide[:, : 2 * P]
-            stage_rest[c + 1] = wide[:, 2 * P : 6 * P]
-        last_prods = keep.tile([P, D * V], F32, align_bytes=64)
+            stage_first[c + 1] = shared[:, : 2 * P]
+            stage_rest[c + 1] = shared[:, 2 * P : 6 * P]
 
-        def as_grouped(ap):
-            return ap.bitcast(BF16).rearrange("p (c j) -> p c j", j=J)
-
-        x_codes, x_scales = [], []
+        def operand_tiles(name, width):
+            codes = keep.tile([P, width], U32, align_bytes=64, name=f"{name}_codes")
+            scales = keep.tile([P, width], U8, align_bytes=64, name=f"{name}_scales")
+            return codes, scales
 
         x_stage = [keep.tile([P, HALF, J], BF16, align_bytes=64, name=f"x_stage{i}")[:] for i in range(2)]
-        for g in range(PASSES):
-            x_codes.append(keep.tile([P, T], U32, align_bytes=64, name=f"x_codes{g}"))
-            x_scales.append(keep.tile([P, T], U8, align_bytes=64, name=f"x_scales{g}"))
+        x_operands = [operand_tiles(f"x{g}", T) for g in range(PASSES)]
 
-        def prepare_x(g):
-            raw = x_raw[g]
-            interleave(ve, x_stage[g % 2], raw[:, :, :HALF])
-            interleave(sc, x_stage[1 - g % 2], raw[:, :, HALF:])
+        def stage_x(g):
+            interleave(on_vector, x_stage[g % 2], x_raw[g][:, :, NODE_HALVES[0]])
+            interleave(on_scalar, x_stage[1 - g % 2], x_raw[g][:, :, NODE_HALVES[1]])
 
         def quantize_x(g, half):
-            cols = slice(half * HALF, (half + 1) * HALF)
-            quantize(nc, x_codes[g][:, cols], x_scales[g][:, cols], x_stage[(g + half) % 2])
+            codes, scales = x_operands[g]
+            cols = NODE_HALVES[half]
+            quantize(nc, codes[:, cols], scales[:, cols], x_stage[(g + half) % 2])
 
-        def prepare_w1(c, g, copy):
-            codes = keep.tile([P, P], U32, align_bytes=64, name=f"w1_codes{c}_{g}")
-            scales = keep.tile([P, P], U8, align_bytes=64, name=f"w1_scales{c}_{g}")
-            if c == 0:
-                stage = keep.tile([P, V], F32, align_bytes=64, name=f"w1_stage{g}")[:]
-            else:
-                stage = stage_first[c]
-            grouped = as_grouped(stage)
-            interleave(copy, grouped, w1_raw[c, g][:])
-            quantize(nc, codes[:], scales[:], grouped)
+        def quantize_w1_slice(c, g, copy, stage):
+            codes, scales = operand_tiles(f"w1_{c}_{g}", P)
+            interleave(copy, as_grouped(stage), w1_raw[c, g][:])
+            quantize(nc, codes[:], scales[:], as_grouped(stage))
             return codes[:], scales[:]
 
-        def product(acc, g, codes, scales, cols):
+        def project_pass(acc, g, codes, scales, cols):
+            x_codes, x_scales = x_operands[g]
             nc.tensor.matmul_mx(
                 out=acc,
                 lhsT=codes.bitcast(FP8X4),
                 lhsT_scale=scales,
-                rhs=x_codes[g][:, cols].bitcast(FP8X4),
-                rhs_scale=x_scales[g][:, cols],
+                rhs=x_codes[:, cols].bitcast(FP8X4),
+                rhs_scale=x_scales[:, cols],
                 start=(g == 0),
                 stop=(g == PASSES - 1),
             )
 
         def spread_gates():
-            ve(out=gate_rows[:D, :], in_=gate_raw[:])
-            turned = psum_m.tile([P, VH, P], F32, name="turned", tag="m")
-            for vh in range(VH):
+            on_vector(out=gate_rows[:D, :], in_=gate_raw[:])
+            turned = psum_m.tile([P, TARGET_HALVES, P], F32, name="turned", tag="m")
+            for vh in range(TARGET_HALVES):
                 nc.tensor.transpose(turned[:, vh, :], gate_rows[:, vh * P : (vh + 1) * P], ident[:])
-            columns = keep.tile([P, VH, D], F32, name="gate_columns")
-            ve(out=columns[:], in_=turned[:, :, :D])
-            for pair, (tag, copy) in enumerate((("late0", ve), ("late1", sc), ("early0", sc))):
+            columns = keep.tile([P, TARGET_HALVES, D], F32, name="gate_columns")
+            on_vector(out=columns[:], in_=turned[:, :, :D])
+            gates = []
+            for pair, (tag, copy) in enumerate((("late0", on_vector), ("late1", on_scalar), ("early0", on_scalar))):
                 bank = psum_z.tile([P, 2, V], F32, name="spread", tag=tag)
                 for i in range(2):
-                    for vh in range(VH):
-                        d = 2 * pair + i
-                        nc.tensor.transpose(
-                            bank[:, i, vh * P : (vh + 1) * P], columns[:, vh, d : d + 1].to_broadcast([P, P]), ident[:]
-                        )
+                    d = 2 * pair + i
+                    for vh in range(TARGET_HALVES):
+                        column = columns[:, vh, d : d + 1].to_broadcast([P, P])
+                        nc.tensor.transpose(bank[:, i, vh * P : (vh + 1) * P], column, ident[:])
                 t = keep.tile([P, 2, V], F32, name=f"gate{pair}")
                 copy(out=t[:], in_=bank[:])
                 gates.extend([t[:, 0, :], t[:, 1, :]])
+            return gates
 
-        def project_first():
+        def project_first_group():
             h = keep.tile([P, T], F32, name="h0")
             banks = [psum_h.tile([P, T], F32, name="hp", tag="hp") for i in range(2)]
-            halves = [slice(0, HALF), slice(HALF, T)]
             for g in range(PASSES):
-                last = g == PASSES - 1
-                if g == 1:
-                    codes, scales = prepare_w1(0, g, sc)
-                prepare_x(g)
+                stage = keep.tile([P, V], F32, align_bytes=64, name=f"w1_stage{g}")[:]
+                w1_first = g == 1
+                if w1_first:
+                    codes, scales = quantize_w1_slice(0, g, on_scalar, stage)
+                stage_x(g)
                 quantize_x(g, 0)
-                if g != 1:
-                    codes, scales = prepare_w1(0, g, ve if last else sc)
-                product(banks[0][:, :HALF], g, codes, scales, halves[0])
+                if not w1_first:
+                    codes, scales = quantize_w1_slice(0, g, on_vector if g == PASSES - 1 else on_scalar, stage)
+                project_pass(banks[0][:, :HALF], g, codes, scales, NODE_HALVES[0])
                 quantize_x(g, 1)
-                product(banks[1][:, :HALF], g, codes, scales, halves[1])
-            for bank, cols in zip(banks, halves):
-                relu_vector(h[:, cols], bank[:, :HALF])
+                project_pass(banks[1][:, :HALF], g, codes, scales, NODE_HALVES[1])
+            for bank, cols in zip(banks, NODE_HALVES):
+                nc.vector.tensor_relu(out=h[:, cols], in_=bank[:, :HALF])
             return h
 
-        def project(c):
+        def project_group(c):
             h = keep.tile([P, T], F32, name=f"h{c}")
             banks = [psum_h.tile([P, HALF], F32, name="hp", tag="hp") for i in range(2)]
-            halves = [slice(0, HALF), slice(HALF, T)]
-            codes, scales = prepare_w1(c, 0, sc)
-            for bank, cols in zip(banks, halves):
-                product(bank[:], 0, codes, scales, cols)
-            codes = keep.tile([P, 2 * P], U32, align_bytes=64, name=f"w1_codes{c}_rest")
-            scales = keep.tile([P, 2 * P], U8, align_bytes=64, name=f"w1_scales{c}_rest")
+            codes, scales = quantize_w1_slice(c, 0, on_scalar, stage_first[c])
+            for bank, cols in zip(banks, NODE_HALVES):
+                project_pass(bank[:], 0, codes, scales, cols)
+            codes, scales = operand_tiles(f"w1_{c}_rest", (PASSES - 1) * P)
             grouped = as_grouped(stage_rest[c])
-            for i in range(2):
-                interleave(sc, grouped[:, i * P : (i + 1) * P, :], w1_raw[c, 1 + i][:])
+            for i in range(PASSES - 1):
+                interleave(on_scalar, grouped[:, i * P : (i + 1) * P, :], w1_raw[c, 1 + i][:])
             quantize(nc, codes[:], scales[:], grouped)
-            for bank, cols in zip(banks, halves):
-                for i in range(2):
-                    product(bank[:], 1 + i, codes[:, i * P : (i + 1) * P], scales[:, i * P : (i + 1) * P], cols)
-                relu_scalar(h[:, cols], bank[:])
+            for bank, cols in zip(banks, NODE_HALVES):
+                for i in range(PASSES - 1):
+                    project_pass(bank[:], 1 + i, codes[:, i * P : (i + 1) * P], scales[:, i * P : (i + 1) * P], cols)
+                nc.scalar.activation(out=h[:, cols], in_=bank[:], func=RELU)
             return h
-
-        def relu_scalar(o, i):
-            nc.scalar.activation(out=o, in_=i, func=RELU)
-
-        def relu_vector(o, i):
-            nc.vector.tensor_relu(out=o, in_=i)
 
         def add_transposed(acc, prod, d):
             nc.tensor.matmul(acc, prod, ident[:], start=(d == 0), stop=(d == D - 1), is_transpose=True)
 
-        def gather_block(c, h):
-            for d in range(D):
-                prod = prods[c, d]
-                nc.vector.tensor_tensor(prod, h[:].indirect(lists[d][:]), gates[d], MULT)
-                for vh in range(VH):
-                    add_transposed(early[vh][:, c * P : (c + 1) * P], prod[:, vh * P : (vh + 1) * P], d)
+        gates = spread_gates()
+        h = project_first_group()
 
-        def gather_half(vh, h):
+        zt_words, zt, early, late = [], [], [], []
+        for vh in range(TARGET_HALVES):
+            zt_words.append(keep.tile([P, 2 * P], F32, align_bytes=64, name=f"zt{vh}"))
+            zt.append(zt_words[vh][:].bitcast(BF16).rearrange("v (u p e) -> v u p e", u=2, e=2))
+            early.append(psum_z.tile([P, (GROUPS - 1) * P], F32, name=f"early{vh}", tag=f"early{vh}"))
+            late.append(psum_z.tile([P, P], F32, name=f"late{vh}", tag=f"late{vh}"))
+
+        for c in range(GROUPS - 1):
+            h_next = project_group(c + 1)
             for d in range(D):
-                prod = last_prods[:, (vh * D + d) * P : (vh * D + d + 1) * P]
-                if vh == 0 and d < VH:
-                    prod = zt_words[d][:, :P]
-                if vh == 0 and d == VH:
-                    prod = w2_stage[:, :P]
-                nc.vector.tensor_tensor(
-                    prod, h[:].indirect(lists[d][:, vh * 8 : (vh + 1) * 8]), gates[d][:, vh * P : (vh + 1) * P], MULT
-                )
+                nc.vector.tensor_tensor(prods[c, d], h[:].indirect(lists[d][:]), gates[d], MULT)
+                for vh in range(TARGET_HALVES):
+                    add_transposed(early[vh][:, c * P : (c + 1) * P], prods[c, d][:, vh * P : (vh + 1) * P], d)
+            h = h_next
+
+        last_prods = keep.tile([P, 8 * P], F32, align_bytes=64)
+        before_w2 = keep.tile([P, N], F32, align_bytes=64, name="before_w2", tag="w2_slot")
+        own = [last_prods[:, i * P : (i + 1) * P] for i in range(8)]
+        half_prods = (
+            [zt_words[0][:, :P], zt_words[1][:, :P]] + own[:4],
+            own[4:7] + [before_w2[:, :P], before_w2[:, P:]] + own[7:],
+        )
+
+        def gather_half(vh):
+            offsets = slice(vh * LIST_COLUMNS, (vh + 1) * LIST_COLUMNS)
+            for d in range(D):
+                prod = half_prods[vh][d]
+                nc.vector.tensor_tensor(prod, h[:].indirect(lists[d][:, offsets]), gates[d][:, vh * P : (vh + 1) * P], MULT)
                 add_transposed(late[vh][:], prod, d)
 
-        def round_sums(copy, vh, acc, first, count):
-            copy(
-                out=zt[vh][:, :, 32 * first : 32 * (first + count), :],
-                in_=acc.rearrange("v (p u e) -> v u p e", u=2, e=2),
-            )
+        def round_sums(copy, vh, acc, first_group, groups):
+            partitions = slice(GROUP_PARTITIONS * first_group, GROUP_PARTITIONS * (first_group + groups))
+            copy(out=zt[vh][:, :, partitions, :], in_=acc.rearrange("v (p u e) -> v u p e", u=2, e=2))
 
-        w2_stage = keep.tile([P, 2 * N], F32, align_bytes=64)
-        w2_codes = keep.tile([P, N], U32, align_bytes=64)
+        w2_stage = keep.tile([P, N, J], BF16, align_bytes=64)
+        interleave(on_scalar, w2_stage[:], w2_raw[:])
+        gather_half(0)
+        for vh in range(TARGET_HALVES):
+            round_sums(on_scalar, vh, early[vh][:], 0, GROUPS - 1)
+        gather_half(1)
+        w2_codes = keep.tile([P, N], U32, align_bytes=64, name="w2_codes", tag="w2_slot")
         w2_scales = keep.tile([P, N], U8, align_bytes=64)
-        z_codes = keep.tile([P, V], U32, align_bytes=64)
-        z_scales = keep.tile([P, V], U8, align_bytes=64)
+        quantize(nc, w2_codes[:], w2_scales[:], w2_stage[:])
 
-        def finish(vh):
-            copy = (sc, ve)[vh]
-            round_sums(copy, vh, late[vh][:], CB - 1, 1)
+        z_codes, z_scales = operand_tiles("z", V)
+        for vh, copy in enumerate((on_scalar, on_vector)):
             cols = slice(vh * P, (vh + 1) * P)
-            words = zt_words[vh]
+            round_sums(copy, vh, late[vh][:], GROUPS - 1, 1)
             back = psum_m.tile([P, 2, P], F32, name="back", tag="m")
             for u in range(2):
-                nc.tensor.transpose(back[:, u, :], words[:, u * P : (u + 1) * P], ident[:])
-            grouped = keep.tile([P, P, J], BF16, align_bytes=64, name=f"z_grouped{vh}")
-            copy(
-                out=grouped[:].rearrange("p v j -> p (v j)").bitcast(F32).rearrange("p (v u) -> p v u", u=2),
-                in_=back[:].rearrange("p u v -> p v u"),
-            )
-            quantize(nc, z_codes[:, cols], z_scales[:, cols], grouped[:])
+                nc.tensor.transpose(back[:, u, :], zt_words[vh][:, u * P : (u + 1) * P], ident[:])
+            z_words = keep.tile([P, P, 2], F32, align_bytes=64, name=f"z_words{vh}")
+            copy(out=z_words[:], in_=back[:].rearrange("p u v -> p v u"))
+            quantize(nc, z_codes[:, cols], z_scales[:, cols], as_grouped(z_words[:].rearrange("p v u -> p (v u)")))
             for mb in range(N // P):
-                res = keep.tile([P, P], F32, name=f"res{vh}_{mb}")
+                rows = slice(mb * P, (mb + 1) * P)
                 if vh == 0:
-                    ops = psum_h.tile([P, P], F32, name="ops", tag="hp")
+                    acc = psum_h.tile([P, P], F32, name="acc", tag="hp")
                 else:
-                    ops = psum_z.tile([P, P], F32, name="ops", tag=f"early{mb}")
+                    acc = psum_z.tile([P, P], F32, name="acc", tag=f"early{mb}")
                 nc.tensor.matmul_mx(
-                    out=ops[:],
-                    lhsT=w2_codes[:, mb * P : (mb + 1) * P].bitcast(FP8X4),
-                    lhsT_scale=w2_scales[:, mb * P : (mb + 1) * P],
+                    out=acc[:],
+                    lhsT=w2_codes[:, rows].bitcast(FP8X4),
+                    lhsT_scale=w2_scales[:, rows],
                     rhs=z_codes[:, cols].bitcast(FP8X4),
                     rhs_scale=z_scales[:, cols],
                     start=True,
                     stop=True,
                 )
-                (sc, copy)[mb](out=res[:], in_=ops[:])
-                nc.sync.dma_start(out=out[mb * P : (mb + 1) * P, cols], in_=res[:])
-
-        spread_gates()
-        h = project_first()
-        zt_words, zt, early, late = [], [], [], []
-        for vh in range(VH):
-            zt_words.append(keep.tile([P, 2 * P], F32, align_bytes=64, name=f"zt{vh}"))
-            zt.append(zt_words[vh][:].bitcast(BF16).rearrange("v (u p e) -> v u p e", u=2, e=2))
-            early.append(psum_z.tile([P, (CB - 1) * P], F32, name=f"early{vh}", tag=f"early{vh}"))
-            late.append(psum_z.tile([P, P], F32, name=f"late{vh}", tag=f"late{vh}"))
-
-        for c in range(CB - 1):
-            h_next = project(c + 1)
-            gather_block(c, h)
-            h = h_next
-        gather_half(0, h)
-        for vh in range(VH):
-            round_sums(sc, vh, early[vh][:], 0, CB - 1)
-        w2_grouped = as_grouped(w2_stage[:])
-        interleave(sc, w2_grouped, w2_raw[:])
-        gather_half(1, h)
-        quantize(nc, w2_codes[:], w2_scales[:], w2_grouped)
-        for vh in range(VH):
-            finish(vh)
+                res = keep.tile([P, P], F32, name=f"res{vh}_{mb}")
+                (on_scalar, copy)[mb](out=res[:], in_=acc[:])
+                nc.sync.dma_start(out=out[rows, cols], in_=res[:])

@@ -25,6 +25,8 @@ HALF = T // 2
 NODE_HALVES = (slice(0, HALF), slice(HALF, T))
 LIST_COLUMNS = P // 16
 GROUP_PARTITIONS = P // J
+SLICE_STAGE = KP // 2
+SPLIT_LISTS = 2
 
 
 def interleave(copy, grouped, raw):
@@ -38,8 +40,12 @@ def quantize(nc, codes, scales, grouped):
     nc.vector.quantize_mx(out=codes.bitcast(FP8X4), scales=scales, in_=grouped.rearrange("p c j -> p (c j)"))
 
 
-def as_grouped(words):
-    return words.bitcast(BF16).rearrange("p (c j) -> p c j", j=J)
+def as_grouped(area):
+    return area.bitcast(BF16).rearrange("p (c j) -> p c j", j=J)
+
+
+def part(area, i, n=1):
+    return area[:, i * SLICE_STAGE : (i + n) * SLICE_STAGE]
 
 
 def tile_picked_gcn_mlp_relu_sub_l_kernel(
@@ -48,10 +54,21 @@ def tile_picked_gcn_mlp_relu_sub_l_kernel(
     nc = tc.nc
     with ExitStack() as ctx:
         keep = ctx.enter_context(tc.tile_pool(name="keep", bufs=1))
-        psum_h = ctx.enter_context(tc.psum_pool(name="psum_h", bufs=2))
-        psum_z = ctx.enter_context(tc.psum_pool(name="psum_z", bufs=1))
-        psum_m = ctx.enter_context(tc.psum_pool(name="psum_m", bufs=2))
+        psum = ctx.enter_context(tc.psum_pool(name="psum", bufs=1))
         on_scalar, on_vector = nc.scalar.copy, nc.vector.tensor_copy
+
+        def bank(b, shape, name):
+            t = psum.tile(shape, F32, name=name, tag=f"bank{b}")
+            return t
+
+        def words(name, width, tag=None):
+            t = keep.tile([P, width], F32, align_bytes=64, name=name, tag=tag or name)
+            return t[:]
+
+        def operand_tiles(name, width, codes_tag=None, scales_tag=None):
+            codes = keep.tile([P, width], U32, align_bytes=64, name=f"{name}_codes", tag=codes_tag or f"{name}_codes")
+            scales = keep.tile([P, width], U8, align_bytes=64, name=f"{name}_scales", tag=scales_tag or f"{name}_scales")
+            return codes, scales
 
         x_raw, w1_raw, lists = {}, {}, []
 
@@ -61,10 +78,11 @@ def tile_picked_gcn_mlp_relu_sub_l_kernel(
             x_raw[g] = t
 
         def load_w1(c, g):
-            t = keep.tile([P, J, P], F32, name=f"w1_raw{c}_{g}")
+            w1_raw[c, g] = words(f"w1_raw{c}_{g}", KP)
             rows = w1[g * KP : (g + 1) * KP, c * P : (c + 1) * P]
-            nc.sync.dma_start(out=t[:], in_=rows.rearrange("(p j) c -> p j c", j=J))
-            w1_raw[c, g] = t
+            nc.sync.dma_start(
+                out=w1_raw[c, g].rearrange("p (j c) -> p j c", j=J), in_=rows.rearrange("(p j) c -> p j c", j=J)
+            )
 
         def load_list(d):
             t = keep.tile([P, V // 16], U16, name=f"list{d}")
@@ -72,24 +90,20 @@ def tile_picked_gcn_mlp_relu_sub_l_kernel(
             lists.append(t)
 
         gate_raw = keep.tile([D, V], F32)
-        gate_rows = keep.tile([P, V], F32)
-        nc.vector.memset(gate_rows[:], 0.0)
+        gate_rows = keep.tile([P, V], F32, align_bytes=64, tag="after_gate_rows")
         for rows in (slice(0, 4), slice(4, D)):
             nc.sync.dma_start(out=gate_raw[rows, :], in_=gate[rows, 0, :])
         load_x(0)
         load_w1(0, 0)
-        load_w1(0, 1)
         load_x(1)
         load_x(2)
+        load_w1(0, 1)
         load_w1(0, 2)
-        for d in range(3):
+        for g in range(PASSES):
+            load_list(g)
+            load_w1(1, g)
+        for d in range(PASSES, D):
             load_list(d)
-        load_w1(1, 0)
-        load_w1(1, 1)
-        load_list(3)
-        load_w1(1, 2)
-        load_list(4)
-        load_list(5)
         for c in range(2, GROUPS):
             for g in range(PASSES):
                 load_w1(c, g)
@@ -98,169 +112,183 @@ def tile_picked_gcn_mlp_relu_sub_l_kernel(
 
         ident = keep.tile([P, P], F32)
         make_identity(nc, ident[:])
+        for vh in range(TARGET_HALVES):
+            on_scalar(out=gate_rows[:, vh * P : (vh + 1) * P], in_=ident[:])
 
-        prods, stage_first, stage_rest = {}, {}, {}
-        for c in range(GROUPS - 1):
-            if c == 0:
-                prods[c, 0] = keep.tile([P, V], F32, align_bytes=64, name="prod_first")[:]
-                shared = x_raw[PASSES - 1][:].rearrange("p j t -> p (j t)")[:, HALF : HALF + 7 * P]
-            else:
-                prods[c, 0] = prods[c - 1, 1]
-                shared = keep.tile([P, 7 * P], F32, align_bytes=64, name=f"shared{c}")[:]
-            for d in range(1, 4):
-                prods[c, d] = shared[:, (2 * d - 1) * P : (2 * d + 1) * P]
-            raw = w1_raw[c + 1, PASSES - 1][:].rearrange("p j c -> p (j c)")
-            for d in range(4, D):
-                prods[c, d] = raw[:, (d - 4) * V : (d - 3) * V]
-            stage_first[c + 1] = shared[:, : 2 * P]
-            stage_rest[c + 1] = shared[:, 2 * P : 6 * P]
-
-        def operand_tiles(name, width):
-            codes = keep.tile([P, width], U32, align_bytes=64, name=f"{name}_codes")
-            scales = keep.tile([P, width], U8, align_bytes=64, name=f"{name}_scales")
-            return codes, scales
-
-        x_stage = [keep.tile([P, HALF, J], BF16, align_bytes=64, name=f"x_stage{i}")[:] for i in range(2)]
         x_operands = [operand_tiles(f"x{g}", T) for g in range(PASSES)]
 
-        def stage_x(g):
-            interleave(on_vector, x_stage[g % 2], x_raw[g][:, :, NODE_HALVES[0]])
-            interleave(on_scalar, x_stage[1 - g % 2], x_raw[g][:, :, NODE_HALVES[1]])
+        def stage_w1(copy, area, c, g):
+            interleave(copy, as_grouped(area), w1_raw[c, g].rearrange("p (j c) -> p j c", j=J))
 
-        def quantize_x(g, half):
-            codes, scales = x_operands[g]
-            cols = NODE_HALVES[half]
-            quantize(nc, codes[:, cols], scales[:, cols], x_stage[(g + half) % 2])
+        def quantize_w1(c, passes, area, codes_tag=None, scales_tag=None):
+            codes, scales = operand_tiles(f"w1_{c}_{passes[0]}", len(passes) * P, codes_tag, scales_tag)
+            for i, g in enumerate(passes):
+                stage_w1(on_scalar, part(area, i), c, g)
+            quantize(nc, codes[:], scales[:], as_grouped(area))
+            return {g: (codes[:, i * P : (i + 1) * P], scales[:, i * P : (i + 1) * P]) for i, g in enumerate(passes)}
 
-        def quantize_w1_slice(c, g, copy, stage):
-            codes, scales = operand_tiles(f"w1_{c}_{g}", P)
-            interleave(copy, as_grouped(stage), w1_raw[c, g][:])
-            quantize(nc, codes[:], scales[:], as_grouped(stage))
-            return codes[:], scales[:]
-
-        def project_pass(acc, g, codes, scales, cols):
+        def project_pass(acc, g, weights, cols, start, stop):
             x_codes, x_scales = x_operands[g]
+            codes, scales = weights
             nc.tensor.matmul_mx(
                 out=acc,
                 lhsT=codes.bitcast(FP8X4),
                 lhsT_scale=scales,
                 rhs=x_codes[:, cols].bitcast(FP8X4),
                 rhs_scale=x_scales[:, cols],
-                start=(g == 0),
-                stop=(g == PASSES - 1),
+                start=start,
+                stop=stop,
             )
+
+        def relu_on_scalar(out, in_):
+            nc.scalar.activation(out=out, in_=in_, func=RELU)
 
         def spread_gates():
             on_vector(out=gate_rows[:D, :], in_=gate_raw[:])
-            turned = psum_m.tile([P, TARGET_HALVES, P], F32, name="turned", tag="m")
+            turned = bank(7, [P, TARGET_HALVES, P], "turned")
             for vh in range(TARGET_HALVES):
                 nc.tensor.transpose(turned[:, vh, :], gate_rows[:, vh * P : (vh + 1) * P], ident[:])
-            columns = keep.tile([P, TARGET_HALVES, D], F32, name="gate_columns")
+            columns = keep.tile([P, TARGET_HALVES, D], F32, align_bytes=64, name="gate_columns", tag="after_columns")
             on_vector(out=columns[:], in_=turned[:, :, :D])
             gates = []
-            for pair, (tag, copy) in enumerate((("late0", on_vector), ("late1", on_scalar), ("early0", on_scalar))):
-                bank = psum_z.tile([P, 2, V], F32, name="spread", tag=tag)
+            for pair, b in enumerate((2, 0, 1)):
+                spread = bank(b, [P, 2, V], "spread")
                 for i in range(2):
                     d = 2 * pair + i
                     for vh in range(TARGET_HALVES):
                         column = columns[:, vh, d : d + 1].to_broadcast([P, P])
-                        nc.tensor.transpose(bank[:, i, vh * P : (vh + 1) * P], column, ident[:])
+                        nc.tensor.transpose(spread[:, i, vh * P : (vh + 1) * P], column, ident[:])
                 t = keep.tile([P, 2, V], F32, name=f"gate{pair}")
-                copy(out=t[:], in_=bank[:])
+                on_vector(out=t[:], in_=spread[:])
                 gates.extend([t[:, 0, :], t[:, 1, :]])
             return gates
 
         def project_first_group():
+            width = 2 * HALF
+            first = words("x_stage_first", 2 * width, "after_gate_rows")
+            second = words("x_stage_second", width, "after_columns")
+            third = x_raw[1][:].rearrange("p j t -> p (j t)")[:, HALF : HALF + width]
+            areas = ((first[:, :width], first[:, width:]), (first[:, :width], second), (second, third))
             h = keep.tile([P, T], F32, name="h0")
-            banks = [psum_h.tile([P, T], F32, name="hp", tag="hp") for i in range(2)]
-            for g in range(PASSES):
-                stage = keep.tile([P, V], F32, align_bytes=64, name=f"w1_stage{g}")[:]
-                w1_first = g == 1
-                if w1_first:
-                    codes, scales = quantize_w1_slice(0, g, on_scalar, stage)
+            banks = [bank(i, [P, HALF], "h_acc") for i in range(2)]
+
+            def stage_x(g):
+                for area, cols, copy in zip(areas[g], NODE_HALVES, (on_vector, on_scalar)):
+                    interleave(copy, as_grouped(area), x_raw[g][:, :, cols])
+
+            def quantize_x(g, half):
+                codes, scales = x_operands[g]
+                cols = NODE_HALVES[half]
+                quantize(nc, codes[:, cols], scales[:, cols], as_grouped(areas[g][half]))
+
+            def project(g, weights):
+                for acc, cols in zip(banks, NODE_HALVES):
+                    project_pass(acc[:], g, weights, cols, g == 0, g == PASSES - 1)
+
+            for g in range(PASSES - 1):
                 stage_x(g)
                 quantize_x(g, 0)
-                if not w1_first:
-                    codes, scales = quantize_w1_slice(0, g, on_vector if g == PASSES - 1 else on_scalar, stage)
-                project_pass(banks[0][:, :HALF], g, codes, scales, NODE_HALVES[0])
                 quantize_x(g, 1)
-                project_pass(banks[1][:, :HALF], g, codes, scales, NODE_HALVES[1])
-            for bank, cols in zip(banks, NODE_HALVES):
-                nc.vector.tensor_relu(out=h[:, cols], in_=bank[:, :HALF])
+                if g == 0:
+                    project(0, quantize_w1(0, [0], x_raw[0][:, 0, NODE_HALVES[1]])[0])
+            stage_x(2)
+            area = x_raw[2][:, 0, NODE_HALVES[0]]
+            stage_w1(on_vector, area, 0, 1)
+            quantize_x(2, 0)
+            codes, scales = operand_tiles("w1_0_1", P)
+            quantize(nc, codes[:], scales[:], as_grouped(area))
+            project(1, (codes[:], scales[:]))
+            quantize_x(2, 1)
+            project(2, quantize_w1(0, [2], x_raw[2][:, 0, NODE_HALVES[1]], "last_codes0", "last_scales0")[2])
+            for acc, cols, relu in zip(banks, NODE_HALVES, (nc.vector.tensor_relu, relu_on_scalar)):
+                relu(out=h[:, cols], in_=acc[:])
             return h
+
+        prods, late_stage = {}, {}
 
         def project_group(c):
             h = keep.tile([P, T], F32, name=f"h{c}")
-            banks = [psum_h.tile([P, HALF], F32, name="hp", tag="hp") for i in range(2)]
-            codes, scales = quantize_w1_slice(c, 0, on_scalar, stage_first[c])
-            for bank, cols in zip(banks, NODE_HALVES):
-                project_pass(bank[:], 0, codes, scales, cols)
-            codes, scales = operand_tiles(f"w1_{c}_rest", (PASSES - 1) * P)
-            grouped = as_grouped(stage_rest[c])
-            for i in range(PASSES - 1):
-                interleave(on_scalar, grouped[:, i * P : (i + 1) * P, :], w1_raw[c, 1 + i][:])
-            quantize(nc, codes[:], scales[:], grouped)
-            for bank, cols in zip(banks, NODE_HALVES):
-                for i in range(PASSES - 1):
-                    project_pass(bank[:], 1 + i, codes[:, i * P : (i + 1) * P], scales[:, i * P : (i + 1) * P], cols)
-                nc.scalar.activation(out=h[:, cols], in_=bank[:], func=RELU)
+            banks = [bank(2 * c + i, [P, HALF], "h_acc") for i in range(2)]
+            held_codes, held_scales = f"last_codes{c - 1}", f"last_scales{c - 1}"
+            prods[c - 1, 0] = words(f"prod{c - 1}", V)
+            if c < GROUPS - 1:
+                first_area = x_raw[2][:, 1, NODE_HALVES[1]] if c == 1 else part(late_stage[1], 0)
+                weights = quantize_w1(c, [0], first_area, "after_codes_2_0" if c == 2 else None, held_scales)
+                late_stage[c] = words(f"late_stage{c}", (2 if c == 1 else 2 + PASSES) * SLICE_STAGE, held_codes)
+                weights.update(quantize_w1(c, [1], part(late_stage[c], 0)))
+                weights.update(quantize_w1(c, [2], part(late_stage[c], 1), f"last_codes{c}", f"last_scales{c}"))
+                for d in range(1, D - 1):
+                    prods[c - 1, d] = part(w1_raw[c, (d + 1) // 2], (d + 1) % 2)
+                prods[c - 1, D - 1] = part(late_stage[c], 1)
+                order = (0, 1, 2) if c == 1 else (1, 0, 2)
+                for g in order:
+                    for acc, cols in zip(banks, NODE_HALVES):
+                        project_pass(acc[:], g, weights[g], cols, g == order[0], g == order[-1])
+            else:
+                weights = quantize_w1(c, [0, 1], part(late_stage[2], 2, 2), None, held_scales)
+                weights.update(quantize_w1(c, [2], part(late_stage[2], 4), held_codes))
+                for d in range(1, D):
+                    prods[c - 1, d] = words(f"prod{c - 1}_{d}", V)
+                for acc, cols in zip(banks, NODE_HALVES):
+                    for g in reversed(range(PASSES)):
+                        project_pass(acc[:], g, weights[g], cols, g == PASSES - 1, g == 0)
+            for acc, cols in zip(banks, NODE_HALVES):
+                relu_on_scalar(h[:, cols], acc[:])
             return h
 
         def add_transposed(acc, prod, d):
             nc.tensor.matmul(acc, prod, ident[:], start=(d == 0), stop=(d == D - 1), is_transpose=True)
 
-        gates = spread_gates()
-        h = project_first_group()
-
-        zt_words, zt, early, late = [], [], [], []
+        zt_words, zt = [], []
         for vh in range(TARGET_HALVES):
             zt_words.append(keep.tile([P, 2 * P], F32, align_bytes=64, name=f"zt{vh}"))
             zt.append(zt_words[vh][:].bitcast(BF16).rearrange("v (u p e) -> v u p e", u=2, e=2))
-            early.append(psum_z.tile([P, (GROUPS - 1) * P], F32, name=f"early{vh}", tag=f"early{vh}"))
-            late.append(psum_z.tile([P, P], F32, name=f"late{vh}", tag=f"late{vh}"))
 
-        for c in range(GROUPS - 1):
-            h_next = project_group(c + 1)
-            for d in range(D):
-                nc.vector.tensor_tensor(prods[c, d], h[:].indirect(lists[d][:]), gates[d], MULT)
-                for vh in range(TARGET_HALVES):
-                    add_transposed(early[vh][:, c * P : (c + 1) * P], prods[c, d][:, vh * P : (vh + 1) * P], d)
-            h = h_next
-
-        last_prods = keep.tile([P, 8 * P], F32, align_bytes=64)
-        before_w2 = keep.tile([P, N], F32, align_bytes=64, name="before_w2", tag="w2_slot")
-        own = [last_prods[:, i * P : (i + 1) * P] for i in range(8)]
-        half_prods = (
-            [zt_words[0][:, :P], zt_words[1][:, :P]] + own[:4],
-            own[4:7] + [before_w2[:, :P], before_w2[:, P:]] + own[7:],
-        )
-
-        def gather_half(vh):
-            offsets = slice(vh * LIST_COLUMNS, (vh + 1) * LIST_COLUMNS)
-            for d in range(D):
-                prod = half_prods[vh][d]
-                nc.vector.tensor_tensor(prod, h[:].indirect(lists[d][:, offsets]), gates[d][:, vh * P : (vh + 1) * P], MULT)
-                add_transposed(late[vh][:], prod, d)
-
-        def round_sums(copy, vh, acc, first_group, groups):
-            partitions = slice(GROUP_PARTITIONS * first_group, GROUP_PARTITIONS * (first_group + groups))
+        def round_sums(copy, vh, acc, c):
+            partitions = slice(GROUP_PARTITIONS * c, GROUP_PARTITIONS * (c + 1))
             copy(out=zt[vh][:, :, partitions, :], in_=acc.rearrange("v (p u e) -> v u p e", u=2, e=2))
 
-        w2_stage = keep.tile([P, N, J], BF16, align_bytes=64)
+        def gather_whole(h, d, prod, sums):
+            nc.vector.tensor_tensor(prod, h[:].indirect(lists[d][:]), gates[d], MULT)
+            for vh in range(TARGET_HALVES):
+                add_transposed(sums[vh][:], prod[:, vh * P : (vh + 1) * P], d)
+
+        gates = spread_gates()
+        h = project_first_group()
+
+        for c, first_bank in enumerate((2, 4, 2)):
+            h_next = project_group(c + 1)
+            sums = [bank(first_bank + vh, [P, P], "sums") for vh in range(TARGET_HALVES)]
+            for d in range(D):
+                gather_whole(h, d, prods[c, d], sums)
+            for vh in range(TARGET_HALVES):
+                round_sums(on_scalar, vh, sums[vh][:], c)
+            h = h_next
+
+        w2_stage = keep.tile([P, N, J], BF16, align_bytes=64, name="w2_stage", tag="after_codes_2_0")
         interleave(on_scalar, w2_stage[:], w2_raw[:])
-        gather_half(0)
+
+        sums = [bank(vh, [P, P], "sums") for vh in range(TARGET_HALVES)]
+        for d in range(D - SPLIT_LISTS):
+            gather_whole(h, d, words(f"prod3_{d}", V), sums)
+        before_w2 = words("before_w2", N, "w2_codes")
+        own = words("half_prods", (2 * SPLIT_LISTS - 2) * P)
+        own = [own[:, i * P : (i + 1) * P] for i in range(2 * SPLIT_LISTS - 2)]
+        half_prods = own[:-1] + [before_w2[:, :P], before_w2[:, P:]] + own[-1:]
         for vh in range(TARGET_HALVES):
-            round_sums(on_scalar, vh, early[vh][:], 0, GROUPS - 1)
-        gather_half(1)
-        w2_codes = keep.tile([P, N], U32, align_bytes=64, name="w2_codes", tag="w2_slot")
-        w2_scales = keep.tile([P, N], U8, align_bytes=64)
+            offsets = slice(vh * LIST_COLUMNS, (vh + 1) * LIST_COLUMNS)
+            for i, d in enumerate(range(D - SPLIT_LISTS, D)):
+                prod = half_prods[vh * SPLIT_LISTS + i]
+                nc.vector.tensor_tensor(prod, h[:].indirect(lists[d][:, offsets]), gates[d][:, vh * P : (vh + 1) * P], MULT)
+                add_transposed(sums[vh][:], prod, d)
+        w2_codes, w2_scales = operand_tiles("w2", N)
         quantize(nc, w2_codes[:], w2_scales[:], w2_stage[:])
 
         z_codes, z_scales = operand_tiles("z", V)
-        for vh, copy in enumerate((on_scalar, on_vector)):
+        for vh, (copy, out_bank) in enumerate(((on_scalar, 6), (on_vector, 2))):
             cols = slice(vh * P, (vh + 1) * P)
-            round_sums(copy, vh, late[vh][:], GROUPS - 1, 1)
-            back = psum_m.tile([P, 2, P], F32, name="back", tag="m")
+            round_sums(copy, vh, sums[vh][:], GROUPS - 1)
+            back = bank(4 + vh, [P, 2, P], "back")
             for u in range(2):
                 nc.tensor.transpose(back[:, u, :], zt_words[vh][:, u * P : (u + 1) * P], ident[:])
             z_words = keep.tile([P, P, 2], F32, align_bytes=64, name=f"z_words{vh}")
@@ -268,10 +296,7 @@ def tile_picked_gcn_mlp_relu_sub_l_kernel(
             quantize(nc, z_codes[:, cols], z_scales[:, cols], as_grouped(z_words[:].rearrange("p v u -> p (v u)")))
             for mb in range(N // P):
                 rows = slice(mb * P, (mb + 1) * P)
-                if vh == 0:
-                    acc = psum_h.tile([P, P], F32, name="acc", tag="hp")
-                else:
-                    acc = psum_z.tile([P, P], F32, name="acc", tag=f"early{mb}")
+                acc = bank(out_bank + mb, [P, P], "out_acc")
                 nc.tensor.matmul_mx(
                     out=acc[:],
                     lhsT=w2_codes[:, rows].bitcast(FP8X4),

@@ -292,7 +292,7 @@ def tile_picked_gcn_mlp_relu_sub_l_kernel(
             for u in range(2):
                 nc.tensor.transpose(back[:, u, :], zt_words[vh][:, u * P : (u + 1) * P], ident[:])
             z_words = keep.tile([P, P, 2], F32, align_bytes=64, name=f"z_words{vh}")
-            copy(out=z_words[:], in_=back[:].rearrange("p u v -> p v u"))
+            on_scalar(out=z_words[:], in_=back[:].rearrange("p u v -> p v u"))
             quantize(nc, z_codes[:, cols], z_scales[:, cols], as_grouped(z_words[:].rearrange("p v u -> p (v u)")))
             for mb in range(N // P):
                 rows = slice(mb * P, (mb + 1) * P)

@@ -13,6 +13,7 @@ U16 = mybir.dt.uint16
 U8 = mybir.dt.uint8
 FP8X4 = mybir.dt.float8_e4m3fn_x4
 RELU = mybir.ActivationFunctionType.Relu
+COPY = mybir.ActivationFunctionType.Copy
 MULT = mybir.AluOpType.mult
 
 P = 128
@@ -70,7 +71,7 @@ def tile_picked_gcn_mlp_relu_sub_l_kernel(
             scales = keep.tile([P, width], U8, align_bytes=64, name=f"{name}_scales", tag=scales_tag or f"{name}_scales")
             return codes, scales
 
-        x_raw, w1_raw, lists = {}, {}, []
+        x_raw, w1_raw, group_raw, lists = {}, {}, {}, []
 
         def load_x(g):
             t = keep.tile([P, J, T], F32, align_bytes=64, name=f"x_raw{g}")
@@ -78,7 +79,9 @@ def tile_picked_gcn_mlp_relu_sub_l_kernel(
             x_raw[g] = t
 
         def load_w1(c, g):
-            w1_raw[c, g] = words(f"w1_raw{c}_{g}", KP)
+            if c not in group_raw:
+                group_raw[c] = words(f"w1_raw{c}", PASSES * KP)
+            w1_raw[c, g] = group_raw[c][:, g * KP : (g + 1) * KP]
             rows = w1[g * KP : (g + 1) * KP, c * P : (c + 1) * P]
             nc.sync.dma_start(
                 out=w1_raw[c, g].rearrange("p (j c) -> p j c", j=J), in_=rows.rearrange("(p j) c -> p j c", j=J)
@@ -150,7 +153,7 @@ def tile_picked_gcn_mlp_relu_sub_l_kernel(
                 nc.tensor.transpose(turned[:, vh, :], gate_rows[:, vh * P : (vh + 1) * P], ident[:])
             columns = keep.tile([P, TARGET_HALVES, D], F32, align_bytes=64, name="gate_columns", tag="after_columns")
             on_vector(out=columns[:], in_=turned[:, :, :D])
-            gates = []
+            gates, pairs = [], []
             for pair, b in enumerate((2, 0, 1)):
                 spread = bank(b, [P, 2, V], "spread")
                 for i in range(2):
@@ -161,7 +164,8 @@ def tile_picked_gcn_mlp_relu_sub_l_kernel(
                 t = keep.tile([P, 2, V], F32, name=f"gate{pair}")
                 on_vector(out=t[:], in_=spread[:])
                 gates.extend([t[:, 0, :], t[:, 1, :]])
-            return gates
+                pairs.append(t[:].rearrange("p i v -> p (i v)"))
+            return gates, pairs
 
         def project_first_group():
             width = 2 * HALF
@@ -204,91 +208,163 @@ def tile_picked_gcn_mlp_relu_sub_l_kernel(
                 relu(out=h[:, cols], in_=acc[:])
             return h
 
-        prods, late_stage = {}, {}
-
-        def project_group(c):
-            h = keep.tile([P, T], F32, name=f"h{c}")
-            banks = [bank(2 * c + i, [P, HALF], "h_acc") for i in range(2)]
-            held_codes, held_scales = f"last_codes{c - 1}", f"last_scales{c - 1}"
-            prods[c - 1, 0] = words(f"prod{c - 1}", V)
-            if c < GROUPS - 1:
-                first_area = x_raw[2][:, 1, NODE_HALVES[1]] if c == 1 else part(late_stage[1], 0)
-                weights = quantize_w1(c, [0], first_area, "after_codes_2_0" if c == 2 else None, held_scales)
-                late_stage[c] = words(f"late_stage{c}", (2 if c == 1 else 2 + PASSES) * SLICE_STAGE, held_codes)
-                weights.update(quantize_w1(c, [1], part(late_stage[c], 0)))
-                weights.update(quantize_w1(c, [2], part(late_stage[c], 1), f"last_codes{c}", f"last_scales{c}"))
-                for d in range(1, D - 1):
-                    prods[c - 1, d] = part(w1_raw[c, (d + 1) // 2], (d + 1) % 2)
-                prods[c - 1, D - 1] = part(late_stage[c], 1)
-                order = (0, 1, 2) if c == 1 else (1, 0, 2)
-                for g in order:
-                    for acc, cols in zip(banks, NODE_HALVES):
-                        project_pass(acc[:], g, weights[g], cols, g == order[0], g == order[-1])
-            else:
-                weights = quantize_w1(c, [0, 1], part(late_stage[2], 2, 2), None, held_scales)
-                weights.update(quantize_w1(c, [2], part(late_stage[2], 4), held_codes))
-                for d in range(1, D):
-                    prods[c - 1, d] = words(f"prod{c - 1}_{d}", V)
-                for acc, cols in zip(banks, NODE_HALVES):
-                    for g in reversed(range(PASSES)):
-                        project_pass(acc[:], g, weights[g], cols, g == PASSES - 1, g == 0)
-            for acc, cols in zip(banks, NODE_HALVES):
-                relu_on_scalar(h[:, cols], acc[:])
-            return h
-
-        def add_transposed(acc, prod, d):
-            nc.tensor.matmul(acc, prod, ident[:], start=(d == 0), stop=(d == D - 1), is_transpose=True)
+        def add_transposed(acc, prod, first, last):
+            nc.tensor.matmul(acc, prod, ident[:], start=first, stop=last, is_transpose=True)
 
         zt_words, zt = [], []
-        for vh in range(TARGET_HALVES):
-            zt_words.append(keep.tile([P, 2 * P], F32, align_bytes=64, name=f"zt{vh}"))
-            zt.append(zt_words[vh][:].bitcast(BF16).rearrange("v (u p e) -> v u p e", u=2, e=2))
 
-        def round_sums(copy, vh, acc, c):
-            partitions = slice(GROUP_PARTITIONS * c, GROUP_PARTITIONS * (c + 1))
+        def round_sums(copy, vh, acc, first_group, groups):
+            partitions = slice(GROUP_PARTITIONS * first_group, GROUP_PARTITIONS * (first_group + groups))
             copy(out=zt[vh][:, :, partitions, :], in_=acc.rearrange("v (p u e) -> v u p e", u=2, e=2))
 
-        def gather_whole(h, d, prod, sums):
+        def gather_on_vector(prod, h, d):
             nc.vector.tensor_tensor(prod, h[:].indirect(lists[d][:]), gates[d], MULT)
-            for vh in range(TARGET_HALVES):
-                add_transposed(sums[vh][:], prod[:, vh * P : (vh + 1) * P], d)
 
-        gates = spread_gates()
+        def gather_on_scalar(picked, h, offsets):
+            nc.scalar.activation(picked, h[:].indirect(offsets), COPY)
+
+        gates, gate_pairs = spread_gates()
         h = project_first_group()
 
-        for c, first_bank in enumerate((2, 4, 2)):
-            h_next = project_group(c + 1)
-            sums = [bank(first_bank + vh, [P, P], "sums") for vh in range(TARGET_HALVES)]
-            for d in range(D):
-                gather_whole(h, d, prods[c, d], sums)
-            for vh in range(TARGET_HALVES):
-                round_sums(on_scalar, vh, sums[vh][:], c)
-            h = h_next
+        early_sums = {}
+        h_tiles, h_banks, weights = {0: h}, {}, {}
 
-        w2_stage = keep.tile([P, N, J], BF16, align_bytes=64, name="w2_stage", tag="after_codes_2_0")
+        def quantize_slices(n, passes, area, codes_tag=None, scales_tag=None):
+            codes, scales = operand_tiles(f"w1_{n}_{passes[0]}", len(passes) * P, codes_tag, scales_tag)
+            quantize(nc, codes[:], scales[:], as_grouped(area))
+            if n not in h_banks:
+                h_banks[n] = [bank(2 * (n % 3) + i, [P, HALF], "h_acc") for i in range(2)]
+            for i, g in enumerate(passes):
+                cols = slice(i * P, (i + 1) * P)
+                for acc, nodes in zip(h_banks[n], NODE_HALVES):
+                    project_pass(acc[:], g, (codes[:, cols], scales[:, cols]), nodes, g == 0, g == PASSES - 1)
+
+        def relu_group(n):
+            h_tiles[n] = keep.tile([P, T], F32, name=f"h{n}")
+            for acc, nodes in zip(h_banks[n], NODE_HALVES):
+                relu_on_scalar(h_tiles[n][:, nodes], acc[:])
+            early_sums[n - 1] = [bank(2 * (n % 3) + vh, [P, P], "sums") for vh in range(TARGET_HALVES)]
+
+        products = {c: [] for c in range(GROUPS - 1)}
+
+        def add(c, prod):
+            products[c].extend(part(prod, i) for i in range(prod.shape[1] // V))
+
+        def add_group(c):
+            for k, prod in enumerate(products[c]):
+                for vh in range(TARGET_HALVES):
+                    add_transposed(early_sums[c][vh][:], prod[:, vh * P : (vh + 1) * P], k == 0, k == D - 1)
+
+        def fused(c, d, prod):
+            gather_on_vector(prod, h_tiles[c], d)
+            add(c, prod)
+
+        def multiply(c, name, picked, factor):
+            prod = words(name, picked.shape[1])
+            nc.vector.tensor_tensor(prod, picked, factor, MULT)
+            add(c, prod)
+
+        area = x_raw[2][:, 1, NODE_HALVES[1]]
+        stage_w1(on_scalar, area, 1, 0)
+        quantize_slices(1, [0], area, None, "last_scales0")
+        stage_a = words("stage_a", 3 * SLICE_STAGE, "last_codes0")
+        stage_w1(on_scalar, part(stage_a, 0), 1, 1)
+        stage_w1(on_scalar, part(stage_a, 1), 1, 2)
+        picked = part(group_raw[1], 3)
+        gather_on_scalar(picked, h, lists[2][:])
+        stage_w1(on_scalar, part(stage_a, 2), 2, 0)
+        fused(0, 0, words("prod0_0", V))
+        quantize_slices(1, [1], part(stage_a, 0))
+        fused(0, 1, part(group_raw[1], 2))
+        quantize_slices(1, [2], part(stage_a, 1), "last_codes1")
+        relu_group(1)
+        multiply(0, "prod0_2", picked, gates[2])
+        fused(0, 3, part(group_raw[2], 0))
+        quantize_slices(2, [0], part(stage_a, 2))
+        fused(0, 4, part(group_raw[2], 1))
+
+        stage_b = words("stage_b", 3 * SLICE_STAGE, "last_codes1")
+        stage_w1(on_scalar, part(stage_b, 0), 2, 1)
+        stage_w1(on_scalar, part(stage_b, 1), 2, 2)
+        picked = part(group_raw[2], 3, 2)
+        for i in range(2):
+            gather_on_scalar(part(picked, i), h_tiles[1], lists[2 + i][:])
+        stage_w1(on_scalar, part(stage_b, 2), 3, 0)
+        quantize_slices(2, [1], part(stage_b, 0), "middle_codes2")
+        fused(1, 0, part(group_raw[2], 2))
+        quantize_slices(2, [2], part(stage_b, 1), "last_codes2")
+        fused(1, 1, part(group_raw[2], 5))
+        fused(0, 5, words("prod0_5", V, "middle_codes2"))
+        add_group(0)
+        relu_group(2)
+        multiply(1, "prod1_23", picked, gate_pairs[1])
+        quantize_slices(3, [0], part(stage_b, 2))
+        fused(1, 4, part(group_raw[3], 0))
+
+        stage_c = words("stage_c", 2 * SLICE_STAGE, "last_codes2")
+        stage_w1(on_scalar, part(stage_c, 0), 3, 1)
+        stage_w1(on_scalar, part(stage_c, 1), 3, 2)
+        picked = part(group_raw[3], 3, 2)
+        for i in range(2):
+            gather_on_scalar(part(picked, i), h_tiles[2], lists[2 + i][:])
+        quantize_slices(3, [1], part(stage_c, 0), "middle_codes3")
+        fused(2, 0, part(group_raw[3], 2))
+        quantize_slices(3, [2], part(stage_c, 1), "last_codes3", "last_scales3")
+        fused(2, 1, part(group_raw[3], 5))
+        fused(1, 5, words("prod1_5", V, "middle_codes3"))
+        add_group(1)
+        relu_group(3)
+        third = words("picked2_4", V, "last_codes3")
+        gather_on_scalar(third, h_tiles[2], lists[4][:])
+        multiply(2, "prod2_23", picked, gate_pairs[1])
+        fused(2, 5, part(stage_c, 1))
+        multiply(2, "prod2_4", third, gates[4])
+        add_group(2)
+        h = h_tiles[3]
+
+        sums = [bank(6 + vh, [P, P], "sums") for vh in range(TARGET_HALVES)]
+        picked = words("picked3", V)
+        gather_on_scalar(picked, h, lists[2][:])
+        w2_stage = keep.tile([P, N, J], BF16, align_bytes=64, name="w2_stage", tag="last_codes3")
         interleave(on_scalar, w2_stage[:], w2_raw[:])
-
-        sums = [bank(vh, [P, P], "sums") for vh in range(TARGET_HALVES)]
-        for d in range(D - SPLIT_LISTS):
-            gather_whole(h, d, words(f"prod3_{d}", V), sums)
-        before_w2 = words("before_w2", N, "w2_codes")
-        own = words("half_prods", (2 * SPLIT_LISTS - 2) * P)
-        own = [own[:, i * P : (i + 1) * P] for i in range(2 * SPLIT_LISTS - 2)]
-        half_prods = own[:-1] + [before_w2[:, :P], before_w2[:, P:]] + own[-1:]
+        halves = []
         for vh in range(TARGET_HALVES):
             offsets = slice(vh * LIST_COLUMNS, (vh + 1) * LIST_COLUMNS)
-            for i, d in enumerate(range(D - SPLIT_LISTS, D)):
-                prod = half_prods[vh * SPLIT_LISTS + i]
-                nc.vector.tensor_tensor(prod, h[:].indirect(lists[d][:, offsets]), gates[d][:, vh * P : (vh + 1) * P], MULT)
-                add_transposed(sums[vh][:], prod, d)
+            t = words(f"picked3_{vh}", 2 * P, "w2_codes" if vh == 0 else None)
+            for i in range(2):
+                gather_on_scalar(t[:, i * P : (i + 1) * P], h, lists[4 + i][:, offsets])
+            halves.append(t)
+        both = words("zt", 4 * P, "last_scales3")
+        for vh in range(TARGET_HALVES):
+            zt_words.append(both[:, vh * 2 * P : (vh + 1) * 2 * P])
+            zt.append(zt_words[vh].bitcast(BF16).rearrange("v (u p e) -> v u p e", u=2, e=2))
+        for c in range(GROUPS - 1):
+            for vh in range(TARGET_HALVES):
+                round_sums(on_scalar, vh, early_sums[c][vh][:], c, 1)
+        for i, d in enumerate((0, 1, 3, 2)):
+            prod = words(f"prod3_{d}", V)
+            if d == 2:
+                nc.vector.tensor_tensor(prod, picked, gates[d], MULT)
+            else:
+                gather_on_vector(prod, h, d)
+            for vh in range(TARGET_HALVES):
+                add_transposed(sums[vh][:], prod[:, vh * P : (vh + 1) * P], i == 0, False)
+        for vh in range(TARGET_HALVES):
+            prod = words(f"prod3_45_{vh}", 2 * P)
+            pair = gate_pairs[2].rearrange("p (i v) -> p i v", i=2)[:, :, vh * P : (vh + 1) * P]
+            nc.vector.tensor_tensor(
+                prod.rearrange("p (i v) -> p i v", i=2), halves[vh].rearrange("p (i v) -> p i v", i=2), pair, MULT
+            )
+            for i in range(2):
+                add_transposed(sums[vh][:], prod[:, i * P : (i + 1) * P], False, i == 1)
         w2_codes, w2_scales = operand_tiles("w2", N)
         quantize(nc, w2_codes[:], w2_scales[:], w2_stage[:])
 
         z_codes, z_scales = operand_tiles("z", V)
-        for vh, (copy, out_bank) in enumerate(((on_scalar, 6), (on_vector, 2))):
+        for vh, (copy, out_bank) in enumerate(((on_scalar, 4), (on_vector, 0))):
             cols = slice(vh * P, (vh + 1) * P)
-            round_sums(copy, vh, sums[vh][:], GROUPS - 1)
-            back = bank(4 + vh, [P, 2, P], "back")
+            round_sums(copy, vh, sums[vh][:], GROUPS - 1, 1)
+            back = bank(2 + vh, [P, 2, P], "back")
             for u in range(2):
                 nc.tensor.transpose(back[:, u, :], zt_words[vh][:, u * P : (u + 1) * P], ident[:])
             z_words = keep.tile([P, P, 2], F32, align_bytes=64, name=f"z_words{vh}")

@@ -110,8 +110,13 @@ def tile_picked_gcn_mlp_relu_sub_l_kernel(
         for c in range(2, GROUPS):
             for g in range(PASSES):
                 load_w1(c, g)
-        w2_raw = keep.tile([P, J, N], F32)
-        nc.sync.dma_start(out=w2_raw[:], in_=w2.rearrange("(p j) m -> p j m", j=J))
+        w2_raw = []
+        for mb in range(N // P):
+            w2_raw.append(words(f"w2_raw{mb}", KP))
+            nc.sync.dma_start(
+                out=w2_raw[mb].rearrange("p (j c) -> p j c", j=J),
+                in_=w2[:, mb * P : (mb + 1) * P].rearrange("(p j) c -> p j c", j=J),
+            )
 
         ident = keep.tile([P, P], F32)
         make_identity(nc, ident[:])
@@ -212,6 +217,9 @@ def tile_picked_gcn_mlp_relu_sub_l_kernel(
             nc.tensor.matmul(acc, prod, ident[:], start=first, stop=last, is_transpose=True)
 
         zt_words, zt = [], []
+        for vh in range(TARGET_HALVES):
+            zt_words.append(keep.tile([P, 2 * P], F32, align_bytes=64, name=f"zt{vh}"))
+            zt.append(zt_words[vh][:].bitcast(BF16).rearrange("v (u p e) -> v u p e", u=2, e=2))
 
         def round_sums(copy, vh, acc, first_group, groups):
             partitions = slice(GROUP_PARTITIONS * first_group, GROUP_PARTITIONS * (first_group + groups))
@@ -226,14 +234,14 @@ def tile_picked_gcn_mlp_relu_sub_l_kernel(
         gates, gate_pairs = spread_gates()
         h = project_first_group()
 
-        early_sums = {}
+        early_sums = [bank(4 + vh, [P, (GROUPS - 1) * P], "early_sums") for vh in range(TARGET_HALVES)]
         h_tiles, h_banks, weights = {0: h}, {}, {}
 
         def quantize_slices(n, passes, area, codes_tag=None, scales_tag=None):
             codes, scales = operand_tiles(f"w1_{n}_{passes[0]}", len(passes) * P, codes_tag, scales_tag)
             quantize(nc, codes[:], scales[:], as_grouped(area))
             if n not in h_banks:
-                h_banks[n] = [bank(2 * (n % 3) + i, [P, HALF], "h_acc") for i in range(2)]
+                h_banks[n] = [bank(2 * (n % 2) + i, [P, HALF], "h_acc") for i in range(2)]
             for i, g in enumerate(passes):
                 cols = slice(i * P, (i + 1) * P)
                 for acc, nodes in zip(h_banks[n], NODE_HALVES):
@@ -243,17 +251,16 @@ def tile_picked_gcn_mlp_relu_sub_l_kernel(
             h_tiles[n] = keep.tile([P, T], F32, name=f"h{n}")
             for acc, nodes in zip(h_banks[n], NODE_HALVES):
                 relu_on_scalar(h_tiles[n][:, nodes], acc[:])
-            early_sums[n - 1] = [bank(2 * (n % 3) + vh, [P, P], "sums") for vh in range(TARGET_HALVES)]
 
-        products = {c: [] for c in range(GROUPS - 1)}
+        counts = {}
 
         def add(c, prod):
-            products[c].extend(part(prod, i) for i in range(prod.shape[1] // V))
-
-        def add_group(c):
-            for k, prod in enumerate(products[c]):
+            for i in range(prod.shape[1] // V):
+                k = counts.get(c, 0)
                 for vh in range(TARGET_HALVES):
-                    add_transposed(early_sums[c][vh][:], prod[:, vh * P : (vh + 1) * P], k == 0, k == D - 1)
+                    acc = early_sums[vh][:, c * P : (c + 1) * P]
+                    add_transposed(acc, part(prod, i)[:, vh * P : (vh + 1) * P], k == 0, k == D - 1)
+                counts[c] = k + 1
 
         def fused(c, d, prod):
             gather_on_vector(prod, h_tiles[c], d)
@@ -267,80 +274,72 @@ def tile_picked_gcn_mlp_relu_sub_l_kernel(
         area = x_raw[2][:, 1, NODE_HALVES[1]]
         stage_w1(on_scalar, area, 1, 0)
         quantize_slices(1, [0], area, None, "last_scales0")
-        stage_a = words("stage_a", 3 * SLICE_STAGE, "last_codes0")
+        stage_a = words("stage_a", 4 * SLICE_STAGE, "last_codes0")
         stage_w1(on_scalar, part(stage_a, 0), 1, 1)
         stage_w1(on_scalar, part(stage_a, 1), 1, 2)
-        picked = part(group_raw[1], 3)
-        gather_on_scalar(picked, h, lists[2][:])
         stage_w1(on_scalar, part(stage_a, 2), 2, 0)
+        picked = part(group_raw[1], 4)
+        gather_on_scalar(picked, h, lists[2][:])
+        stage_w1(on_scalar, part(stage_a, 3), 2, 1)
         fused(0, 0, words("prod0_0", V))
         quantize_slices(1, [1], part(stage_a, 0))
         fused(0, 1, part(group_raw[1], 2))
         quantize_slices(1, [2], part(stage_a, 1), "last_codes1")
         relu_group(1)
-        multiply(0, "prod0_2", picked, gates[2])
+        quantize_slices(2, [0], part(stage_a, 2), "first_codes2")
         fused(0, 3, part(group_raw[2], 0))
-        quantize_slices(2, [0], part(stage_a, 2))
+        multiply(0, "prod0_2", picked, gates[2])
         fused(0, 4, part(group_raw[2], 1))
+        quantize_slices(2, [1], part(stage_a, 3))
+        fused(0, 5, part(group_raw[2], 2))
 
         stage_b = words("stage_b", 3 * SLICE_STAGE, "last_codes1")
-        stage_w1(on_scalar, part(stage_b, 0), 2, 1)
-        stage_w1(on_scalar, part(stage_b, 1), 2, 2)
-        picked = part(group_raw[2], 3, 2)
+        stage_w1(on_scalar, part(stage_b, 0), 2, 2)
+        stage_w1(on_scalar, part(stage_b, 1), 3, 0)
+        picked = part(group_raw[2], 4, 2)
         for i in range(2):
             gather_on_scalar(part(picked, i), h_tiles[1], lists[2 + i][:])
-        stage_w1(on_scalar, part(stage_b, 2), 3, 0)
-        quantize_slices(2, [1], part(stage_b, 0), "middle_codes2")
-        fused(1, 0, part(group_raw[2], 2))
-        quantize_slices(2, [2], part(stage_b, 1), "last_codes2")
-        fused(1, 1, part(group_raw[2], 5))
-        fused(0, 5, words("prod0_5", V, "middle_codes2"))
-        add_group(0)
+        stage_w1(on_scalar, part(stage_b, 2), 3, 1)
+        quantize_slices(2, [2], part(stage_b, 0), "last_codes2")
         relu_group(2)
+        fused(1, 0, words("prod1_0", V, "first_codes2"))
+        quantize_slices(3, [0], part(stage_b, 1))
+        fused(1, 1, part(group_raw[3], 0))
+        fused(1, 4, part(group_raw[3], 1))
         multiply(1, "prod1_23", picked, gate_pairs[1])
-        quantize_slices(3, [0], part(stage_b, 2))
-        fused(1, 4, part(group_raw[3], 0))
+        quantize_slices(3, [1], part(stage_b, 2))
+        fused(1, 5, part(group_raw[3], 2))
 
+        fused(2, 5, part(group_raw[3], 3))
         stage_c = words("stage_c", 2 * SLICE_STAGE, "last_codes2")
-        stage_w1(on_scalar, part(stage_c, 0), 3, 1)
-        stage_w1(on_scalar, part(stage_c, 1), 3, 2)
-        picked = part(group_raw[3], 3, 2)
+        stage_w1(on_scalar, part(stage_c, 0), 3, 2)
+        w2_stage = part(stage_c, 1)
+        interleave(on_scalar, as_grouped(part(w2_stage, 0)), w2_raw[0].rearrange("p (j c) -> p j c", j=J))
+        picked = part(group_raw[3], 4, 2)
         for i in range(2):
             gather_on_scalar(part(picked, i), h_tiles[2], lists[2 + i][:])
-        quantize_slices(3, [1], part(stage_c, 0), "middle_codes3")
-        fused(2, 0, part(group_raw[3], 2))
-        quantize_slices(3, [2], part(stage_c, 1), "last_codes3", "last_scales3")
-        fused(2, 1, part(group_raw[3], 5))
-        fused(1, 5, words("prod1_5", V, "middle_codes3"))
-        add_group(1)
+        quantize_slices(3, [2], part(stage_c, 0), "last_codes3")
         relu_group(3)
         third = words("picked2_4", V, "last_codes3")
         gather_on_scalar(third, h_tiles[2], lists[4][:])
+        fused(2, 0, part(w2_raw[0], 0))
+        fused(2, 1, part(w2_raw[0], 1))
         multiply(2, "prod2_23", picked, gate_pairs[1])
-        fused(2, 5, part(stage_c, 1))
         multiply(2, "prod2_4", third, gates[4])
-        add_group(2)
         h = h_tiles[3]
 
         sums = [bank(6 + vh, [P, P], "sums") for vh in range(TARGET_HALVES)]
         picked = words("picked3", V)
         gather_on_scalar(picked, h, lists[2][:])
-        w2_stage = keep.tile([P, N, J], BF16, align_bytes=64, name="w2_stage", tag="last_codes3")
-        interleave(on_scalar, w2_stage[:], w2_raw[:])
         halves = []
         for vh in range(TARGET_HALVES):
             offsets = slice(vh * LIST_COLUMNS, (vh + 1) * LIST_COLUMNS)
-            t = words(f"picked3_{vh}", 2 * P, "w2_codes" if vh == 0 else None)
+            t = words(f"picked3_{vh}", 2 * P)
             for i in range(2):
                 gather_on_scalar(t[:, i * P : (i + 1) * P], h, lists[4 + i][:, offsets])
             halves.append(t)
-        both = words("zt", 4 * P, "last_scales3")
         for vh in range(TARGET_HALVES):
-            zt_words.append(both[:, vh * 2 * P : (vh + 1) * 2 * P])
-            zt.append(zt_words[vh].bitcast(BF16).rearrange("v (u p e) -> v u p e", u=2, e=2))
-        for c in range(GROUPS - 1):
-            for vh in range(TARGET_HALVES):
-                round_sums(on_scalar, vh, early_sums[c][vh][:], c, 1)
+            round_sums(on_scalar, vh, early_sums[vh][:], 0, GROUPS - 1)
         for i, d in enumerate((0, 1, 3, 2)):
             prod = words(f"prod3_{d}", V)
             if d == 2:
@@ -357,14 +356,17 @@ def tile_picked_gcn_mlp_relu_sub_l_kernel(
             )
             for i in range(2):
                 add_transposed(sums[vh][:], prod[:, i * P : (i + 1) * P], False, i == 1)
-        w2_codes, w2_scales = operand_tiles("w2", N)
-        quantize(nc, w2_codes[:], w2_scales[:], w2_stage[:])
+        w2_operands = [operand_tiles("w2_0", P, "picked3_0"), operand_tiles("w2_1", P)]
+        quantize(nc, w2_operands[0][0][:], w2_operands[0][1][:], as_grouped(part(w2_stage, 0)))
+        late = words("w2_late", SLICE_STAGE, "picked3_1")
+        interleave(on_vector, as_grouped(late), w2_raw[1].rearrange("p (j c) -> p j c", j=J))
 
+        quantize(nc, w2_operands[1][0][:], w2_operands[1][1][:], as_grouped(late))
         z_codes, z_scales = operand_tiles("z", V)
-        for vh, (copy, out_bank) in enumerate(((on_scalar, 4), (on_vector, 0))):
+        for vh, (copy, out_bank) in enumerate(((on_scalar, 2), (on_vector, 4))):
             cols = slice(vh * P, (vh + 1) * P)
             round_sums(copy, vh, sums[vh][:], GROUPS - 1, 1)
-            back = bank(2 + vh, [P, 2, P], "back")
+            back = bank(vh, [P, 2, P], "back")
             for u in range(2):
                 nc.tensor.transpose(back[:, u, :], zt_words[vh][:, u * P : (u + 1) * P], ident[:])
             z_words = keep.tile([P, P, 2], F32, align_bytes=64, name=f"z_words{vh}")
@@ -375,8 +377,8 @@ def tile_picked_gcn_mlp_relu_sub_l_kernel(
                 acc = bank(out_bank + mb, [P, P], "out_acc")
                 nc.tensor.matmul_mx(
                     out=acc[:],
-                    lhsT=w2_codes[:, rows].bitcast(FP8X4),
-                    lhsT_scale=w2_scales[:, rows],
+                    lhsT=w2_operands[mb][0][:].bitcast(FP8X4),
+                    lhsT_scale=w2_operands[mb][1][:],
                     rhs=z_codes[:, cols].bitcast(FP8X4),
                     rhs_scale=z_scales[:, cols],
                     start=True,

@@ -102,21 +102,13 @@ def tile_picked_gcn_mlp_relu_sub_l_kernel(
         load_x(2)
         load_w1(0, 1)
         load_w1(0, 2)
-        for g in range(PASSES):
-            load_list(g)
-            load_w1(1, g)
-        for d in range(PASSES, D):
+        for d in range(D):
             load_list(d)
-        for c in range(2, GROUPS):
-            for g in range(PASSES):
-                load_w1(c, g)
-        w2_raw = []
-        for mb in range(N // P):
-            w2_raw.append(words(f"w2_raw{mb}", KP))
-            nc.sync.dma_start(
-                out=w2_raw[mb].rearrange("p (j c) -> p j c", j=J),
-                in_=w2[:, mb * P : (mb + 1) * P].rearrange("(p j) c -> p j c", j=J),
-            )
+            load_w1(1 + d // PASSES, d % PASSES)
+        for g in range(PASSES):
+            load_w1(GROUPS - 1, g)
+        w2_raw = keep.tile([P, J, N], F32)
+        nc.sync.dma_start(out=w2_raw[:], in_=w2.rearrange("(p j) m -> p j m", j=J))
 
         ident = keep.tile([P, P], F32)
         make_identity(nc, ident[:])
@@ -217,9 +209,6 @@ def tile_picked_gcn_mlp_relu_sub_l_kernel(
             nc.tensor.matmul(acc, prod, ident[:], start=first, stop=last, is_transpose=True)
 
         zt_words, zt = [], []
-        for vh in range(TARGET_HALVES):
-            zt_words.append(keep.tile([P, 2 * P], F32, align_bytes=64, name=f"zt{vh}"))
-            zt.append(zt_words[vh][:].bitcast(BF16).rearrange("v (u p e) -> v u p e", u=2, e=2))
 
         def round_sums(copy, vh, acc, first_group, groups):
             partitions = slice(GROUP_PARTITIONS * first_group, GROUP_PARTITIONS * (first_group + groups))
@@ -234,14 +223,15 @@ def tile_picked_gcn_mlp_relu_sub_l_kernel(
         gates, gate_pairs = spread_gates()
         h = project_first_group()
 
-        early_sums = [bank(4 + vh, [P, (GROUPS - 1) * P], "early_sums") for vh in range(TARGET_HALVES)]
+        early_sums = [bank(4 + vh, [P, 2 * P], "early_sums") for vh in range(TARGET_HALVES)]
+        first_products = []
         h_tiles, h_banks, weights = {0: h}, {}, {}
 
         def quantize_slices(n, passes, area, codes_tag=None, scales_tag=None):
             codes, scales = operand_tiles(f"w1_{n}_{passes[0]}", len(passes) * P, codes_tag, scales_tag)
             quantize(nc, codes[:], scales[:], as_grouped(area))
             if n not in h_banks:
-                h_banks[n] = [bank(2 * (n % 2) + i, [P, HALF], "h_acc") for i in range(2)]
+                h_banks[n] = [bank((2, 0, 6)[n - 1] + i, [P, HALF], "h_acc") for i in range(2)]
             for i, g in enumerate(passes):
                 cols = slice(i * P, (i + 1) * P)
                 for acc, nodes in zip(h_banks[n], NODE_HALVES):
@@ -255,10 +245,13 @@ def tile_picked_gcn_mlp_relu_sub_l_kernel(
         counts = {}
 
         def add(c, prod):
+            if c == 0:
+                first_products.extend(part(prod, i) for i in range(prod.shape[1] // V))
+                return
             for i in range(prod.shape[1] // V):
                 k = counts.get(c, 0)
                 for vh in range(TARGET_HALVES):
-                    acc = early_sums[vh][:, c * P : (c + 1) * P]
+                    acc = early_sums[vh][:, (c - 1) * P : c * P]
                     add_transposed(acc, part(prod, i)[:, vh * P : (vh + 1) * P], k == 0, k == D - 1)
                 counts[c] = k + 1
 
@@ -271,64 +264,70 @@ def tile_picked_gcn_mlp_relu_sub_l_kernel(
             nc.vector.tensor_tensor(prod, picked, factor, MULT)
             add(c, prod)
 
+        def gather_pair(picked, c):
+            for i in range(2):
+                gather_on_scalar(part(picked, i), h_tiles[c], lists[2 + i][:])
+
         area = x_raw[2][:, 1, NODE_HALVES[1]]
         stage_w1(on_scalar, area, 1, 0)
         quantize_slices(1, [0], area, None, "last_scales0")
-        stage_a = words("stage_a", 4 * SLICE_STAGE, "last_codes0")
+        stage_a = words("stage_a", 2 * SLICE_STAGE, "last_codes0")
         stage_w1(on_scalar, part(stage_a, 0), 1, 1)
         stage_w1(on_scalar, part(stage_a, 1), 1, 2)
-        stage_w1(on_scalar, part(stage_a, 2), 2, 0)
-        picked = part(group_raw[1], 4)
-        gather_on_scalar(picked, h, lists[2][:])
-        stage_w1(on_scalar, part(stage_a, 3), 2, 1)
+        picked = words("picked0", 2 * V)
+        gather_pair(picked, 0)
         fused(0, 0, words("prod0_0", V))
         quantize_slices(1, [1], part(stage_a, 0))
         fused(0, 1, part(group_raw[1], 2))
         quantize_slices(1, [2], part(stage_a, 1), "last_codes1")
         relu_group(1)
-        quantize_slices(2, [0], part(stage_a, 2), "first_codes2")
-        fused(0, 3, part(group_raw[2], 0))
-        multiply(0, "prod0_2", picked, gates[2])
-        fused(0, 4, part(group_raw[2], 1))
-        quantize_slices(2, [1], part(stage_a, 3))
-        fused(0, 5, part(group_raw[2], 2))
+        stage_w1(on_vector, part(group_raw[1], 5), 2, 0)
+        fused(0, 4, part(group_raw[1], 4))
+        quantize_slices(2, [0], part(group_raw[1], 5))
+        multiply(0, "prod0_23", picked, gate_pairs[1])
+        fused(0, 5, part(group_raw[2], 0))
 
         stage_b = words("stage_b", 3 * SLICE_STAGE, "last_codes1")
-        stage_w1(on_scalar, part(stage_b, 0), 2, 2)
-        stage_w1(on_scalar, part(stage_b, 1), 3, 0)
-        picked = part(group_raw[2], 4, 2)
-        for i in range(2):
-            gather_on_scalar(part(picked, i), h_tiles[1], lists[2 + i][:])
-        stage_w1(on_scalar, part(stage_b, 2), 3, 1)
-        quantize_slices(2, [2], part(stage_b, 0), "last_codes2")
+        stage_w1(on_scalar, part(stage_b, 0), 2, 1)
+        stage_w1(on_scalar, part(stage_b, 1), 2, 2)
+        picked = part(group_raw[2], 2, 2)
+        gather_on_scalar(part(picked, 0), h_tiles[1], lists[2][:])
+        stage_w1(on_scalar, part(stage_b, 2), 3, 0)
+        gather_on_scalar(part(picked, 1), h_tiles[1], lists[3][:])
+        quantize_slices(2, [1], part(stage_b, 0))
+        quantize_slices(2, [2], part(stage_b, 1), "last_codes2")
+        first_sums = [bank(2 + vh, [P, P], "first_sums") for vh in range(TARGET_HALVES)]
+        for k, prod in enumerate(first_products):
+            for vh in range(TARGET_HALVES):
+                add_transposed(first_sums[vh][:], prod[:, vh * P : (vh + 1) * P], k == 0, k == D - 1)
         relu_group(2)
-        fused(1, 0, words("prod1_0", V, "first_codes2"))
-        quantize_slices(3, [0], part(stage_b, 1))
-        fused(1, 1, part(group_raw[3], 0))
-        fused(1, 4, part(group_raw[3], 1))
+        fused(1, 0, part(group_raw[2], 4))
+        fused(1, 1, part(group_raw[2], 5))
+        quantize_slices(3, [0], part(stage_b, 2))
+        fused(1, 4, part(group_raw[3], 0))
         multiply(1, "prod1_23", picked, gate_pairs[1])
-        quantize_slices(3, [1], part(stage_b, 2))
-        fused(1, 5, part(group_raw[3], 2))
+        fused(1, 5, part(group_raw[3], 1))
 
-        fused(2, 5, part(group_raw[3], 3))
         stage_c = words("stage_c", 2 * SLICE_STAGE, "last_codes2")
-        stage_w1(on_scalar, part(stage_c, 0), 3, 2)
-        w2_stage = part(stage_c, 1)
-        interleave(on_scalar, as_grouped(part(w2_stage, 0)), w2_raw[0].rearrange("p (j c) -> p j c", j=J))
-        picked = part(group_raw[3], 4, 2)
-        for i in range(2):
-            gather_on_scalar(part(picked, i), h_tiles[2], lists[2 + i][:])
-        quantize_slices(3, [2], part(stage_c, 0), "last_codes3")
-        relu_group(3)
-        third = words("picked2_4", V, "last_codes3")
+        stage_w1(on_scalar, part(stage_c, 0), 3, 1)
+        stage_w1(on_scalar, part(stage_c, 1), 3, 2)
+        picked = part(group_raw[3], 2, 2)
+        gather_pair(picked, 2)
+        third = words("picked2_4", V)
         gather_on_scalar(third, h_tiles[2], lists[4][:])
-        fused(2, 0, part(w2_raw[0], 0))
-        fused(2, 1, part(w2_raw[0], 1))
+        quantize_slices(3, [1], part(stage_c, 0), None, "middle_scales3")
+        quantize_slices(3, [2], part(stage_c, 1), "last_codes3", "last_scales3")
+        relu_group(3)
+        w2_stage = words("w2_stage", SLICE_STAGE, "last_scales3")
+        interleave(on_scalar, as_grouped(w2_stage), w2_raw[:, :, :P])
+        fused(2, 0, part(group_raw[3], 4))
+        fused(2, 1, part(group_raw[3], 5))
         multiply(2, "prod2_23", picked, gate_pairs[1])
+        fused(2, 5, part(stage_c, 0))
         multiply(2, "prod2_4", third, gates[4])
         h = h_tiles[3]
 
-        sums = [bank(6 + vh, [P, P], "sums") for vh in range(TARGET_HALVES)]
+        sums = [bank(vh, [P, P], "sums") for vh in range(TARGET_HALVES)]
         picked = words("picked3", V)
         gather_on_scalar(picked, h, lists[2][:])
         halves = []
@@ -338,8 +337,13 @@ def tile_picked_gcn_mlp_relu_sub_l_kernel(
             for i in range(2):
                 gather_on_scalar(t[:, i * P : (i + 1) * P], h, lists[4 + i][:, offsets])
             halves.append(t)
+        both = words("zt", 4 * P, "middle_scales3")
         for vh in range(TARGET_HALVES):
-            round_sums(on_scalar, vh, early_sums[vh][:], 0, GROUPS - 1)
+            zt_words.append(both[:, vh * 2 * P : (vh + 1) * 2 * P])
+            zt.append(zt_words[vh].bitcast(BF16).rearrange("v (u p e) -> v u p e", u=2, e=2))
+        for vh in range(TARGET_HALVES):
+            round_sums(on_scalar, vh, first_sums[vh][:], 0, 1)
+            round_sums(on_scalar, vh, early_sums[vh][:], 1, 2)
         for i, d in enumerate((0, 1, 3, 2)):
             prod = words(f"prod3_{d}", V)
             if d == 2:
@@ -357,16 +361,16 @@ def tile_picked_gcn_mlp_relu_sub_l_kernel(
             for i in range(2):
                 add_transposed(sums[vh][:], prod[:, i * P : (i + 1) * P], False, i == 1)
         w2_operands = [operand_tiles("w2_0", P, "picked3_0"), operand_tiles("w2_1", P)]
-        quantize(nc, w2_operands[0][0][:], w2_operands[0][1][:], as_grouped(part(w2_stage, 0)))
+        quantize(nc, w2_operands[0][0][:], w2_operands[0][1][:], as_grouped(w2_stage))
         late = words("w2_late", SLICE_STAGE, "picked3_1")
-        interleave(on_vector, as_grouped(late), w2_raw[1].rearrange("p (j c) -> p j c", j=J))
+        interleave(on_vector, as_grouped(late), w2_raw[:, :, P:])
 
         quantize(nc, w2_operands[1][0][:], w2_operands[1][1][:], as_grouped(late))
         z_codes, z_scales = operand_tiles("z", V)
-        for vh, (copy, out_bank) in enumerate(((on_scalar, 2), (on_vector, 4))):
+        for vh, (copy, out_bank) in enumerate(((on_scalar, 6), (on_vector, 4))):
             cols = slice(vh * P, (vh + 1) * P)
             round_sums(copy, vh, sums[vh][:], GROUPS - 1, 1)
-            back = bank(vh, [P, 2, P], "back")
+            back = bank(2 + vh, [P, 2, P], "back")
             for u in range(2):
                 nc.tensor.transpose(back[:, u, :], zt_words[vh][:, u * P : (u + 1) * P], ident[:])
             z_words = keep.tile([P, P, 2], F32, align_bytes=64, name=f"z_words{vh}")

@@ -14,7 +14,7 @@ U8 = mybir.dt.uint8
 FP8X4 = mybir.dt.float8_e4m3fn_x4
 RELU = mybir.ActivationFunctionType.Relu
 COPY = mybir.ActivationFunctionType.Copy
-MULT = mybir.AluOpType.mult
+MULT, ADD, MAX = mybir.AluOpType.mult, mybir.AluOpType.add, mybir.AluOpType.max
 
 P = 128
 J = 4
@@ -27,7 +27,8 @@ NODE_HALVES = (slice(0, HALF), slice(HALF, T))
 LIST_COLUMNS = P // 16
 GROUP_PARTITIONS = P // J
 SLICE_STAGE = KP // 2
-SPLIT_LISTS = 2
+PLAIN_LIST = 2
+GATED = (0, 1, 3, 4, 5)
 
 
 def interleave(copy, grouped, raw):
@@ -148,25 +149,41 @@ def tile_picked_gcn_mlp_relu_sub_l_kernel(
             turned = bank(7, [P, TARGET_HALVES, P], "turned")
             for vh in range(TARGET_HALVES):
                 nc.tensor.transpose(turned[:, vh, :], gate_rows[:, vh * P : (vh + 1) * P], ident[:])
-            columns = keep.tile([P, TARGET_HALVES, D], F32, align_bytes=64, name="gate_columns", tag="after_columns")
-            on_vector(out=columns[:], in_=turned[:, :, :D])
-            gates, pairs = [], []
-            for pair, b in enumerate((2, 0, 1)):
-                spread = bank(b, [P, 2, V], "spread")
-                for i in range(2):
-                    d = 2 * pair + i
+            columns = keep.tile([P, TARGET_HALVES, D + 1], F32, align_bytes=64, name="gate_columns")
+            nc.gpsimd.memset(columns[:, :, D:], 2.0**-102)
+            on_vector(out=columns[:, :, :D], in_=turned[:, :, :D])
+            own = columns[:, :, PLAIN_LIST]
+            small = keep.tile([P, 4, TARGET_HALVES], F32, name="gate_guard")
+            top, size, half_sign, guarded = (small[:, i, :] for i in range(4))
+            nc.vector.tensor_reduce(top, columns[:], mybir.AxisListType.X, MAX, apply_absolute_value=True)
+            nc.vector.scalar_tensor_tensor(size, own, -1.0, own, MULT, MAX)
+            nc.vector.tensor_scalar(half_sign, own, 0.0, 0.5, mybir.AluOpType.is_ge, mybir.AluOpType.subtract)
+            nc.vector.scalar_tensor_tensor(guarded, top, 2.0**-24, size, MULT, MAX)
+            along_lists = [P, TARGET_HALVES, D]
+            signed = keep.tile(along_lists, F32, align_bytes=64, name="signed", tag="after_ratios")
+            nc.vector.tensor_tensor(signed[:], columns[:, :, :D], half_sign.unsqueeze(2).to_broadcast(along_lists), MULT)
+            inverse = keep.tile([P, TARGET_HALVES], F32, name="inverse")
+            nc.vector.reciprocal(inverse[:], guarded)
+            factor = keep.tile([P, TARGET_HALVES], F32, name="factor")
+            nc.vector.scalar_tensor_tensor(factor[:], half_sign, 2.0, guarded, MULT, MULT)
+            ratios = keep.tile(along_lists, F32, align_bytes=64, name="ratios", tag="after_columns")
+            nc.vector.scalar_tensor_tensor(
+                ratios[:], signed[:], 2.0, inverse[:].unsqueeze(2).to_broadcast(along_lists), MULT, MULT
+            )
+            spread_all = words("gates", len(GATED) * V)
+            for first, b in ((0, 2), (2, 0), (4, 1)):
+                ds = GATED[first : first + 2]
+                spread = bank(b, [P, len(ds) * V], "spread")
+                for i, d in enumerate(ds):
                     for vh in range(TARGET_HALVES):
-                        column = columns[:, vh, d : d + 1].to_broadcast([P, P])
-                        nc.tensor.transpose(spread[:, i, vh * P : (vh + 1) * P], column, ident[:])
-                t = keep.tile([P, 2, V], F32, name=f"gate{pair}")
-                on_vector(out=t[:], in_=spread[:])
-                gates.extend([t[:, 0, :], t[:, 1, :]])
-                pairs.append(t[:].rearrange("p i v -> p (i v)"))
-            return gates, pairs
+                        column = ratios[:, vh, d : d + 1].to_broadcast([P, P])
+                        nc.tensor.transpose(spread[:, i * V + vh * P : i * V + (vh + 1) * P], column, ident[:])
+                on_vector(out=part(spread_all, first, len(ds)), in_=spread[:])
+            return spread_all, factor
 
         def project_first_group():
             width = 2 * HALF
-            first = words("x_stage_first", 2 * width, "after_gate_rows")
+            first = words("x_stage_first", 2 * width, "after_ratios")
             second = words("x_stage_second", width, "after_columns")
             third = x_raw[1][:].rearrange("p j t -> p (j t)")[:, HALF : HALF + width]
             areas = ((first[:, :width], first[:, width:]), (first[:, :width], second), (second, third))
@@ -210,9 +227,15 @@ def tile_picked_gcn_mlp_relu_sub_l_kernel(
 
         zt_words, zt = [], []
 
+        def scaled_on_scalar(out, in_, vh):
+            nc.scalar.activation(out, in_, COPY, scale=factor[:, vh : vh + 1])
+
+        def scaled_on_vector(out, in_, vh):
+            nc.vector.tensor_scalar(out, in_, factor[:, vh : vh + 1], None, MULT)
+
         def round_sums(copy, vh, acc, first_group, groups):
             partitions = slice(GROUP_PARTITIONS * first_group, GROUP_PARTITIONS * (first_group + groups))
-            copy(out=zt[vh][:, :, partitions, :], in_=acc.rearrange("v (p u e) -> v u p e", u=2, e=2))
+            copy(zt[vh][:, :, partitions, :], acc.rearrange("v (p u e) -> v u p e", u=2, e=2), vh)
 
         def gather_on_vector(prod, h, d):
             nc.vector.tensor_tensor(prod, h[:].indirect(lists[d][:]), gates[d], MULT)
@@ -220,7 +243,8 @@ def tile_picked_gcn_mlp_relu_sub_l_kernel(
         def gather_on_scalar(picked, h, offsets):
             nc.scalar.activation(picked, h[:].indirect(offsets), COPY)
 
-        gates, gate_pairs = spread_gates()
+        spread_all, factor = spread_gates()
+        gates = {d: part(spread_all, i) for i, d in enumerate(GATED)}
         h = project_first_group()
 
         early_sums = [bank(4 + vh, [P, 2 * P], "early_sums") for vh in range(TARGET_HALVES)]
@@ -264,36 +288,34 @@ def tile_picked_gcn_mlp_relu_sub_l_kernel(
             nc.vector.tensor_tensor(prod, picked, factor, MULT)
             add(c, prod)
 
-        def gather_pair(picked, c):
-            for i in range(2):
-                gather_on_scalar(part(picked, i), h_tiles[c], lists[2 + i][:])
-
         area = x_raw[2][:, 1, NODE_HALVES[1]]
         stage_w1(on_scalar, area, 1, 0)
         quantize_slices(1, [0], area, None, "last_scales0")
-        stage_a = words("stage_a", 2 * SLICE_STAGE, "last_codes0")
+        stage_a = words("stage_a", 3 * SLICE_STAGE, "last_codes0")
         stage_w1(on_scalar, part(stage_a, 0), 1, 1)
         stage_w1(on_scalar, part(stage_a, 1), 1, 2)
-        picked = words("picked0", 2 * V)
-        gather_pair(picked, 0)
+        plain = words("plain0", V)
+        gather_on_scalar(plain, h, lists[2][:])
+        stage_w1(on_scalar, part(stage_a, 2), 2, 0)
         fused(0, 0, words("prod0_0", V))
         quantize_slices(1, [1], part(stage_a, 0))
         fused(0, 1, part(group_raw[1], 2))
         quantize_slices(1, [2], part(stage_a, 1), "last_codes1")
         relu_group(1)
-        stage_w1(on_vector, part(group_raw[1], 5), 2, 0)
-        fused(0, 4, part(group_raw[1], 4))
-        quantize_slices(2, [0], part(group_raw[1], 5))
-        multiply(0, "prod0_23", picked, gate_pairs[1])
+        add(0, plain)
+        fused(0, 3, part(group_raw[1], 4))
+        fused(0, 4, part(group_raw[1], 5))
+        quantize_slices(2, [0], part(stage_a, 2))
         fused(0, 5, part(group_raw[2], 0))
 
-        stage_b = words("stage_b", 3 * SLICE_STAGE, "last_codes1")
+        stage_b = words("stage_b", 4 * SLICE_STAGE, "last_codes1")
         stage_w1(on_scalar, part(stage_b, 0), 2, 1)
         stage_w1(on_scalar, part(stage_b, 1), 2, 2)
-        picked = part(group_raw[2], 2, 2)
-        gather_on_scalar(part(picked, 0), h_tiles[1], lists[2][:])
         stage_w1(on_scalar, part(stage_b, 2), 3, 0)
-        gather_on_scalar(part(picked, 1), h_tiles[1], lists[3][:])
+        stage_w1(on_scalar, part(stage_b, 3), 3, 1)
+        plain = part(group_raw[2], 2)
+        gather_on_scalar(plain, h_tiles[1], lists[2][:])
+        fused(1, 0, part(group_raw[2], 1))
         quantize_slices(2, [1], part(stage_b, 0))
         quantize_slices(2, [2], part(stage_b, 1), "last_codes2")
         first_sums = [bank(2 + vh, [P, P], "first_sums") for vh in range(TARGET_HALVES)]
@@ -301,35 +323,37 @@ def tile_picked_gcn_mlp_relu_sub_l_kernel(
             for vh in range(TARGET_HALVES):
                 add_transposed(first_sums[vh][:], prod[:, vh * P : (vh + 1) * P], k == 0, k == D - 1)
         relu_group(2)
-        fused(1, 0, part(group_raw[2], 4))
-        fused(1, 1, part(group_raw[2], 5))
-        quantize_slices(3, [0], part(stage_b, 2))
-        fused(1, 4, part(group_raw[3], 0))
-        multiply(1, "prod1_23", picked, gate_pairs[1])
-        fused(1, 5, part(group_raw[3], 1))
+        fused(1, 1, part(group_raw[2], 4))
+        quantize_slices(3, [0, 1], part(stage_b, 2, 2))
+        fused(1, 4, part(group_raw[3], 2))
+        add(1, plain)
+        fused(1, 5, part(group_raw[3], 3))
 
         stage_c = words("stage_c", 2 * SLICE_STAGE, "last_codes2")
-        stage_w1(on_scalar, part(stage_c, 0), 3, 1)
-        stage_w1(on_scalar, part(stage_c, 1), 3, 2)
-        picked = part(group_raw[3], 2, 2)
-        gather_pair(picked, 2)
-        third = words("picked2_4", V)
-        gather_on_scalar(third, h_tiles[2], lists[4][:])
-        quantize_slices(3, [1], part(stage_c, 0), None, "middle_scales3")
-        quantize_slices(3, [2], part(stage_c, 1), "last_codes3", "last_scales3")
+        stage_w1(on_scalar, part(stage_c, 0), 3, 2)
+        picked, plain = part(stage_c, 1), words("plain2", V)
+        gather_on_scalar(picked, h_tiles[1], lists[3][:])
+        gather_on_scalar(plain, h_tiles[2], lists[2][:])
+        first = words("prod2_0", V)
+        gather_on_vector(first, h_tiles[2], 0)
+        quantize_slices(3, [2], part(stage_c, 0), "last_codes3", "last_scales3")
         relu_group(3)
-        w2_stage = words("w2_stage", SLICE_STAGE, "last_scales3")
-        interleave(on_scalar, as_grouped(w2_stage), w2_raw[:, :, :P])
-        fused(2, 0, part(group_raw[3], 4))
-        fused(2, 1, part(group_raw[3], 5))
-        multiply(2, "prod2_23", picked, gate_pairs[1])
+        multiply(1, "prod1_3", picked, gates[3])
+        add(2, first)
+        picked = words("picked2", V, "last_codes3")
+        gather_on_scalar(picked, h_tiles[2], lists[3][:])
+        fused(2, 1, part(group_raw[3], 4))
+        add(2, plain)
+        fused(2, 4, part(group_raw[3], 5))
         fused(2, 5, part(stage_c, 0))
-        multiply(2, "prod2_4", third, gates[4])
+        multiply(2, "prod2_3", picked, gates[3])
         h = h_tiles[3]
 
         sums = [bank(vh, [P, P], "sums") for vh in range(TARGET_HALVES)]
-        picked = words("picked3", V)
-        gather_on_scalar(picked, h, lists[2][:])
+        plain = words("plain3", V)
+        gather_on_scalar(plain, h, lists[2][:])
+        w2_stage = words("w2_stage", SLICE_STAGE, "last_scales3")
+        interleave(on_scalar, as_grouped(w2_stage), w2_raw[:, :, :P])
         halves = []
         for vh in range(TARGET_HALVES):
             offsets = slice(vh * LIST_COLUMNS, (vh + 1) * LIST_COLUMNS)
@@ -337,24 +361,23 @@ def tile_picked_gcn_mlp_relu_sub_l_kernel(
             for i in range(2):
                 gather_on_scalar(t[:, i * P : (i + 1) * P], h, lists[4 + i][:, offsets])
             halves.append(t)
-        both = words("zt", 4 * P, "middle_scales3")
+        for i, d in enumerate((0, 2, 1, 3)):
+            prod = plain
+            if d != 2:
+                prod = words(f"prod3_{d}", V)
+                gather_on_vector(prod, h, d)
+            for vh in range(TARGET_HALVES):
+                add_transposed(sums[vh][:], prod[:, vh * P : (vh + 1) * P], i == 0, False)
+        both = words("zt", 4 * P, "plain3")
         for vh in range(TARGET_HALVES):
             zt_words.append(both[:, vh * 2 * P : (vh + 1) * 2 * P])
             zt.append(zt_words[vh].bitcast(BF16).rearrange("v (u p e) -> v u p e", u=2, e=2))
         for vh in range(TARGET_HALVES):
-            round_sums(on_scalar, vh, first_sums[vh][:], 0, 1)
-            round_sums(on_scalar, vh, early_sums[vh][:], 1, 2)
-        for i, d in enumerate((0, 1, 3, 2)):
-            prod = words(f"prod3_{d}", V)
-            if d == 2:
-                nc.vector.tensor_tensor(prod, picked, gates[d], MULT)
-            else:
-                gather_on_vector(prod, h, d)
-            for vh in range(TARGET_HALVES):
-                add_transposed(sums[vh][:], prod[:, vh * P : (vh + 1) * P], i == 0, False)
+            round_sums(scaled_on_scalar, vh, first_sums[vh][:], 0, 1)
+            round_sums(scaled_on_scalar, vh, early_sums[vh][:], 1, 2)
         for vh in range(TARGET_HALVES):
             prod = words(f"prod3_45_{vh}", 2 * P)
-            pair = gate_pairs[2].rearrange("p (i v) -> p i v", i=2)[:, :, vh * P : (vh + 1) * P]
+            pair = part(spread_all, 3, 2).rearrange("p (i v) -> p i v", i=2)[:, :, vh * P : (vh + 1) * P]
             nc.vector.tensor_tensor(
                 prod.rearrange("p (i v) -> p i v", i=2), halves[vh].rearrange("p (i v) -> p i v", i=2), pair, MULT
             )
@@ -364,12 +387,12 @@ def tile_picked_gcn_mlp_relu_sub_l_kernel(
         quantize(nc, w2_operands[0][0][:], w2_operands[0][1][:], as_grouped(w2_stage))
         late = words("w2_late", SLICE_STAGE, "picked3_1")
         interleave(on_vector, as_grouped(late), w2_raw[:, :, P:])
-
         quantize(nc, w2_operands[1][0][:], w2_operands[1][1][:], as_grouped(late))
+
         z_codes, z_scales = operand_tiles("z", V)
         for vh, (copy, out_bank) in enumerate(((on_scalar, 6), (on_vector, 4))):
             cols = slice(vh * P, (vh + 1) * P)
-            round_sums(copy, vh, sums[vh][:], GROUPS - 1, 1)
+            round_sums((scaled_on_scalar, scaled_on_vector)[vh], vh, sums[vh][:], GROUPS - 1, 1)
             back = bank(2 + vh, [P, 2, P], "back")
             for u in range(2):
                 nc.tensor.transpose(back[:, u, :], zt_words[vh][:, u * P : (u + 1) * P], ident[:])

@@ -313,9 +313,11 @@ def tile_picked_gcn_mlp_relu_sub_l_kernel(
         stage_w1(on_scalar, part(stage_b, 1), 2, 2)
         stage_w1(on_scalar, part(stage_b, 2), 3, 0)
         stage_w1(on_scalar, part(stage_b, 3), 3, 1)
-        plain = part(group_raw[2], 2)
+        plain, picked = part(group_raw[2], 2), part(group_raw[3], 1)
         gather_on_scalar(plain, h_tiles[1], lists[2][:])
+        gather_on_scalar(picked, h_tiles[1], lists[3][:])
         fused(1, 0, part(group_raw[2], 1))
+        fused(1, 1, part(group_raw[2], 3))
         quantize_slices(2, [1], part(stage_b, 0))
         quantize_slices(2, [2], part(stage_b, 1), "last_codes2")
         first_sums = [bank(2 + vh, [P, P], "first_sums") for vh in range(TARGET_HALVES)]
@@ -323,41 +325,35 @@ def tile_picked_gcn_mlp_relu_sub_l_kernel(
             for vh in range(TARGET_HALVES):
                 add_transposed(first_sums[vh][:], prod[:, vh * P : (vh + 1) * P], k == 0, k == D - 1)
         relu_group(2)
-        fused(1, 1, part(group_raw[2], 4))
+        fused(1, 4, part(group_raw[3], 0))
         quantize_slices(3, [0, 1], part(stage_b, 2, 2))
-        fused(1, 4, part(group_raw[3], 2))
+        fused(1, 5, part(group_raw[3], 2))
         add(1, plain)
-        fused(1, 5, part(group_raw[3], 3))
-
-        stage_c = words("stage_c", 2 * SLICE_STAGE, "last_codes2")
-        stage_w1(on_scalar, part(stage_c, 0), 3, 2)
-        picked, plain = part(stage_c, 1), words("plain2", V)
-        gather_on_scalar(picked, h_tiles[1], lists[3][:])
-        gather_on_scalar(plain, h_tiles[2], lists[2][:])
-        first = words("prod2_0", V)
-        gather_on_vector(first, h_tiles[2], 0)
-        quantize_slices(3, [2], part(stage_c, 0), "last_codes3", "last_scales3")
-        relu_group(3)
         multiply(1, "prod1_3", picked, gates[3])
-        add(2, first)
-        picked = words("picked2", V, "last_codes3")
+
+        stage_c = words("stage_c", 3 * SLICE_STAGE, "last_codes2")
+        stage_w1(on_scalar, part(stage_c, 0), 3, 2)
+        plain, picked = part(stage_c, 1), part(stage_c, 2)
+        gather_on_scalar(plain, h_tiles[2], lists[2][:])
         gather_on_scalar(picked, h_tiles[2], lists[3][:])
+        fused(2, 0, words("prod2_0", V))
+        quantize_slices(3, [2], part(stage_c, 0), "last_codes3")
+        relu_group(3)
         fused(2, 1, part(group_raw[3], 4))
         add(2, plain)
         fused(2, 4, part(group_raw[3], 5))
-        fused(2, 5, part(stage_c, 0))
         multiply(2, "prod2_3", picked, gates[3])
+        fused(2, 5, part(stage_c, 0))
         h = h_tiles[3]
 
         sums = [bank(vh, [P, P], "sums") for vh in range(TARGET_HALVES)]
         plain = words("plain3", V)
         gather_on_scalar(plain, h, lists[2][:])
-        w2_stage = words("w2_stage", SLICE_STAGE, "last_scales3")
-        interleave(on_scalar, as_grouped(w2_stage), w2_raw[:, :, :P])
         halves = []
+        picked_last = words("picked_last", 2 * SLICE_STAGE)
         for vh in range(TARGET_HALVES):
             offsets = slice(vh * LIST_COLUMNS, (vh + 1) * LIST_COLUMNS)
-            t = words(f"picked3_{vh}", 2 * P)
+            t = part(picked_last, vh)
             for i in range(2):
                 gather_on_scalar(t[:, i * P : (i + 1) * P], h, lists[4 + i][:, offsets])
             halves.append(t)
@@ -383,16 +379,14 @@ def tile_picked_gcn_mlp_relu_sub_l_kernel(
             )
             for i in range(2):
                 add_transposed(sums[vh][:], prod[:, i * P : (i + 1) * P], False, i == 1)
-        w2_operands = [operand_tiles("w2_0", P, "picked3_0"), operand_tiles("w2_1", P)]
-        quantize(nc, w2_operands[0][0][:], w2_operands[0][1][:], as_grouped(w2_stage))
-        late = words("w2_late", SLICE_STAGE, "picked3_1")
-        interleave(on_vector, as_grouped(late), w2_raw[:, :, P:])
-        quantize(nc, w2_operands[1][0][:], w2_operands[1][1][:], as_grouped(late))
-
+            interleave(on_vector, as_grouped(halves[vh]), w2_raw[:, :, vh * P : (vh + 1) * P])
+        w2_codes, w2_scales = operand_tiles("w2", N)
         z_codes, z_scales = operand_tiles("z", V)
+        for vh, scaled in enumerate((scaled_on_scalar, scaled_on_vector)):
+            round_sums(scaled, vh, sums[vh][:], GROUPS - 1, 1)
+        quantize(nc, w2_codes[:], w2_scales[:], as_grouped(picked_last))
         for vh, (copy, out_bank) in enumerate(((on_scalar, 6), (on_vector, 4))):
             cols = slice(vh * P, (vh + 1) * P)
-            round_sums((scaled_on_scalar, scaled_on_vector)[vh], vh, sums[vh][:], GROUPS - 1, 1)
             back = bank(2 + vh, [P, 2, P], "back")
             for u in range(2):
                 nc.tensor.transpose(back[:, u, :], zt_words[vh][:, u * P : (u + 1) * P], ident[:])
@@ -404,8 +398,8 @@ def tile_picked_gcn_mlp_relu_sub_l_kernel(
                 acc = bank(out_bank + mb, [P, P], "out_acc")
                 nc.tensor.matmul_mx(
                     out=acc[:],
-                    lhsT=w2_operands[mb][0][:].bitcast(FP8X4),
-                    lhsT_scale=w2_operands[mb][1][:],
+                    lhsT=w2_codes[:, rows].bitcast(FP8X4),
+                    lhsT_scale=w2_scales[:, rows],
                     rhs=z_codes[:, cols].bitcast(FP8X4),
                     rhs_scale=z_scales[:, cols],
                     start=True,

@@ -291,12 +291,13 @@ def tile_picked_gcn_mlp_relu_sub_l_kernel(
         area = x_raw[2][:, 1, NODE_HALVES[1]]
         stage_w1(on_scalar, area, 1, 0)
         quantize_slices(1, [0], area, None, "last_scales0")
-        stage_a = words("stage_a", 3 * SLICE_STAGE, "last_codes0")
+        stage_a = words("stage_a", 4 * SLICE_STAGE, "last_codes0")
         stage_w1(on_scalar, part(stage_a, 0), 1, 1)
         stage_w1(on_scalar, part(stage_a, 1), 1, 2)
+        stage_w1(on_scalar, part(stage_a, 2), 2, 0)
         plain = words("plain0", V)
         gather_on_scalar(plain, h, lists[2][:])
-        stage_w1(on_scalar, part(stage_a, 2), 2, 0)
+        stage_w1(on_scalar, part(stage_a, 3), 2, 1)
         fused(0, 0, words("prod0_0", V))
         quantize_slices(1, [1], part(stage_a, 0))
         fused(0, 1, part(group_raw[1], 2))
@@ -304,29 +305,29 @@ def tile_picked_gcn_mlp_relu_sub_l_kernel(
         relu_group(1)
         add(0, plain)
         fused(0, 3, part(group_raw[1], 4))
-        fused(0, 4, part(group_raw[1], 5))
         quantize_slices(2, [0], part(stage_a, 2))
-        fused(0, 5, part(group_raw[2], 0))
+        fused(0, 4, part(group_raw[2], 0))
+        fused(0, 5, part(group_raw[2], 1))
+        quantize_slices(2, [1], part(stage_a, 3))
 
-        stage_b = words("stage_b", 4 * SLICE_STAGE, "last_codes1")
-        stage_w1(on_scalar, part(stage_b, 0), 2, 1)
-        stage_w1(on_scalar, part(stage_b, 1), 2, 2)
-        stage_w1(on_scalar, part(stage_b, 2), 3, 0)
-        stage_w1(on_scalar, part(stage_b, 3), 3, 1)
-        plain, picked = part(group_raw[2], 2), part(group_raw[3], 1)
+        stage_b = words("stage_b", 3 * SLICE_STAGE, "last_codes1")
+        stage_w1(on_scalar, part(stage_b, 0), 2, 2)
+        stage_w1(on_scalar, part(stage_b, 1), 3, 0)
+        stage_w1(on_scalar, part(stage_b, 2), 3, 1)
+        plain, picked = part(group_raw[2], 3), part(group_raw[3], 1)
         gather_on_scalar(plain, h_tiles[1], lists[2][:])
         gather_on_scalar(picked, h_tiles[1], lists[3][:])
-        fused(1, 0, part(group_raw[2], 1))
-        fused(1, 1, part(group_raw[2], 3))
-        quantize_slices(2, [1], part(stage_b, 0))
-        quantize_slices(2, [2], part(stage_b, 1), "last_codes2")
+        fused(1, 0, part(group_raw[2], 2))
+        quantize_slices(2, [2], part(stage_b, 0), "last_codes2")
         first_sums = [bank(2 + vh, [P, P], "first_sums") for vh in range(TARGET_HALVES)]
         for k, prod in enumerate(first_products):
             for vh in range(TARGET_HALVES):
                 add_transposed(first_sums[vh][:], prod[:, vh * P : (vh + 1) * P], k == 0, k == D - 1)
         relu_group(2)
+        fused(1, 1, part(group_raw[2], 4))
+        quantize_slices(3, [0], part(stage_b, 1))
         fused(1, 4, part(group_raw[3], 0))
-        quantize_slices(3, [0, 1], part(stage_b, 2, 2))
+        quantize_slices(3, [1], part(stage_b, 2))
         fused(1, 5, part(group_raw[3], 2))
         add(1, plain)
         multiply(1, "prod1_3", picked, gates[3])

@@ -247,8 +247,7 @@ def tile_picked_gcn_mlp_relu_sub_l_kernel(
         gates = {d: part(spread_all, i) for i, d in enumerate(GATED)}
         h = project_first_group()
 
-        early_sums = [bank(4 + vh, [P, 2 * P], "early_sums") for vh in range(TARGET_HALVES)]
-        first_products = []
+        sum_tiles, held_products = {}, []
         h_tiles, h_banks, weights = {0: h}, {}, {}
 
         def quantize_slices(n, passes, area, codes_tag=None, scales_tag=None):
@@ -269,13 +268,13 @@ def tile_picked_gcn_mlp_relu_sub_l_kernel(
         counts = {}
 
         def add(c, prod):
-            if c == 0:
-                first_products.extend(part(prod, i) for i in range(prod.shape[1] // V))
+            if c not in sum_tiles:
+                held_products.append((c, prod))
                 return
             for i in range(prod.shape[1] // V):
                 k = counts.get(c, 0)
                 for vh in range(TARGET_HALVES):
-                    acc = early_sums[vh][:, (c - 1) * P : c * P]
+                    acc = sum_tiles[c][vh]
                     add_transposed(acc, part(prod, i)[:, vh * P : (vh + 1) * P], k == 0, k == D - 1)
                 counts[c] = k + 1
 
@@ -319,10 +318,13 @@ def tile_picked_gcn_mlp_relu_sub_l_kernel(
         gather_on_scalar(picked, h_tiles[1], lists[3][:])
         fused(1, 0, part(group_raw[2], 2))
         quantize_slices(2, [2], part(stage_b, 0), "last_codes2")
-        first_sums = [bank(2 + vh, [P, P], "first_sums") for vh in range(TARGET_HALVES)]
-        for k, prod in enumerate(first_products):
-            for vh in range(TARGET_HALVES):
-                add_transposed(first_sums[vh][:], prod[:, vh * P : (vh + 1) * P], k == 0, k == D - 1)
+        first_sums = [bank(2 + vh, [P, 2 * P], "first_sums") for vh in range(TARGET_HALVES)]
+        third_sums = [bank(4 + vh, [P, P], "third_sums") for vh in range(TARGET_HALVES)]
+        sum_tiles[0] = [t[:, :P] for t in first_sums]
+        sum_tiles[1] = [t[:, P:] for t in first_sums]
+        sum_tiles[2] = [t[:] for t in third_sums]
+        for c, prod in held_products:
+            add(c, prod)
         relu_group(2)
         fused(1, 1, part(group_raw[2], 4))
         quantize_slices(3, [0], part(stage_b, 1))
@@ -338,7 +340,7 @@ def tile_picked_gcn_mlp_relu_sub_l_kernel(
         gather_on_scalar(plain, h_tiles[2], lists[2][:])
         gather_on_scalar(picked, h_tiles[2], lists[3][:])
         fused(2, 0, words("prod2_0", V))
-        quantize_slices(3, [2], part(stage_c, 0), "last_codes3")
+        quantize_slices(3, [2], part(stage_c, 0), "last_codes3", "last_scales3")
         relu_group(3)
         fused(2, 1, part(group_raw[3], 4))
         add(2, plain)
@@ -350,6 +352,11 @@ def tile_picked_gcn_mlp_relu_sub_l_kernel(
         sums = [bank(vh, [P, P], "sums") for vh in range(TARGET_HALVES)]
         plain = words("plain3", V)
         gather_on_scalar(plain, h, lists[2][:])
+        both = words("zt", 4 * P, "last_scales3")
+        for vh in range(TARGET_HALVES):
+            zt_words.append(both[:, vh * 2 * P : (vh + 1) * 2 * P])
+            zt.append(zt_words[vh].bitcast(BF16).rearrange("v (u p e) -> v u p e", u=2, e=2))
+            round_sums(scaled_on_scalar, vh, first_sums[vh][:], 0, 2)
         halves = []
         picked_last = words("picked_last", 2 * SLICE_STAGE)
         for vh in range(TARGET_HALVES):
@@ -358,34 +365,36 @@ def tile_picked_gcn_mlp_relu_sub_l_kernel(
             for i in range(2):
                 gather_on_scalar(t[:, i * P : (i + 1) * P], h, lists[4 + i][:, offsets])
             halves.append(t)
-        for i, d in enumerate((0, 2, 1, 3)):
+        for vh in range(TARGET_HALVES):
+            round_sums(scaled_on_scalar, vh, third_sums[vh][:], 2, 1)
+        last_products = []
+        for i, d in enumerate((0, 2, 1)):
             prod = plain
             if d != 2:
                 prod = words(f"prod3_{d}", V)
                 gather_on_vector(prod, h, d)
             for vh in range(TARGET_HALVES):
                 add_transposed(sums[vh][:], prod[:, vh * P : (vh + 1) * P], i == 0, False)
-        both = words("zt", 4 * P, "plain3")
         for vh in range(TARGET_HALVES):
-            zt_words.append(both[:, vh * 2 * P : (vh + 1) * 2 * P])
-            zt.append(zt_words[vh].bitcast(BF16).rearrange("v (u p e) -> v u p e", u=2, e=2))
-        for vh in range(TARGET_HALVES):
-            round_sums(scaled_on_scalar, vh, first_sums[vh][:], 0, 1)
-            round_sums(scaled_on_scalar, vh, early_sums[vh][:], 1, 2)
-        for vh in range(TARGET_HALVES):
+            cols = slice(vh * P, (vh + 1) * P)
+            offsets = slice(vh * LIST_COLUMNS, (vh + 1) * LIST_COLUMNS)
+            prod = words(f"prod3_3_{vh}", P)
+            nc.vector.tensor_tensor(prod, h[:].indirect(lists[3][:, offsets]), gates[3][:, cols], MULT)
+            add_transposed(sums[vh][:], prod, False, False)
             prod = words(f"prod3_45_{vh}", 2 * P)
-            pair = part(spread_all, 3, 2).rearrange("p (i v) -> p i v", i=2)[:, :, vh * P : (vh + 1) * P]
-            nc.vector.tensor_tensor(
-                prod.rearrange("p (i v) -> p i v", i=2), halves[vh].rearrange("p (i v) -> p i v", i=2), pair, MULT
-            )
             for i in range(2):
-                add_transposed(sums[vh][:], prod[:, i * P : (i + 1) * P], False, i == 1)
-            interleave(on_vector, as_grouped(halves[vh]), w2_raw[:, :, vh * P : (vh + 1) * P])
-        w2_codes, w2_scales = operand_tiles("w2", N)
+                one = slice(i * P, (i + 1) * P)
+                nc.vector.tensor_tensor(prod[:, one], halves[vh][:, one], gates[4 + i][:, cols], MULT)
+                add_transposed(sums[vh][:], prod[:, one], False, i == 1)
+            last_products.append(prod)
+        interleave(on_vector, as_grouped(halves[1]), w2_raw[:, :, P:])
+        w2_codes, w2_scales = operand_tiles("w2", N, "prod3_45_1")
         z_codes, z_scales = operand_tiles("z", V)
         for vh, scaled in enumerate((scaled_on_scalar, scaled_on_vector)):
             round_sums(scaled, vh, sums[vh][:], GROUPS - 1, 1)
-        quantize(nc, w2_codes[:], w2_scales[:], as_grouped(picked_last))
+        interleave(on_scalar, as_grouped(last_products[0]), w2_raw[:, :, :P])
+        quantize(nc, w2_codes[:, P:], w2_scales[:, P:], as_grouped(halves[1]))
+        quantize(nc, w2_codes[:, :P], w2_scales[:, :P], as_grouped(last_products[0]))
         for vh, (copy, out_bank) in enumerate(((on_scalar, 6), (on_vector, 4))):
             cols = slice(vh * P, (vh + 1) * P)
             back = bank(2 + vh, [P, 2, P], "back")

@@ -14,7 +14,7 @@ U8 = mybir.dt.uint8
 FP8X4 = mybir.dt.float8_e4m3fn_x4
 RELU = mybir.ActivationFunctionType.Relu
 COPY = mybir.ActivationFunctionType.Copy
-MULT, ADD, MAX = mybir.AluOpType.mult, mybir.AluOpType.add, mybir.AluOpType.max
+MULT, MAX = mybir.AluOpType.mult, mybir.AluOpType.max
 
 P = 128
 J = 4
@@ -26,9 +26,11 @@ HALF = T // 2
 NODE_HALVES = (slice(0, HALF), slice(HALF, T))
 LIST_COLUMNS = P // 16
 GROUP_PARTITIONS = P // J
-SLICE_STAGE = KP // 2
+PART = KP // 2
 PLAIN_LIST = 2
-GATED = (0, 1, 3, 4, 5)
+GATED = tuple(d for d in range(D) if d != PLAIN_LIST)
+LEAST_SHARE = 2.0**-24
+LEAST_TOP = 2.0**-102
 
 
 def interleave(copy, grouped, raw):
@@ -47,7 +49,11 @@ def as_grouped(area):
 
 
 def part(area, i, n=1):
-    return area[:, i * SLICE_STAGE : (i + n) * SLICE_STAGE]
+    return area[:, i * PART : (i + n) * PART]
+
+
+def block(i):
+    return slice(i * P, (i + 1) * P)
 
 
 def tile_picked_gcn_mlp_relu_sub_l_kernel(
@@ -72,7 +78,7 @@ def tile_picked_gcn_mlp_relu_sub_l_kernel(
             scales = keep.tile([P, width], U8, align_bytes=64, name=f"{name}_scales", tag=scales_tag or f"{name}_scales")
             return codes, scales
 
-        x_raw, w1_raw, group_raw, lists = {}, {}, {}, []
+        x_raw, w1_raw, lists = {}, {}, []
 
         def load_x(g):
             t = keep.tile([P, J, T], F32, align_bytes=64, name=f"x_raw{g}")
@@ -80,10 +86,8 @@ def tile_picked_gcn_mlp_relu_sub_l_kernel(
             x_raw[g] = t
 
         def load_w1(c, g):
-            if c not in group_raw:
-                group_raw[c] = words(f"w1_raw{c}", PASSES * KP)
-            w1_raw[c, g] = group_raw[c][:, g * KP : (g + 1) * KP]
-            rows = w1[g * KP : (g + 1) * KP, c * P : (c + 1) * P]
+            w1_raw[c, g] = words(f"w1_raw{c}_{g}", KP)
+            rows = w1[g * KP : (g + 1) * KP, block(c)]
             nc.sync.dma_start(
                 out=w1_raw[c, g].rearrange("p (j c) -> p j c", j=J), in_=rows.rearrange("(p j) c -> p j c", j=J)
             )
@@ -94,7 +98,7 @@ def tile_picked_gcn_mlp_relu_sub_l_kernel(
             lists.append(t)
 
         gate_raw = keep.tile([D, V], F32)
-        gate_rows = keep.tile([P, V], F32, align_bytes=64, tag="after_gate_rows")
+        gate_rows = keep.tile([P, V], F32, align_bytes=64)
         for rows in (slice(0, 4), slice(4, D)):
             nc.sync.dma_start(out=gate_raw[rows, :], in_=gate[rows, 0, :])
         load_x(0)
@@ -114,118 +118,215 @@ def tile_picked_gcn_mlp_relu_sub_l_kernel(
         ident = keep.tile([P, P], F32)
         make_identity(nc, ident[:])
         for vh in range(TARGET_HALVES):
-            on_scalar(out=gate_rows[:, vh * P : (vh + 1) * P], in_=ident[:])
+            on_scalar(out=gate_rows[:, block(vh)], in_=ident[:])
 
         x_operands = [operand_tiles(f"x{g}", T) for g in range(PASSES)]
 
-        def stage_w1(copy, area, c, g):
+        def stage_slice(copy, area, c, g):
             interleave(copy, as_grouped(area), w1_raw[c, g].rearrange("p (j c) -> p j c", j=J))
 
-        def quantize_w1(c, passes, area, codes_tag=None, scales_tag=None):
-            codes, scales = operand_tiles(f"w1_{c}_{passes[0]}", len(passes) * P, codes_tag, scales_tag)
-            for i, g in enumerate(passes):
-                stage_w1(on_scalar, part(area, i), c, g)
+        def project_slice(c, g, area, accs, node_parts, scales_tag=None):
+            codes, scales = operand_tiles(f"w1_{c}_{g}", P, None, scales_tag)
             quantize(nc, codes[:], scales[:], as_grouped(area))
-            return {g: (codes[:, i * P : (i + 1) * P], scales[:, i * P : (i + 1) * P]) for i, g in enumerate(passes)}
-
-        def project_pass(acc, g, weights, cols, start, stop):
             x_codes, x_scales = x_operands[g]
-            codes, scales = weights
-            nc.tensor.matmul_mx(
-                out=acc,
-                lhsT=codes.bitcast(FP8X4),
-                lhsT_scale=scales,
-                rhs=x_codes[:, cols].bitcast(FP8X4),
-                rhs_scale=x_scales[:, cols],
-                start=start,
-                stop=stop,
-            )
+            for acc, nodes in zip(accs, node_parts):
+                nc.tensor.matmul_mx(
+                    out=acc[:],
+                    lhsT=codes[:].bitcast(FP8X4),
+                    lhsT_scale=scales[:],
+                    rhs=x_codes[:, nodes].bitcast(FP8X4),
+                    rhs_scale=x_scales[:, nodes],
+                    start=(g == 0),
+                    stop=(g == PASSES - 1),
+                )
 
         def relu_on_scalar(out, in_):
             nc.scalar.activation(out=out, in_=in_, func=RELU)
 
-        def spread_gates():
+        def spread_ratios():
             on_vector(out=gate_rows[:D, :], in_=gate_raw[:])
             turned = bank(7, [P, TARGET_HALVES, P], "turned")
             for vh in range(TARGET_HALVES):
-                nc.tensor.transpose(turned[:, vh, :], gate_rows[:, vh * P : (vh + 1) * P], ident[:])
+                nc.tensor.transpose(turned[:, vh, :], gate_rows[:, block(vh)], ident[:])
             columns = keep.tile([P, TARGET_HALVES, D + 1], F32, align_bytes=64, name="gate_columns")
-            nc.gpsimd.memset(columns[:, :, D:], 2.0**-102)
+            nc.gpsimd.memset(columns[:, :, D:], LEAST_TOP)
             on_vector(out=columns[:, :, :D], in_=turned[:, :, :D])
             own = columns[:, :, PLAIN_LIST]
-            small = keep.tile([P, 4, TARGET_HALVES], F32, name="gate_guard")
-            top, size, half_sign, guarded = (small[:, i, :] for i in range(4))
+            steps = keep.tile([P, 4, TARGET_HALVES], F32, name="factor_steps")
+            top, size, half_sign, guarded = (steps[:, i, :] for i in range(4))
             nc.vector.tensor_reduce(top, columns[:], mybir.AxisListType.X, MAX, apply_absolute_value=True)
             nc.vector.scalar_tensor_tensor(size, own, -1.0, own, MULT, MAX)
             nc.vector.tensor_scalar(half_sign, own, 0.0, 0.5, mybir.AluOpType.is_ge, mybir.AluOpType.subtract)
-            nc.vector.scalar_tensor_tensor(guarded, top, 2.0**-24, size, MULT, MAX)
+            nc.vector.scalar_tensor_tensor(guarded, top, LEAST_SHARE, size, MULT, MAX)
             along_lists = [P, TARGET_HALVES, D]
-            signed = keep.tile(along_lists, F32, align_bytes=64, name="signed", tag="after_ratios")
+            signed = keep.tile(along_lists, F32, align_bytes=64, name="signed", tag="after_division")
             nc.vector.tensor_tensor(signed[:], columns[:, :, :D], half_sign.unsqueeze(2).to_broadcast(along_lists), MULT)
             inverse = keep.tile([P, TARGET_HALVES], F32, name="inverse")
             nc.vector.reciprocal(inverse[:], guarded)
             factor = keep.tile([P, TARGET_HALVES], F32, name="factor")
             nc.vector.scalar_tensor_tensor(factor[:], half_sign, 2.0, guarded, MULT, MULT)
-            ratios = keep.tile(along_lists, F32, align_bytes=64, name="ratios", tag="after_columns")
+            divided = keep.tile(along_lists, F32, align_bytes=64, name="divided", tag="after_spreading")
             nc.vector.scalar_tensor_tensor(
-                ratios[:], signed[:], 2.0, inverse[:].unsqueeze(2).to_broadcast(along_lists), MULT, MULT
+                divided[:], signed[:], 2.0, inverse[:].unsqueeze(2).to_broadcast(along_lists), MULT, MULT
             )
-            spread_all = words("gates", len(GATED) * V)
+            spread = words("ratios", len(GATED) * V)
             for first, b in ((0, 2), (2, 0), (4, 1)):
-                ds = GATED[first : first + 2]
-                spread = bank(b, [P, len(ds) * V], "spread")
-                for i, d in enumerate(ds):
+                in_bank = GATED[first : first + 2]
+                acc = bank(b, [P, len(in_bank) * V], "spread")
+                for i, d in enumerate(in_bank):
                     for vh in range(TARGET_HALVES):
-                        column = ratios[:, vh, d : d + 1].to_broadcast([P, P])
-                        nc.tensor.transpose(spread[:, i * V + vh * P : i * V + (vh + 1) * P], column, ident[:])
-                on_vector(out=part(spread_all, first, len(ds)), in_=spread[:])
-            return spread_all, factor
+                        column = divided[:, vh, d : d + 1].to_broadcast([P, P])
+                        nc.tensor.transpose(acc[:, block(i * TARGET_HALVES + vh)], column, ident[:])
+                on_vector(out=part(spread, first, len(in_bank)), in_=acc[:])
+            return {d: part(spread, i) for i, d in enumerate(GATED)}, factor
 
         def project_first_group():
             width = 2 * HALF
-            first = words("x_stage_first", 2 * width, "after_ratios")
-            second = words("x_stage_second", width, "after_columns")
+            first = words("x_stage_first", 2 * width, "after_division")
+            second = words("x_stage_second", width, "after_spreading")
             third = x_raw[1][:].rearrange("p j t -> p (j t)")[:, HALF : HALF + width]
             areas = ((first[:, :width], first[:, width:]), (first[:, :width], second), (second, third))
             h = keep.tile([P, T], F32, name="h0")
-            banks = [bank(i, [P, HALF], "h_acc") for i in range(2)]
+            node_parts = (NODE_HALVES[0], slice(HALF, HALF + P), slice(HALF + P, T))
+            accs = [bank(b, [P, nodes.stop - nodes.start], "h_acc") for b, nodes in zip((0, 1, 4), node_parts)]
 
             def stage_x(g):
-                for area, cols, copy in zip(areas[g], NODE_HALVES, (on_vector, on_scalar)):
-                    interleave(copy, as_grouped(area), x_raw[g][:, :, cols])
+                for area, nodes, copy in zip(areas[g], NODE_HALVES, (on_vector, on_scalar)):
+                    interleave(copy, as_grouped(area), x_raw[g][:, :, nodes])
 
             def quantize_x(g, half):
                 codes, scales = x_operands[g]
-                cols = NODE_HALVES[half]
-                quantize(nc, codes[:, cols], scales[:, cols], as_grouped(areas[g][half]))
-
-            def project(g, weights):
-                for acc, cols in zip(banks, NODE_HALVES):
-                    project_pass(acc[:], g, weights, cols, g == 0, g == PASSES - 1)
+                nodes = NODE_HALVES[half]
+                quantize(nc, codes[:, nodes], scales[:, nodes], as_grouped(areas[g][half]))
 
             for g in range(PASSES - 1):
                 stage_x(g)
                 quantize_x(g, 0)
                 quantize_x(g, 1)
                 if g == 0:
-                    project(0, quantize_w1(0, [0], x_raw[0][:, 0, NODE_HALVES[1]])[0])
+                    area = x_raw[0][:, 0, NODE_HALVES[1]]
+                    stage_slice(on_scalar, area, 0, 0)
+                    project_slice(0, 0, area, accs, node_parts)
             stage_x(2)
             area = x_raw[2][:, 0, NODE_HALVES[0]]
-            stage_w1(on_vector, area, 0, 1)
+            stage_slice(on_vector, area, 0, 1)
             quantize_x(2, 0)
-            codes, scales = operand_tiles("w1_0_1", P)
-            quantize(nc, codes[:], scales[:], as_grouped(area))
-            project(1, (codes[:], scales[:]))
+            project_slice(0, 1, area, accs, node_parts)
             quantize_x(2, 1)
-            project(2, quantize_w1(0, [2], x_raw[2][:, 0, NODE_HALVES[1]], "last_codes0", "last_scales0")[2])
-            for acc, cols, relu in zip(banks, NODE_HALVES, (nc.vector.tensor_relu, relu_on_scalar)):
-                relu(out=h[:, cols], in_=acc[:])
+            area = x_raw[2][:, 0, NODE_HALVES[1]]
+            stage_slice(on_scalar, area, 0, 2)
+            project_slice(0, 2, area, accs, node_parts)
+            for acc, nodes, relu in zip(accs, node_parts, (nc.vector.tensor_relu, relu_on_scalar, nc.vector.tensor_relu)):
+                relu(out=h[:, nodes], in_=acc[:])
             return h
 
-        def add_transposed(acc, prod, first, last):
-            nc.tensor.matmul(acc, prod, ident[:], start=first, stop=last, is_transpose=True)
+        ratios, factor = spread_ratios()
+        h = {0: project_first_group()}
+        h_accs, staged = {}, {}
 
-        zt_words, zt = [], []
+        def stage(c, g, area):
+            staged[c, g] = area
+            stage_slice(on_scalar, area, c, g)
+
+        def project(c, g, scales_tag=None):
+            if g == 0:
+                h_accs[c] = [bank({1: 2, 2: 0, 3: 6}[c] + i, [P, HALF], "h_acc") for i in range(2)]
+            project_slice(c, g, staged[c, g], h_accs[c], NODE_HALVES, scales_tag)
+
+        def finish_h(c):
+            h[c] = keep.tile([P, T], F32, name=f"h{c}")
+            for acc, nodes in zip(h_accs[c], NODE_HALVES):
+                relu_on_scalar(h[c][:, nodes], acc[:])
+
+        sums, added, waiting = {}, {}, []
+
+        def add_half(c, vh, term):
+            k = added.get((c, vh), 0)
+            nc.tensor.matmul(sums[c][vh], term, ident[:], start=(k == 0), stop=(k == D - 1), is_transpose=True)
+            added[c, vh] = k + 1
+
+        def add(c, term):
+            if c not in sums:
+                waiting.append((c, term))
+                return
+            for vh in range(TARGET_HALVES):
+                add_half(c, vh, term[:, block(vh)])
+
+        def offsets(d, vh=None):
+            return lists[d][:] if vh is None else lists[d][:, vh * LIST_COLUMNS : (vh + 1) * LIST_COLUMNS]
+
+        def pick(picked, c, d, vh=None):
+            nc.scalar.activation(picked, h[c][:].indirect(offsets(d, vh)), COPY)
+            return picked
+
+        def fused(term, c, d):
+            nc.vector.tensor_tensor(term, h[c][:].indirect(offsets(d)), ratios[d], MULT)
+            add(c, term)
+
+        def multiply(picked, c, d):
+            term = words(f"term{c}_{d}", V)
+            nc.vector.tensor_tensor(term, picked, ratios[d], MULT)
+            add(c, term)
+
+        def after_staging(c, g, i):
+            return part(w1_raw[c, g], i)
+
+        stage(1, 0, x_raw[2][:, 1, NODE_HALVES[1]])
+        project(1, 0, "w1_0_2_scales")
+        round_a = words("round_a", 4 * PART, "w1_0_2_codes")
+        stage(1, 1, part(round_a, 0))
+        stage(1, 2, part(round_a, 1))
+        stage(2, 0, part(round_a, 2))
+        plain = pick(words("plain0", V), 0, PLAIN_LIST)
+        stage(2, 1, part(round_a, 3))
+        fused(words("term0_0", V), 0, 0)
+        project(1, 1)
+        fused(after_staging(1, 1, 0), 0, 1)
+        project(1, 2)
+        finish_h(1)
+        add(0, plain)
+        fused(after_staging(1, 2, 0), 0, 3)
+        project(2, 0)
+        fused(after_staging(2, 0, 0), 0, 4)
+        fused(after_staging(2, 0, 1), 0, 5)
+        project(2, 1)
+
+        round_b = words("round_b", 3 * PART, "w1_1_2_codes")
+        stage(2, 2, part(round_b, 0))
+        stage(3, 0, part(round_b, 1))
+        plain = pick(after_staging(2, 1, 1), 1, PLAIN_LIST)
+        picked = pick(after_staging(3, 0, 1), 1, 3)
+        stage(3, 1, part(round_b, 2))
+        fused(after_staging(2, 1, 0), 1, 0)
+        project(2, 2)
+        first_sums = [bank(2 + vh, [P, 2 * P], "first_sums") for vh in range(TARGET_HALVES)]
+        third_sums = [bank(4 + vh, [P, P], "third_sums") for vh in range(TARGET_HALVES)]
+        sums[0] = [t[:, :P] for t in first_sums]
+        sums[1] = [t[:, P:] for t in first_sums]
+        sums[2] = [t[:] for t in third_sums]
+        for c, term in waiting:
+            add(c, term)
+        finish_h(2)
+        fused(after_staging(2, 2, 0), 1, 1)
+        fused(after_staging(2, 2, 1), 1, 4)
+        project(3, 0)
+        add(1, plain)
+        fused(after_staging(3, 0, 0), 1, 5)
+        multiply(picked, 1, 3)
+        project(3, 1)
+
+        round_c = words("round_c", 3 * PART, "w1_2_2_codes")
+        stage(3, 2, part(round_c, 0))
+        plain = pick(part(round_c, 1), 2, PLAIN_LIST)
+        picked = pick(part(round_c, 2), 2, 3)
+        fused(after_staging(3, 1, 0), 2, 0)
+        project(3, 2)
+        finish_h(3)
+        fused(after_staging(3, 2, 0), 2, 1)
+        add(2, plain)
+        fused(after_staging(3, 2, 1), 2, 4)
+        multiply(picked, 2, 3)
+        fused(staged[3, 2], 2, 5)
 
         def scaled_on_scalar(out, in_, vh):
             nc.scalar.activation(out, in_, COPY, scale=factor[:, vh : vh + 1])
@@ -233,188 +334,68 @@ def tile_picked_gcn_mlp_relu_sub_l_kernel(
         def scaled_on_vector(out, in_, vh):
             nc.vector.tensor_scalar(out, in_, factor[:, vh : vh + 1], None, MULT)
 
-        def round_sums(copy, vh, acc, first_group, groups):
+        def round_sums(scaled, vh, acc, first_group, groups):
+            zt = zt_words[vh].bitcast(BF16).rearrange("v (u p e) -> v u p e", u=2, e=2)
             partitions = slice(GROUP_PARTITIONS * first_group, GROUP_PARTITIONS * (first_group + groups))
-            copy(zt[vh][:, :, partitions, :], acc.rearrange("v (p u e) -> v u p e", u=2, e=2), vh)
+            scaled(zt[:, :, partitions, :], acc.rearrange("v (p u e) -> v u p e", u=2, e=2), vh)
 
-        def gather_on_vector(prod, h, d):
-            nc.vector.tensor_tensor(prod, h[:].indirect(lists[d][:]), gates[d], MULT)
-
-        def gather_on_scalar(picked, h, offsets):
-            nc.scalar.activation(picked, h[:].indirect(offsets), COPY)
-
-        spread_all, factor = spread_gates()
-        gates = {d: part(spread_all, i) for i, d in enumerate(GATED)}
-        h = project_first_group()
-
-        sum_tiles, held_products = {}, []
-        h_tiles, h_banks, weights = {0: h}, {}, {}
-
-        def quantize_slices(n, passes, area, codes_tag=None, scales_tag=None):
-            codes, scales = operand_tiles(f"w1_{n}_{passes[0]}", len(passes) * P, codes_tag, scales_tag)
-            quantize(nc, codes[:], scales[:], as_grouped(area))
-            if n not in h_banks:
-                h_banks[n] = [bank((2, 0, 6)[n - 1] + i, [P, HALF], "h_acc") for i in range(2)]
-            for i, g in enumerate(passes):
-                cols = slice(i * P, (i + 1) * P)
-                for acc, nodes in zip(h_banks[n], NODE_HALVES):
-                    project_pass(acc[:], g, (codes[:, cols], scales[:, cols]), nodes, g == 0, g == PASSES - 1)
-
-        def relu_group(n):
-            h_tiles[n] = keep.tile([P, T], F32, name=f"h{n}")
-            for acc, nodes in zip(h_banks[n], NODE_HALVES):
-                relu_on_scalar(h_tiles[n][:, nodes], acc[:])
-
-        counts = {}
-
-        def add(c, prod):
-            if c not in sum_tiles:
-                held_products.append((c, prod))
-                return
-            for i in range(prod.shape[1] // V):
-                k = counts.get(c, 0)
-                for vh in range(TARGET_HALVES):
-                    acc = sum_tiles[c][vh]
-                    add_transposed(acc, part(prod, i)[:, vh * P : (vh + 1) * P], k == 0, k == D - 1)
-                counts[c] = k + 1
-
-        def fused(c, d, prod):
-            gather_on_vector(prod, h_tiles[c], d)
-            add(c, prod)
-
-        def multiply(c, name, picked, factor):
-            prod = words(name, picked.shape[1])
-            nc.vector.tensor_tensor(prod, picked, factor, MULT)
-            add(c, prod)
-
-        area = x_raw[2][:, 1, NODE_HALVES[1]]
-        stage_w1(on_scalar, area, 1, 0)
-        quantize_slices(1, [0], area, None, "last_scales0")
-        stage_a = words("stage_a", 4 * SLICE_STAGE, "last_codes0")
-        stage_w1(on_scalar, part(stage_a, 0), 1, 1)
-        stage_w1(on_scalar, part(stage_a, 1), 1, 2)
-        stage_w1(on_scalar, part(stage_a, 2), 2, 0)
-        plain = words("plain0", V)
-        gather_on_scalar(plain, h, lists[2][:])
-        stage_w1(on_scalar, part(stage_a, 3), 2, 1)
-        fused(0, 0, words("prod0_0", V))
-        quantize_slices(1, [1], part(stage_a, 0))
-        fused(0, 1, part(group_raw[1], 2))
-        quantize_slices(1, [2], part(stage_a, 1), "last_codes1")
-        relu_group(1)
-        add(0, plain)
-        fused(0, 3, part(group_raw[1], 4))
-        quantize_slices(2, [0], part(stage_a, 2))
-        fused(0, 4, part(group_raw[2], 0))
-        fused(0, 5, part(group_raw[2], 1))
-        quantize_slices(2, [1], part(stage_a, 3))
-
-        stage_b = words("stage_b", 3 * SLICE_STAGE, "last_codes1")
-        stage_w1(on_scalar, part(stage_b, 0), 2, 2)
-        stage_w1(on_scalar, part(stage_b, 1), 3, 0)
-        stage_w1(on_scalar, part(stage_b, 2), 3, 1)
-        plain, picked = part(group_raw[2], 3), part(group_raw[3], 1)
-        gather_on_scalar(plain, h_tiles[1], lists[2][:])
-        gather_on_scalar(picked, h_tiles[1], lists[3][:])
-        fused(1, 0, part(group_raw[2], 2))
-        quantize_slices(2, [2], part(stage_b, 0), "last_codes2")
-        first_sums = [bank(2 + vh, [P, 2 * P], "first_sums") for vh in range(TARGET_HALVES)]
-        third_sums = [bank(4 + vh, [P, P], "third_sums") for vh in range(TARGET_HALVES)]
-        sum_tiles[0] = [t[:, :P] for t in first_sums]
-        sum_tiles[1] = [t[:, P:] for t in first_sums]
-        sum_tiles[2] = [t[:] for t in third_sums]
-        for c, prod in held_products:
-            add(c, prod)
-        relu_group(2)
-        fused(1, 1, part(group_raw[2], 4))
-        quantize_slices(3, [0], part(stage_b, 1))
-        fused(1, 4, part(group_raw[3], 0))
-        quantize_slices(3, [1], part(stage_b, 2))
-        fused(1, 5, part(group_raw[3], 2))
-        add(1, plain)
-        multiply(1, "prod1_3", picked, gates[3])
-
-        stage_c = words("stage_c", 3 * SLICE_STAGE, "last_codes2")
-        stage_w1(on_scalar, part(stage_c, 0), 3, 2)
-        plain, picked = part(stage_c, 1), part(stage_c, 2)
-        gather_on_scalar(plain, h_tiles[2], lists[2][:])
-        gather_on_scalar(picked, h_tiles[2], lists[3][:])
-        fused(2, 0, words("prod2_0", V))
-        quantize_slices(3, [2], part(stage_c, 0), "last_codes3", "last_scales3")
-        relu_group(3)
-        fused(2, 1, part(group_raw[3], 4))
-        add(2, plain)
-        fused(2, 4, part(group_raw[3], 5))
-        multiply(2, "prod2_3", picked, gates[3])
-        fused(2, 5, part(stage_c, 0))
-        h = h_tiles[3]
-
-        sums = [bank(vh, [P, P], "sums") for vh in range(TARGET_HALVES)]
-        plain = words("plain3", V)
-        gather_on_scalar(plain, h, lists[2][:])
-        both = words("zt", 4 * P, "last_scales3")
+        last = GROUPS - 1
+        last_sums = [bank(vh, [P, P], "last_sums") for vh in range(TARGET_HALVES)]
+        sums[last] = [t[:] for t in last_sums]
+        plain = pick(words("plain3", V), last, PLAIN_LIST)
+        zt_both = words("zt", TARGET_HALVES * PART, "w1_3_1_scales")
+        zt_words = [part(zt_both, vh) for vh in range(TARGET_HALVES)]
         for vh in range(TARGET_HALVES):
-            zt_words.append(both[:, vh * 2 * P : (vh + 1) * 2 * P])
-            zt.append(zt_words[vh].bitcast(BF16).rearrange("v (u p e) -> v u p e", u=2, e=2))
             round_sums(scaled_on_scalar, vh, first_sums[vh][:], 0, 2)
-        halves = []
-        picked_last = words("picked_last", 2 * SLICE_STAGE)
+        picked_last = words("picked_last", TARGET_HALVES * PART)
         for vh in range(TARGET_HALVES):
-            offsets = slice(vh * LIST_COLUMNS, (vh + 1) * LIST_COLUMNS)
-            t = part(picked_last, vh)
-            for i in range(2):
-                gather_on_scalar(t[:, i * P : (i + 1) * P], h, lists[4 + i][:, offsets])
-            halves.append(t)
+            for i, d in enumerate((4, 5)):
+                pick(part(picked_last, vh)[:, block(i)], last, d, vh)
         for vh in range(TARGET_HALVES):
             round_sums(scaled_on_scalar, vh, third_sums[vh][:], 2, 1)
-        last_products = []
-        for i, d in enumerate((0, 2, 1)):
-            prod = plain
-            if d != 2:
-                prod = words(f"prod3_{d}", V)
-                gather_on_vector(prod, h, d)
-            for vh in range(TARGET_HALVES):
-                add_transposed(sums[vh][:], prod[:, vh * P : (vh + 1) * P], i == 0, False)
+        fused(words("term3_0", V), last, 0)
+        add(last, plain)
+        fused(words("term3_1", V), last, 1)
+        last_terms = []
         for vh in range(TARGET_HALVES):
-            cols = slice(vh * P, (vh + 1) * P)
-            offsets = slice(vh * LIST_COLUMNS, (vh + 1) * LIST_COLUMNS)
-            prod = words(f"prod3_3_{vh}", P)
-            nc.vector.tensor_tensor(prod, h[:].indirect(lists[3][:, offsets]), gates[3][:, cols], MULT)
-            add_transposed(sums[vh][:], prod, False, False)
-            prod = words(f"prod3_45_{vh}", 2 * P)
-            for i in range(2):
-                one = slice(i * P, (i + 1) * P)
-                nc.vector.tensor_tensor(prod[:, one], halves[vh][:, one], gates[4 + i][:, cols], MULT)
-                add_transposed(sums[vh][:], prod[:, one], False, i == 1)
-            last_products.append(prod)
-        interleave(on_vector, as_grouped(halves[1]), w2_raw[:, :, P:])
-        w2_codes, w2_scales = operand_tiles("w2", N, "prod3_45_1")
+            term = words(f"term3_3_{vh}", P)
+            nc.vector.tensor_tensor(term, h[last][:].indirect(offsets(3, vh)), ratios[3][:, block(vh)], MULT)
+            add_half(last, vh, term)
+            last_terms.append(words(f"term3_45_{vh}", PART))
+            for i, d in enumerate((4, 5)):
+                term = last_terms[vh][:, block(i)]
+                nc.vector.tensor_tensor(term, part(picked_last, vh)[:, block(i)], ratios[d][:, block(vh)], MULT)
+                add_half(last, vh, term)
+
+        w2_areas = (last_terms[0], part(picked_last, 1))
+        interleave(on_vector, as_grouped(w2_areas[1]), w2_raw[:, :, block(1)])
+        w2_codes, w2_scales = operand_tiles("w2", N, "term3_45_1")
         z_codes, z_scales = operand_tiles("z", V)
         for vh, scaled in enumerate((scaled_on_scalar, scaled_on_vector)):
-            round_sums(scaled, vh, sums[vh][:], GROUPS - 1, 1)
-        interleave(on_scalar, as_grouped(last_products[0]), w2_raw[:, :, :P])
-        quantize(nc, w2_codes[:, P:], w2_scales[:, P:], as_grouped(halves[1]))
-        quantize(nc, w2_codes[:, :P], w2_scales[:, :P], as_grouped(last_products[0]))
+            round_sums(scaled, vh, sums[last][vh], last, 1)
+        interleave(on_scalar, as_grouped(w2_areas[0]), w2_raw[:, :, block(0)])
+        for mb in (1, 0):
+            quantize(nc, w2_codes[:, block(mb)], w2_scales[:, block(mb)], as_grouped(w2_areas[mb]))
+
         for vh, (copy, out_bank) in enumerate(((on_scalar, 6), (on_vector, 4))):
-            cols = slice(vh * P, (vh + 1) * P)
             back = bank(2 + vh, [P, 2, P], "back")
             for u in range(2):
-                nc.tensor.transpose(back[:, u, :], zt_words[vh][:, u * P : (u + 1) * P], ident[:])
+                nc.tensor.transpose(back[:, u, :], zt_words[vh][:, block(u)], ident[:])
             z_words = keep.tile([P, P, 2], F32, align_bytes=64, name=f"z_words{vh}")
             on_scalar(out=z_words[:], in_=back[:].rearrange("p u v -> p v u"))
-            quantize(nc, z_codes[:, cols], z_scales[:, cols], as_grouped(z_words[:].rearrange("p v u -> p (v u)")))
+            targets = block(vh)
+            quantize(nc, z_codes[:, targets], z_scales[:, targets], as_grouped(z_words[:].rearrange("p v u -> p (v u)")))
             for mb in range(N // P):
-                rows = slice(mb * P, (mb + 1) * P)
                 acc = bank(out_bank + mb, [P, P], "out_acc")
                 nc.tensor.matmul_mx(
                     out=acc[:],
-                    lhsT=w2_codes[:, rows].bitcast(FP8X4),
-                    lhsT_scale=w2_scales[:, rows],
-                    rhs=z_codes[:, cols].bitcast(FP8X4),
-                    rhs_scale=z_scales[:, cols],
+                    lhsT=w2_codes[:, block(mb)].bitcast(FP8X4),
+                    lhsT_scale=w2_scales[:, block(mb)],
+                    rhs=z_codes[:, targets].bitcast(FP8X4),
+                    rhs_scale=z_scales[:, targets],
                     start=True,
                     stop=True,
                 )
                 res = keep.tile([P, P], F32, name=f"res{vh}_{mb}")
                 (on_scalar, copy)[mb](out=res[:], in_=acc[:])
-                nc.sync.dma_start(out=out[rows, cols], in_=res[:])
+                nc.sync.dma_start(out=out[block(mb), targets], in_=res[:])

@@ -125,11 +125,11 @@ def tile_picked_gcn_mlp_relu_sub_l_kernel(
         def stage_slice(copy, area, c, g):
             interleave(copy, as_grouped(area), w1_raw[c, g].rearrange("p (j c) -> p j c", j=J))
 
-        def project_slice(c, g, area, accs, node_parts, scales_tag=None):
+        def project_slice(c, g, area, accs, scales_tag=None):
             codes, scales = operand_tiles(f"w1_{c}_{g}", P, None, scales_tag)
             quantize(nc, codes[:], scales[:], as_grouped(area))
             x_codes, x_scales = x_operands[g]
-            for acc, nodes in zip(accs, node_parts):
+            for acc, nodes in zip(accs, NODE_HALVES):
                 nc.tensor.matmul_mx(
                     out=acc[:],
                     lhsT=codes[:].bitcast(FP8X4),
@@ -187,8 +187,7 @@ def tile_picked_gcn_mlp_relu_sub_l_kernel(
             third = x_raw[1][:].rearrange("p j t -> p (j t)")[:, HALF : HALF + width]
             areas = ((first[:, :width], first[:, width:]), (first[:, :width], second), (second, third))
             h = keep.tile([P, T], F32, name="h0")
-            node_parts = (NODE_HALVES[0], slice(HALF, HALF + P), slice(HALF + P, T))
-            accs = [bank(b, [P, nodes.stop - nodes.start], "h_acc") for b, nodes in zip((0, 1, 4), node_parts)]
+            accs = [bank(b, [P, HALF], "h_acc") for b in range(2)]
 
             def stage_x(g):
                 for area, nodes, copy in zip(areas[g], NODE_HALVES, (on_vector, on_scalar)):
@@ -206,17 +205,17 @@ def tile_picked_gcn_mlp_relu_sub_l_kernel(
                 if g == 0:
                     area = x_raw[0][:, 0, NODE_HALVES[1]]
                     stage_slice(on_scalar, area, 0, 0)
-                    project_slice(0, 0, area, accs, node_parts)
+                    project_slice(0, 0, area, accs)
             stage_x(2)
             area = x_raw[2][:, 0, NODE_HALVES[0]]
             stage_slice(on_vector, area, 0, 1)
             quantize_x(2, 0)
-            project_slice(0, 1, area, accs, node_parts)
+            project_slice(0, 1, area, accs)
             quantize_x(2, 1)
             area = x_raw[2][:, 0, NODE_HALVES[1]]
             stage_slice(on_scalar, area, 0, 2)
-            project_slice(0, 2, area, accs, node_parts)
-            for acc, nodes, relu in zip(accs, node_parts, (nc.vector.tensor_relu, relu_on_scalar, nc.vector.tensor_relu)):
+            project_slice(0, 2, area, accs)
+            for acc, nodes, relu in zip(accs, NODE_HALVES, (nc.vector.tensor_relu, relu_on_scalar)):
                 relu(out=h[:, nodes], in_=acc[:])
             return h
 
@@ -231,7 +230,7 @@ def tile_picked_gcn_mlp_relu_sub_l_kernel(
         def project(c, g, scales_tag=None):
             if g == 0:
                 h_accs[c] = [bank({1: 2, 2: 0, 3: 6}[c] + i, [P, HALF], "h_acc") for i in range(2)]
-            project_slice(c, g, staged[c, g], h_accs[c], NODE_HALVES, scales_tag)
+            project_slice(c, g, staged[c, g], h_accs[c], scales_tag)
 
         def finish_h(c):
             h[c] = keep.tile([P, T], F32, name=f"h{c}")

@@ -397,4 +397,5 @@ def tile_picked_gcn_mlp_relu_sub_l_kernel(
                 )
                 res = keep.tile([P, P], F32, name=f"res{vh}_{mb}")
                 (on_scalar, copy)[mb](out=res[:], in_=acc[:])
-                nc.sync.dma_start(out=out[block(mb), targets], in_=res[:])
+                queue = nc.scalar if (vh, mb) == (TARGET_HALVES - 1, 0) else nc.sync
+                queue.dma_start(out=out[block(mb), targets], in_=res[:])

@@ -27,6 +27,7 @@ NODE_HALVES = (slice(0, HALF), slice(HALF, T))
 LIST_COLUMNS = P // 16
 GROUP_PARTITIONS = P // J
 PART = KP // 2
+SPLIT = 320
 PLAIN_LIST = 2
 GATED = tuple(d for d in range(D) if d != PLAIN_LIST)
 LEAST_SHARE = 2.0**-24
@@ -85,10 +86,10 @@ def tile_picked_gcn_mlp_relu_sub_l_kernel(
             nc.sync.dma_start(out=t[:], in_=xT[g * KP : (g + 1) * KP, :].rearrange("(p j) t -> p j t", j=J))
             x_raw[g] = t
 
-        def load_w1(c, g):
+        def load_w1(c, g, queue=nc.sync):
             w1_raw[c, g] = words(f"w1_raw{c}_{g}", KP)
             rows = w1[g * KP : (g + 1) * KP, block(c)]
-            nc.sync.dma_start(
+            queue.dma_start(
                 out=w1_raw[c, g].rearrange("p (j c) -> p j c", j=J), in_=rows.rearrange("(p j) c -> p j c", j=J)
             )
 
@@ -102,10 +103,10 @@ def tile_picked_gcn_mlp_relu_sub_l_kernel(
         for rows in (slice(0, 4), slice(4, D)):
             nc.sync.dma_start(out=gate_raw[rows, :], in_=gate[rows, 0, :])
         load_x(0)
-        load_w1(0, 0)
+        load_w1(0, 0, nc.scalar)
+        load_w1(0, 1, nc.scalar)
         load_x(1)
         load_x(2)
-        load_w1(0, 1)
         load_w1(0, 2)
         for d in range(D):
             load_list(d)
@@ -183,15 +184,10 @@ def tile_picked_gcn_mlp_relu_sub_l_kernel(
         def project_first_group():
             width = 2 * HALF
             first = words("x_stage_first", 2 * width, "after_division")
-            second = words("x_stage_second", width, "after_spreading")
-            third = x_raw[1][:].rearrange("p j t -> p (j t)")[:, HALF : HALF + width]
-            areas = ((first[:, :width], first[:, width:]), (first[:, :width], second), (second, third))
+            behind = [x_raw[g][:].rearrange("p j t -> p (j t)")[:, HALF : HALF + width] for g in range(PASSES - 1)]
+            areas = ((first[:, :width], first[:, width:]), (behind[0], w1_raw[0, 0]), (behind[1], w1_raw[0, 1]))
             h = keep.tile([P, T], F32, name="h0")
             accs = [bank(b, [P, HALF], "h_acc") for b in range(2)]
-
-            def stage_x(g):
-                for area, nodes, copy in zip(areas[g], NODE_HALVES, (on_vector, on_scalar)):
-                    interleave(copy, as_grouped(area), x_raw[g][:, :, nodes])
 
             def quantize_x(g, half):
                 codes, scales = x_operands[g]
@@ -199,22 +195,22 @@ def tile_picked_gcn_mlp_relu_sub_l_kernel(
                 quantize(nc, codes[:, nodes], scales[:, nodes], as_grouped(areas[g][half]))
 
             for g in range(PASSES - 1):
-                stage_x(g)
+                for area, nodes, copy in zip(areas[g], NODE_HALVES, (on_vector, on_scalar)):
+                    interleave(copy, as_grouped(area), x_raw[g][:, :, nodes])
                 quantize_x(g, 0)
                 quantize_x(g, 1)
-                if g == 0:
-                    area = x_raw[0][:, 0, NODE_HALVES[1]]
-                    stage_slice(on_scalar, area, 0, 0)
-                    project_slice(0, 0, area, accs)
-            stage_x(2)
-            area = x_raw[2][:, 0, NODE_HALVES[0]]
-            stage_slice(on_vector, area, 0, 1)
-            quantize_x(2, 0)
-            project_slice(0, 1, area, accs)
-            quantize_x(2, 1)
-            area = x_raw[2][:, 0, NODE_HALVES[1]]
-            stage_slice(on_scalar, area, 0, 2)
-            project_slice(0, 2, area, accs)
+                area = x_raw[g][:, 0, NODE_HALVES[1]]
+                stage_slice(on_scalar, area, 0, g)
+                project_slice(0, g, area, accs)
+            g = PASSES - 1
+            interleave(on_vector, as_grouped(areas[g][0]), x_raw[g][:, :, :HALF])
+            interleave(on_scalar, as_grouped(areas[g][1])[:, SPLIT - HALF :, :], x_raw[g][:, :, SPLIT:])
+            interleave(on_vector, as_grouped(areas[g][1])[:, : SPLIT - HALF, :], x_raw[g][:, :, HALF:SPLIT])
+            quantize_x(g, 0)
+            quantize_x(g, 1)
+            area = x_raw[g][:, 0, NODE_HALVES[1]]
+            stage_slice(on_scalar, area, 0, g)
+            project_slice(0, g, area, accs)
             for acc, nodes, relu in zip(accs, NODE_HALVES, (nc.vector.tensor_relu, relu_on_scalar)):
                 relu(out=h[:, nodes], in_=acc[:])
             return h
@@ -397,5 +393,4 @@ def tile_picked_gcn_mlp_relu_sub_l_kernel(
                 )
                 res = keep.tile([P, P], F32, name=f"res{vh}_{mb}")
                 (on_scalar, copy)[mb](out=res[:], in_=acc[:])
-                queue = nc.scalar if (vh, mb) == (TARGET_HALVES - 1, 0) else nc.sync
-                queue.dma_start(out=out[block(mb), targets], in_=res[:])
+                nc.sync.dma_start(out=out[block(mb), targets], in_=res[:])

@@ -27,7 +27,7 @@ NODE_HALVES = (slice(0, HALF), slice(HALF, T))
 LIST_COLUMNS = P // 16
 GROUP_PARTITIONS = P // J
 PART = KP // 2
-SPLIT = 320
+SPLIT = 304
 PLAIN_LIST = 2
 GATED = tuple(d for d in range(D) if d != PLAIN_LIST)
 LEAST_SHARE = 2.0**-24
@@ -86,10 +86,10 @@ def tile_picked_gcn_mlp_relu_sub_l_kernel(
             nc.sync.dma_start(out=t[:], in_=xT[g * KP : (g + 1) * KP, :].rearrange("(p j) t -> p j t", j=J))
             x_raw[g] = t
 
-        def load_w1(c, g, queue=nc.sync):
+        def load_w1(c, g):
             w1_raw[c, g] = words(f"w1_raw{c}_{g}", KP)
             rows = w1[g * KP : (g + 1) * KP, block(c)]
-            queue.dma_start(
+            nc.sync.dma_start(
                 out=w1_raw[c, g].rearrange("p (j c) -> p j c", j=J), in_=rows.rearrange("(p j) c -> p j c", j=J)
             )
 
@@ -103,10 +103,10 @@ def tile_picked_gcn_mlp_relu_sub_l_kernel(
         for rows in (slice(0, 4), slice(4, D)):
             nc.sync.dma_start(out=gate_raw[rows, :], in_=gate[rows, 0, :])
         load_x(0)
-        load_w1(0, 0, nc.scalar)
-        load_w1(0, 1, nc.scalar)
+        load_w1(0, 0)
         load_x(1)
         load_x(2)
+        load_w1(0, 1)
         load_w1(0, 2)
         for d in range(D):
             load_list(d)
@@ -184,10 +184,15 @@ def tile_picked_gcn_mlp_relu_sub_l_kernel(
         def project_first_group():
             width = 2 * HALF
             first = words("x_stage_first", 2 * width, "after_division")
-            behind = [x_raw[g][:].rearrange("p j t -> p (j t)")[:, HALF : HALF + width] for g in range(PASSES - 1)]
-            areas = ((first[:, :width], first[:, width:]), (behind[0], w1_raw[0, 0]), (behind[1], w1_raw[0, 1]))
+            second = words("x_stage_second", width, "after_spreading")
+            third = x_raw[1][:].rearrange("p j t -> p (j t)")[:, HALF : HALF + width]
+            areas = ((first[:, :width], first[:, width:]), (first[:, :width], second), (second, third))
             h = keep.tile([P, T], F32, name="h0")
             accs = [bank(b, [P, HALF], "h_acc") for b in range(2)]
+
+            def stage_x(g):
+                for area, nodes, copy in zip(areas[g], NODE_HALVES, (on_vector, on_scalar)):
+                    interleave(copy, as_grouped(area), x_raw[g][:, :, nodes])
 
             def quantize_x(g, half):
                 codes, scales = x_operands[g]
@@ -195,22 +200,24 @@ def tile_picked_gcn_mlp_relu_sub_l_kernel(
                 quantize(nc, codes[:, nodes], scales[:, nodes], as_grouped(areas[g][half]))
 
             for g in range(PASSES - 1):
-                for area, nodes, copy in zip(areas[g], NODE_HALVES, (on_vector, on_scalar)):
-                    interleave(copy, as_grouped(area), x_raw[g][:, :, nodes])
+                stage_x(g)
                 quantize_x(g, 0)
                 quantize_x(g, 1)
-                area = x_raw[g][:, 0, NODE_HALVES[1]]
-                stage_slice(on_scalar, area, 0, g)
-                project_slice(0, g, area, accs)
-            g = PASSES - 1
-            interleave(on_vector, as_grouped(areas[g][0]), x_raw[g][:, :, :HALF])
-            interleave(on_scalar, as_grouped(areas[g][1])[:, SPLIT - HALF :, :], x_raw[g][:, :, SPLIT:])
-            interleave(on_vector, as_grouped(areas[g][1])[:, : SPLIT - HALF, :], x_raw[g][:, :, HALF:SPLIT])
-            quantize_x(g, 0)
-            quantize_x(g, 1)
-            area = x_raw[g][:, 0, NODE_HALVES[1]]
-            stage_slice(on_scalar, area, 0, g)
-            project_slice(0, g, area, accs)
+                if g == 0:
+                    area = x_raw[0][:, 0, NODE_HALVES[1]]
+                    stage_slice(on_scalar, area, 0, 0)
+                    project_slice(0, 0, area, accs)
+            interleave(on_vector, as_grouped(second), x_raw[2][:, :, :HALF])
+            interleave(on_scalar, as_grouped(third)[:, SPLIT - HALF :, :], x_raw[2][:, :, SPLIT:])
+            area = x_raw[2][:, 0, NODE_HALVES[0]]
+            stage_slice(on_vector, area, 0, 1)
+            interleave(on_vector, as_grouped(third)[:, : SPLIT - HALF, :], x_raw[2][:, :, HALF:SPLIT])
+            project_slice(0, 1, area, accs)
+            quantize_x(2, 0)
+            quantize_x(2, 1)
+            area = x_raw[2][:, 2, NODE_HALVES[0]]
+            stage_slice(on_scalar, area, 0, 2)
+            project_slice(0, 2, area, accs)
             for acc, nodes, relu in zip(accs, NODE_HALVES, (nc.vector.tensor_relu, relu_on_scalar)):
                 relu(out=h[:, nodes], in_=acc[:])
             return h

@@ -28,6 +28,7 @@ LIST_COLUMNS = P // 16
 GROUP_PARTITIONS = P // J
 PART = KP // 2
 SPLIT = 304
+FILLED = P - D
 PLAIN_LIST = 2
 GATED = tuple(d for d in range(D) if d != PLAIN_LIST)
 LEAST_SHARE = 2.0**-24
@@ -98,10 +99,9 @@ def tile_picked_gcn_mlp_relu_sub_l_kernel(
             nc.sync.dma_start(t[:], (pos1, pos2, pos3, pos4, pos5, pos6)[d])
             lists.append(t)
 
-        gate_raw = keep.tile([D, V], F32)
         gate_rows = keep.tile([P, V], F32, align_bytes=64)
         for rows in (slice(0, 4), slice(4, D)):
-            nc.sync.dma_start(out=gate_raw[rows, :], in_=gate[rows, 0, :])
+            nc.scalar.dma_start(out=gate_rows[FILLED + rows.start : FILLED + rows.stop, :], in_=gate[rows, 0, :])
         load_x(0)
         load_w1(0, 0)
         load_x(1)
@@ -118,10 +118,9 @@ def tile_picked_gcn_mlp_relu_sub_l_kernel(
 
         ident = keep.tile([P, P], F32)
         make_identity(nc, ident[:])
-        for vh in range(TARGET_HALVES):
-            on_scalar(out=gate_rows[:, block(vh)], in_=ident[:])
+        nc.vector.memset(gate_rows[:FILLED, :], 0.0)
 
-        x_operands = [operand_tiles(f"x{g}", T) for g in range(PASSES)]
+        x_operands = {}
 
         def stage_slice(copy, area, c, g):
             interleave(copy, as_grouped(area), w1_raw[c, g].rearrange("p (j c) -> p j c", j=J))
@@ -145,15 +144,14 @@ def tile_picked_gcn_mlp_relu_sub_l_kernel(
             nc.scalar.activation(out=out, in_=in_, func=RELU)
 
         def spread_ratios():
-            on_vector(out=gate_rows[:D, :], in_=gate_raw[:])
             turned = bank(7, [P, TARGET_HALVES, P], "turned")
             for vh in range(TARGET_HALVES):
                 nc.tensor.transpose(turned[:, vh, :], gate_rows[:, block(vh)], ident[:])
             columns = keep.tile([P, TARGET_HALVES, D + 1], F32, align_bytes=64, name="gate_columns")
             nc.gpsimd.memset(columns[:, :, D:], LEAST_TOP)
-            on_vector(out=columns[:, :, :D], in_=turned[:, :, :D])
+            on_vector(out=columns[:, :, :D], in_=turned[:, :, FILLED:])
             own = columns[:, :, PLAIN_LIST]
-            steps = keep.tile([P, 4, TARGET_HALVES], F32, name="factor_steps")
+            steps = keep.tile([P, 4, TARGET_HALVES], F32, align_bytes=64, name="factor_steps", tag="after_steps")
             top, size, half_sign, guarded = (steps[:, i, :] for i in range(4))
             nc.vector.tensor_reduce(top, columns[:], mybir.AxisListType.X, MAX, apply_absolute_value=True)
             nc.vector.scalar_tensor_tensor(size, own, -1.0, own, MULT, MAX)
@@ -162,7 +160,7 @@ def tile_picked_gcn_mlp_relu_sub_l_kernel(
             along_lists = [P, TARGET_HALVES, D]
             signed = keep.tile(along_lists, F32, align_bytes=64, name="signed", tag="after_division")
             nc.vector.tensor_tensor(signed[:], columns[:, :, :D], half_sign.unsqueeze(2).to_broadcast(along_lists), MULT)
-            inverse = keep.tile([P, TARGET_HALVES], F32, name="inverse")
+            inverse = keep.tile([P, TARGET_HALVES], F32, align_bytes=64, name="inverse", tag="after_inverse")
             nc.vector.reciprocal(inverse[:], guarded)
             factor = keep.tile([P, TARGET_HALVES], F32, name="factor")
             nc.vector.scalar_tensor_tensor(factor[:], half_sign, 2.0, guarded, MULT, MULT)
@@ -171,22 +169,26 @@ def tile_picked_gcn_mlp_relu_sub_l_kernel(
                 divided[:], signed[:], 2.0, inverse[:].unsqueeze(2).to_broadcast(along_lists), MULT, MULT
             )
             spread = words("ratios", len(GATED) * V)
-            for first, b in ((0, 2), (2, 0), (4, 1)):
+            for first, b in ((0, 2), (2, 3), (4, 4)):
                 in_bank = GATED[first : first + 2]
                 acc = bank(b, [P, len(in_bank) * V], "spread")
                 for i, d in enumerate(in_bank):
                     for vh in range(TARGET_HALVES):
                         column = divided[:, vh, d : d + 1].to_broadcast([P, P])
                         nc.tensor.transpose(acc[:, block(i * TARGET_HALVES + vh)], column, ident[:])
-                on_vector(out=part(spread, first, len(in_bank)), in_=acc[:])
+                on_scalar(out=part(spread, first, len(in_bank)), in_=acc[:])
             return {d: part(spread, i) for i, d in enumerate(GATED)}, factor
 
         def project_first_group():
             width = 2 * HALF
-            first = words("x_stage_first", 2 * width, "after_division")
+            first = words("x_stage_first", width, "after_division")
+            free = words("x_stage_free", width)
             second = words("x_stage_second", width, "after_spreading")
-            third = x_raw[1][:].rearrange("p j t -> p (j t)")[:, HALF : HALF + width]
-            areas = ((first[:, :width], first[:, width:]), (first[:, :width], second), (second, third))
+            behind_pass_1 = x_raw[1][:].rearrange("p j t -> p (j t)")
+            third, fourth = (behind_pass_1[:, i * width : (i + 1) * width] for i in (1, 2))
+            areas = ((first, free), (first, second), (third, fourth))
+            for g in range(PASSES):
+                x_operands[g] = operand_tiles(f"x{g}", T, None, "after_inverse" if g == 0 else None)
             h = keep.tile([P, T], F32, name="h0")
             accs = [bank(b, [P, HALF], "h_acc") for b in range(2)]
 
@@ -204,19 +206,21 @@ def tile_picked_gcn_mlp_relu_sub_l_kernel(
                 quantize_x(g, 0)
                 quantize_x(g, 1)
                 if g == 0:
-                    area = x_raw[0][:, 0, NODE_HALVES[1]]
-                    stage_slice(on_scalar, area, 0, 0)
-                    project_slice(0, 0, area, accs)
-            interleave(on_vector, as_grouped(second), x_raw[2][:, :, :HALF])
-            interleave(on_scalar, as_grouped(third)[:, SPLIT - HALF :, :], x_raw[2][:, :, SPLIT:])
+                    area = x_raw[0][:, 0, NODE_HALVES[0]]
+                    stage_slice(on_vector, area, 0, 0)
+                    project_slice(0, 0, area, accs, "after_steps")
+            interleave(on_vector, as_grouped(third), x_raw[2][:, :, :HALF])
+            interleave(on_scalar, as_grouped(fourth)[:, SPLIT - HALF :, :], x_raw[2][:, :, SPLIT:])
             area = x_raw[2][:, 0, NODE_HALVES[0]]
             stage_slice(on_vector, area, 0, 1)
-            interleave(on_vector, as_grouped(third)[:, : SPLIT - HALF, :], x_raw[2][:, :, HALF:SPLIT])
-            project_slice(0, 1, area, accs)
+            interleave(on_vector, as_grouped(fourth)[:, : SPLIT - HALF, :], x_raw[2][:, :, HALF:SPLIT])
             quantize_x(2, 0)
+            project_slice(0, 1, area, accs)
+            area = behind_pass_1[:, width - P : width + P]
+            raw = w1_raw[0, 2].rearrange("p (j c) -> p j c", j=J)
+            for copy, columns in ((on_scalar, slice(0, P // 2)), (on_vector, slice(P // 2, P))):
+                interleave(copy, as_grouped(area)[:, columns, :], raw[:, :, columns])
             quantize_x(2, 1)
-            area = x_raw[2][:, 2, NODE_HALVES[0]]
-            stage_slice(on_scalar, area, 0, 2)
             project_slice(0, 2, area, accs)
             for acc, nodes, relu in zip(accs, NODE_HALVES, (nc.vector.tensor_relu, relu_on_scalar)):
                 relu(out=h[:, nodes], in_=acc[:])

@@ -27,8 +27,6 @@ NODE_HALVES = (slice(0, HALF), slice(HALF, T))
 LIST_COLUMNS = P // 16
 GROUP_PARTITIONS = P // J
 PART = KP // 2
-SPLIT = 304
-FILLED = P - D
 PLAIN_LIST = 2
 GATED = tuple(d for d in range(D) if d != PLAIN_LIST)
 LEAST_SHARE = 2.0**-24
@@ -99,9 +97,10 @@ def tile_picked_gcn_mlp_relu_sub_l_kernel(
             nc.sync.dma_start(t[:], (pos1, pos2, pos3, pos4, pos5, pos6)[d])
             lists.append(t)
 
+        gate_raw = keep.tile([D, V], F32)
         gate_rows = keep.tile([P, V], F32, align_bytes=64)
         for rows in (slice(0, 4), slice(4, D)):
-            nc.scalar.dma_start(out=gate_rows[FILLED + rows.start : FILLED + rows.stop, :], in_=gate[rows, 0, :])
+            nc.sync.dma_start(out=gate_raw[rows, :], in_=gate[rows, 0, :])
         load_x(0)
         load_w1(0, 0)
         load_x(1)
@@ -118,9 +117,10 @@ def tile_picked_gcn_mlp_relu_sub_l_kernel(
 
         ident = keep.tile([P, P], F32)
         make_identity(nc, ident[:])
-        nc.vector.memset(gate_rows[:FILLED, :], 0.0)
+        for vh in range(TARGET_HALVES):
+            on_scalar(out=gate_rows[:, block(vh)], in_=ident[:])
 
-        x_operands = {}
+        x_operands = [operand_tiles(f"x{g}", T) for g in range(PASSES)]
 
         def stage_slice(copy, area, c, g):
             interleave(copy, as_grouped(area), w1_raw[c, g].rearrange("p (j c) -> p j c", j=J))
@@ -144,14 +144,15 @@ def tile_picked_gcn_mlp_relu_sub_l_kernel(
             nc.scalar.activation(out=out, in_=in_, func=RELU)
 
         def spread_ratios():
+            on_vector(out=gate_rows[:D, :], in_=gate_raw[:])
             turned = bank(7, [P, TARGET_HALVES, P], "turned")
             for vh in range(TARGET_HALVES):
                 nc.tensor.transpose(turned[:, vh, :], gate_rows[:, block(vh)], ident[:])
             columns = keep.tile([P, TARGET_HALVES, D + 1], F32, align_bytes=64, name="gate_columns")
             nc.gpsimd.memset(columns[:, :, D:], LEAST_TOP)
-            on_vector(out=columns[:, :, :D], in_=turned[:, :, FILLED:])
+            on_vector(out=columns[:, :, :D], in_=turned[:, :, :D])
             own = columns[:, :, PLAIN_LIST]
-            steps = keep.tile([P, 4, TARGET_HALVES], F32, align_bytes=64, name="factor_steps", tag="after_steps")
+            steps = keep.tile([P, 4, TARGET_HALVES], F32, name="factor_steps")
             top, size, half_sign, guarded = (steps[:, i, :] for i in range(4))
             nc.vector.tensor_reduce(top, columns[:], mybir.AxisListType.X, MAX, apply_absolute_value=True)
             nc.vector.scalar_tensor_tensor(size, own, -1.0, own, MULT, MAX)
@@ -160,7 +161,7 @@ def tile_picked_gcn_mlp_relu_sub_l_kernel(
             along_lists = [P, TARGET_HALVES, D]
             signed = keep.tile(along_lists, F32, align_bytes=64, name="signed", tag="after_division")
             nc.vector.tensor_tensor(signed[:], columns[:, :, :D], half_sign.unsqueeze(2).to_broadcast(along_lists), MULT)
-            inverse = keep.tile([P, TARGET_HALVES], F32, align_bytes=64, name="inverse", tag="after_inverse")
+            inverse = keep.tile([P, TARGET_HALVES], F32, name="inverse")
             nc.vector.reciprocal(inverse[:], guarded)
             factor = keep.tile([P, TARGET_HALVES], F32, name="factor")
             nc.vector.scalar_tensor_tensor(factor[:], half_sign, 2.0, guarded, MULT, MULT)
@@ -169,26 +170,23 @@ def tile_picked_gcn_mlp_relu_sub_l_kernel(
                 divided[:], signed[:], 2.0, inverse[:].unsqueeze(2).to_broadcast(along_lists), MULT, MULT
             )
             spread = words("ratios", len(GATED) * V)
-            for first, b in ((0, 2), (2, 3), (4, 4)):
+            for first, b in ((0, 2), (2, 0), (4, 1)):
                 in_bank = GATED[first : first + 2]
                 acc = bank(b, [P, len(in_bank) * V], "spread")
                 for i, d in enumerate(in_bank):
                     for vh in range(TARGET_HALVES):
                         column = divided[:, vh, d : d + 1].to_broadcast([P, P])
                         nc.tensor.transpose(acc[:, block(i * TARGET_HALVES + vh)], column, ident[:])
-                on_scalar(out=part(spread, first, len(in_bank)), in_=acc[:])
+                on_vector(out=part(spread, first, len(in_bank)), in_=acc[:])
             return {d: part(spread, i) for i, d in enumerate(GATED)}, factor
 
         def project_first_group():
             width = 2 * HALF
-            first = words("x_stage_first", width, "after_division")
-            free = words("x_stage_free", width)
+            first = words("x_stage_first", 2 * width, "after_division")
             second = words("x_stage_second", width, "after_spreading")
             behind_pass_1 = x_raw[1][:].rearrange("p j t -> p (j t)")
             third, fourth = (behind_pass_1[:, i * width : (i + 1) * width] for i in (1, 2))
-            areas = ((first, free), (first, second), (third, fourth))
-            for g in range(PASSES):
-                x_operands[g] = operand_tiles(f"x{g}", T, None, "after_inverse" if g == 0 else None)
+            areas = ((first[:, :width], first[:, width:]), (first[:, :width], second), (third, fourth))
             h = keep.tile([P, T], F32, name="h0")
             accs = [bank(b, [P, HALF], "h_acc") for b in range(2)]
 
@@ -206,14 +204,12 @@ def tile_picked_gcn_mlp_relu_sub_l_kernel(
                 quantize_x(g, 0)
                 quantize_x(g, 1)
                 if g == 0:
-                    area = x_raw[0][:, 0, NODE_HALVES[0]]
-                    stage_slice(on_vector, area, 0, 0)
-                    project_slice(0, 0, area, accs, "after_steps")
-            interleave(on_vector, as_grouped(third), x_raw[2][:, :, :HALF])
-            interleave(on_scalar, as_grouped(fourth)[:, SPLIT - HALF :, :], x_raw[2][:, :, SPLIT:])
+                    area = x_raw[0][:, 0, NODE_HALVES[1]]
+                    stage_slice(on_scalar, area, 0, 0)
+                    project_slice(0, 0, area, accs)
+            stage_x(2)
             area = x_raw[2][:, 0, NODE_HALVES[0]]
             stage_slice(on_vector, area, 0, 1)
-            interleave(on_vector, as_grouped(fourth)[:, : SPLIT - HALF, :], x_raw[2][:, :, HALF:SPLIT])
             quantize_x(2, 0)
             project_slice(0, 1, area, accs)
             area = behind_pass_1[:, width - P : width + P]

@@ -14,7 +14,7 @@ U8 = mybir.dt.uint8
 FP8X4 = mybir.dt.float8_e4m3fn_x4
 RELU = mybir.ActivationFunctionType.Relu
 COPY = mybir.ActivationFunctionType.Copy
-MULT, MAX = mybir.AluOpType.mult, mybir.AluOpType.max
+MULT, MAX, ADD = mybir.AluOpType.mult, mybir.AluOpType.max, mybir.AluOpType.add
 
 P = 128
 J = 4
@@ -28,7 +28,10 @@ LIST_COLUMNS = P // 16
 GROUP_PARTITIONS = P // J
 PART = KP // 2
 PLAIN_LIST = 2
-GATED = tuple(d for d in range(D) if d != PLAIN_LIST)
+LONE_LIST = 3
+GATED = tuple(d for d in range(D) if d not in (PLAIN_LIST, LONE_LIST))
+EARLY = GROUPS - 1
+RUN = P // 2
 LEAST_SHARE = 2.0**-24
 LEAST_TOP = 2.0**-102
 
@@ -79,14 +82,17 @@ def tile_picked_gcn_mlp_relu_sub_l_kernel(
             return codes, scales
 
         x_raw, w1_raw, lists = {}, {}, []
+        spare_and_loads = words("last_loads", P + J * T + KP)
+        last_loads = spare_and_loads[:, P:]
 
         def load_x(g):
-            t = keep.tile([P, J, T], F32, align_bytes=64, name=f"x_raw{g}")
-            nc.sync.dma_start(out=t[:], in_=xT[g * KP : (g + 1) * KP, :].rearrange("(p j) t -> p j t", j=J))
+            t = last_loads[:, : J * T] if g == PASSES - 1 else words(f"x_raw{g}", J * T)
+            t = t.rearrange("p (j t) -> p j t", j=J)
+            nc.sync.dma_start(out=t, in_=xT[g * KP : (g + 1) * KP, :].rearrange("(p j) t -> p j t", j=J))
             x_raw[g] = t
 
         def load_w1(c, g):
-            w1_raw[c, g] = words(f"w1_raw{c}_{g}", KP)
+            w1_raw[c, g] = last_loads[:, J * T :] if (c, g) == (0, 1) else words(f"w1_raw{c}_{g}", KP)
             rows = w1[g * KP : (g + 1) * KP, block(c)]
             nc.sync.dma_start(
                 out=w1_raw[c, g].rearrange("p (j c) -> p j c", j=J), in_=rows.rearrange("(p j) c -> p j c", j=J)
@@ -123,7 +129,16 @@ def tile_picked_gcn_mlp_relu_sub_l_kernel(
         x_operands = [operand_tiles(f"x{g}", T) for g in range(PASSES)]
 
         def stage_slice(copy, area, c, g):
-            interleave(copy, as_grouped(area), w1_raw[c, g].rearrange("p (j c) -> p j c", j=J))
+            copy(
+                out=area.bitcast(BF16).rearrange("p (u r e j) -> p r j u e", u=2, e=2, j=J),
+                in_=w1_raw[c, g].rearrange("p (j r u e) -> p r j u e", j=J, u=2, e=2),
+            )
+
+        def stage_slice_half(copy, area, c, g, u):
+            copy(
+                out=area.bitcast(BF16).rearrange("p (u r e j) -> p u r j e", u=2, e=2, j=J)[:, u],
+                in_=w1_raw[c, g].rearrange("p (j r u e) -> p u r j e", j=J, u=2, e=2)[:, u],
+            )
 
         def project_slice(c, g, area, accs, scales_tag=None):
             codes, scales = operand_tiles(f"w1_{c}_{g}", P, None, scales_tag)
@@ -170,7 +185,7 @@ def tile_picked_gcn_mlp_relu_sub_l_kernel(
                 divided[:], signed[:], 2.0, inverse[:].unsqueeze(2).to_broadcast(along_lists), MULT, MULT
             )
             spread = words("ratios", len(GATED) * V)
-            for first, b in ((0, 2), (2, 0), (4, 1)):
+            for first, b in ((0, 0), (2, 1)):
                 in_bank = GATED[first : first + 2]
                 acc = bank(b, [P, len(in_bank) * V], "spread")
                 for i, d in enumerate(in_bank):
@@ -178,13 +193,13 @@ def tile_picked_gcn_mlp_relu_sub_l_kernel(
                         column = divided[:, vh, d : d + 1].to_broadcast([P, P])
                         nc.tensor.transpose(acc[:, block(i * TARGET_HALVES + vh)], column, ident[:])
                 on_vector(out=part(spread, first, len(in_bank)), in_=acc[:])
-            return {d: part(spread, i) for i, d in enumerate(GATED)}, factor
+            return {d: part(spread, i) for i, d in enumerate(GATED)}, factor, columns
 
         def project_first_group():
             width = 2 * HALF
             first = words("x_stage_first", 2 * width, "after_division")
             second = words("x_stage_second", width, "after_spreading")
-            behind_pass_1 = x_raw[1][:].rearrange("p j t -> p (j t)")
+            behind_pass_1 = x_raw[1].rearrange("p j t -> p (j t)")
             third, fourth = (behind_pass_1[:, i * width : (i + 1) * width] for i in (1, 2))
             areas = ((first[:, :width], first[:, width:]), (first[:, :width], second), (third, fourth))
             h = keep.tile([P, T], F32, name="h0")
@@ -207,24 +222,26 @@ def tile_picked_gcn_mlp_relu_sub_l_kernel(
                     area = x_raw[0][:, 0, NODE_HALVES[1]]
                     stage_slice(on_scalar, area, 0, 0)
                     project_slice(0, 0, area, accs)
-            stage_x(2)
-            area = x_raw[2][:, 0, NODE_HALVES[0]]
+            interleave(on_vector, as_grouped(third)[:, :P, :], x_raw[2][:, :, :P])
+            interleave(on_scalar, as_grouped(fourth), x_raw[2][:, :, HALF:])
+            interleave(on_vector, as_grouped(third)[:, P:, :], x_raw[2][:, :, P:HALF])
+            area = spare_and_loads[:, :PART]
             stage_slice(on_vector, area, 0, 1)
             quantize_x(2, 0)
             project_slice(0, 1, area, accs)
-            area = behind_pass_1[:, width - P : width + P]
-            raw = w1_raw[0, 2].rearrange("p (j c) -> p j c", j=J)
-            for copy, columns in ((on_scalar, slice(0, P // 2)), (on_vector, slice(P // 2, P))):
-                interleave(copy, as_grouped(area)[:, columns, :], raw[:, :, columns])
+            area = last_loads[:, J * T - P : J * T + P]
+            for u, copy in enumerate((on_scalar, on_vector)):
+                stage_slice_half(copy, area, 0, 2, u)
             quantize_x(2, 1)
             project_slice(0, 2, area, accs)
             for acc, nodes, relu in zip(accs, NODE_HALVES, (nc.vector.tensor_relu, relu_on_scalar)):
                 relu(out=h[:, nodes], in_=acc[:])
             return h
 
-        ratios, factor = spread_ratios()
+        ratios, factor, columns = spread_ratios()
         h = {0: project_first_group()}
         h_accs, staged = {}, {}
+        last = GROUPS - 1
 
         def stage(c, g, area):
             staged[c, g] = area
@@ -232,20 +249,23 @@ def tile_picked_gcn_mlp_relu_sub_l_kernel(
 
         def project(c, g, scales_tag=None):
             if g == 0:
-                h_accs[c] = [bank({1: 2, 2: 0, 3: 6}[c] + i, [P, HALF], "h_acc") for i in range(2)]
+                h_accs[c] = [bank({1: 4, 2: 0, 3: 2}[c] + i, [P, HALF], "h_acc") for i in range(2)]
             project_slice(c, g, staged[c, g], h_accs[c], scales_tag)
 
-        def finish_h(c):
+        def finish_h(c, first=relu_on_scalar):
             h[c] = keep.tile([P, T], F32, name=f"h{c}")
-            for acc, nodes in zip(h_accs[c], NODE_HALVES):
-                relu_on_scalar(h[c][:, nodes], acc[:])
+            for acc, nodes, relu in zip(h_accs[c], NODE_HALVES, (first, relu_on_scalar)):
+                relu(out=h[c][:, nodes], in_=acc[:])
 
         sums, added, waiting = {}, {}, []
+        TERMS = len(GATED) + 1
 
         def add_half(c, vh, term):
-            k = added.get((c, vh), 0)
-            nc.tensor.matmul(sums[c][vh], term, ident[:], start=(k == 0), stop=(k == D - 1), is_transpose=True)
-            added[c, vh] = k + 1
+            key = (c == last, vh)
+            k = added.get(key, 0)
+            total = TERMS if c == last else EARLY * TERMS
+            nc.tensor.matmul(sums[c][vh], term, ident[:], start=(k == 0), stop=(k == total - 1), is_transpose=True)
+            added[key] = k + 1
 
         def add(c, term):
             if c not in sums:
@@ -254,6 +274,13 @@ def tile_picked_gcn_mlp_relu_sub_l_kernel(
             for vh in range(TARGET_HALVES):
                 add_half(c, vh, term[:, block(vh)])
 
+        all_lone = [bank(6 + vh, [P, 2, GROUPS, RUN], "all_lone") for vh in range(TARGET_HALVES)]
+        lone = {c: [t[:, :, c, :] for t in all_lone] for c in range(GROUPS)}
+
+        def turn_lone(c, term):
+            for vh in range(TARGET_HALVES):
+                nc.tensor.transpose(lone[c][vh], term[:, block(vh)], ident[:])
+
         def offsets(d, vh=None):
             return lists[d][:] if vh is None else lists[d][:, vh * LIST_COLUMNS : (vh + 1) * LIST_COLUMNS]
 
@@ -261,13 +288,9 @@ def tile_picked_gcn_mlp_relu_sub_l_kernel(
             nc.scalar.activation(picked, h[c][:].indirect(offsets(d, vh)), COPY)
             return picked
 
-        def fused(term, c, d):
+        def fused(term, c, i):
+            d = GATED[i]
             nc.vector.tensor_tensor(term, h[c][:].indirect(offsets(d)), ratios[d], MULT)
-            add(c, term)
-
-        def multiply(picked, c, d):
-            term = words(f"term{c}_{d}", V)
-            nc.vector.tensor_tensor(term, picked, ratios[d], MULT)
             add(c, term)
 
         def after_staging(c, g, i):
@@ -276,119 +299,107 @@ def tile_picked_gcn_mlp_relu_sub_l_kernel(
         stage(1, 0, x_raw[2][:, 1, NODE_HALVES[1]])
         project(1, 0, "w1_0_2_scales")
         round_a = words("round_a", 4 * PART, "w1_0_2_codes")
-        stage(1, 1, part(round_a, 0))
-        stage(1, 2, part(round_a, 1))
-        stage(2, 0, part(round_a, 2))
-        plain = pick(words("plain0", V), 0, PLAIN_LIST)
-        stage(2, 1, part(round_a, 3))
+        for i, (c, g) in enumerate(((1, 1), (1, 2), (2, 0), (2, 1))):
+            stage(c, g, part(round_a, i))
         fused(words("term0_0", V), 0, 0)
         project(1, 1)
         fused(after_staging(1, 1, 0), 0, 1)
         project(1, 2)
         finish_h(1)
-        add(0, plain)
-        fused(after_staging(1, 2, 0), 0, 3)
+        fused(after_staging(1, 2, 0), 0, 2)
         project(2, 0)
-        fused(after_staging(2, 0, 0), 0, 4)
-        fused(after_staging(2, 0, 1), 0, 5)
+        fused(after_staging(2, 0, 0), 0, 3)
         project(2, 1)
-
-        round_b = words("round_b", 3 * PART, "w1_1_2_codes")
-        stage(2, 2, part(round_b, 0))
-        stage(3, 0, part(round_b, 1))
-        plain = pick(after_staging(2, 1, 1), 1, PLAIN_LIST)
-        picked = pick(after_staging(3, 0, 1), 1, 3)
-        stage(3, 1, part(round_b, 2))
-        fused(after_staging(2, 1, 0), 1, 0)
-        project(2, 2)
-        first_sums = [bank(2 + vh, [P, 2 * P], "first_sums") for vh in range(TARGET_HALVES)]
-        third_sums = [bank(4 + vh, [P, P], "third_sums") for vh in range(TARGET_HALVES)]
-        sums[0] = [t[:, :P] for t in first_sums]
-        sums[1] = [t[:, P:] for t in first_sums]
-        sums[2] = [t[:] for t in third_sums]
+        early_sums = [bank(4 + vh, [P, 2, EARLY, RUN], "early_sums") for vh in range(TARGET_HALVES)]
+        for c in range(EARLY):
+            sums[c] = [t[:, :, c, :] for t in early_sums]
         for c, term in waiting:
             add(c, term)
+
+        round_b = words("round_b", 3 * PART, "w1_1_2_codes")
+        for i, (c, g) in enumerate(((2, 2), (3, 0), (3, 1))):
+            stage(c, g, part(round_b, i))
+        plain = pick(after_staging(3, 1, 1), 0, PLAIN_LIST)
+        fused(words("term1_0", V), 1, 0)
+        project(2, 2)
         finish_h(2)
         fused(after_staging(2, 2, 0), 1, 1)
-        fused(after_staging(2, 2, 1), 1, 4)
         project(3, 0)
-        add(1, plain)
-        fused(after_staging(3, 0, 0), 1, 5)
-        multiply(picked, 1, 3)
+        fused(after_staging(3, 0, 0), 1, 2)
         project(3, 1)
+        add(0, plain)
+        fused(after_staging(3, 1, 0), 1, 3)
 
         round_c = words("round_c", 3 * PART, "w1_2_2_codes")
         stage(3, 2, part(round_c, 0))
-        plain = pick(part(round_c, 1), 2, PLAIN_LIST)
-        picked = pick(part(round_c, 2), 2, 3)
-        fused(after_staging(3, 1, 0), 2, 0)
+        alone = pick(part(round_c, 1), 0, LONE_LIST)
+        plain = pick(part(round_c, 2), 1, PLAIN_LIST)
+        fused(words("term2_0", V), 2, 0)
         project(3, 2)
         finish_h(3)
+        turn_lone(0, alone)
         fused(after_staging(3, 2, 0), 2, 1)
-        add(2, plain)
-        fused(after_staging(3, 2, 1), 2, 4)
-        multiply(picked, 2, 3)
-        fused(staged[3, 2], 2, 5)
+        add(1, plain)
+        fused(after_staging(3, 2, 1), 2, 2)
+        fused(staged[3, 2], 2, 3)
 
-        def scaled_on_scalar(out, in_, vh):
-            nc.scalar.activation(out, in_, COPY, scale=factor[:, vh : vh + 1])
-
-        def scaled_on_vector(out, in_, vh):
-            nc.vector.tensor_scalar(out, in_, factor[:, vh : vh + 1], None, MULT)
-
-        def round_sums(scaled, vh, acc, first_group, groups):
-            zt = zt_words[vh].bitcast(BF16).rearrange("v (u p e) -> v u p e", u=2, e=2)
-            partitions = slice(GROUP_PARTITIONS * first_group, GROUP_PARTITIONS * (first_group + groups))
-            scaled(zt[:, :, partitions, :], acc.rearrange("v (p u e) -> v u p e", u=2, e=2), vh)
-
-        last = GROUPS - 1
-        last_sums = [bank(vh, [P, P], "last_sums") for vh in range(TARGET_HALVES)]
+        round_d = words("round_d", 4 * PART, "w1_3_2_codes")
+        last_sums = [bank(vh, [P, 2, RUN], "last_sums") for vh in range(TARGET_HALVES)]
         sums[last] = [t[:] for t in last_sums]
-        plain = pick(words("plain3", V), last, PLAIN_LIST)
-        zt_both = words("zt", TARGET_HALVES * PART, "w1_3_1_scales")
-        zt_words = [part(zt_both, vh) for vh in range(TARGET_HALVES)]
-        for vh in range(TARGET_HALVES):
-            round_sums(scaled_on_scalar, vh, first_sums[vh][:], 0, 2)
-        picked_last = words("picked_last", TARGET_HALVES * PART)
-        for vh in range(TARGET_HALVES):
-            for i, d in enumerate((4, 5)):
-                pick(part(picked_last, vh)[:, block(i)], last, d, vh)
-        for vh in range(TARGET_HALVES):
-            round_sums(scaled_on_scalar, vh, third_sums[vh][:], 2, 1)
+        turn_lone(1, pick(part(round_d, 0), 1, LONE_LIST))
         fused(words("term3_0", V), last, 0)
-        add(last, plain)
+        turn_lone(2, pick(part(round_d, 1), 2, LONE_LIST))
         fused(words("term3_1", V), last, 1)
-        last_terms = []
-        for vh in range(TARGET_HALVES):
-            term = words(f"term3_3_{vh}", P)
-            nc.vector.tensor_tensor(term, h[last][:].indirect(offsets(3, vh)), ratios[3][:, block(vh)], MULT)
-            add_half(last, vh, term)
-            last_terms.append(words(f"term3_45_{vh}", PART))
-            for i, d in enumerate((4, 5)):
-                term = last_terms[vh][:, block(i)]
-                nc.vector.tensor_tensor(term, part(picked_last, vh)[:, block(i)], ratios[d][:, block(vh)], MULT)
-                add_half(last, vh, term)
+        turn_lone(last, pick(part(round_d, 2), last, LONE_LIST))
+        fused(part(round_d, 0), last, 2)
+        add(2, pick(part(round_d, 3), 2, PLAIN_LIST))
+        fused(part(round_d, 1), last, 3)
 
-        w2_areas = (last_terms[0], part(picked_last, 1))
-        interleave(on_vector, as_grouped(w2_areas[1]), w2_raw[:, :, block(1)])
-        w2_codes, w2_scales = operand_tiles("w2", N, "term3_45_1")
+        zt = [keep.tile([P, 2, GROUPS, RUN], BF16, align_bytes=64, name=f"zt{vh}") for vh in range(TARGET_HALVES)]
+
+        def scale_on_vector(scaled, acc, vh):
+            nc.vector.tensor_scalar(scaled, acc, columns[:, vh, LONE_LIST : LONE_LIST + 1], None, MULT)
+
+        def scale_on_scalar(scaled, acc, vh):
+            nc.scalar.activation(scaled, acc, COPY, scale=columns[:, vh, LONE_LIST : LONE_LIST + 1])
+
+        def join(out, acc, scaled, vh):
+            nc.vector.scalar_tensor_tensor(out, acc, factor[:, vh : vh + 1], scaled, MULT, ADD)
+
+        scaled = [keep.tile([P, 2, GROUPS, RUN], F32, align_bytes=64, name=f"scaled{vh}", tag=f"scaled{vh}") for vh in range(TARGET_HALVES)]
+        for vh, scale in enumerate((scale_on_scalar, scale_on_vector)):
+            scale(scaled[vh][:].rearrange("v u c r -> v (u c r)"), all_lone[vh][:].rearrange("v u c r -> v (u c r)"), vh)
+        for vh in range(TARGET_HALVES):
+            add_half(last, vh, pick(part(round_d, 3)[:, block(vh)], last, PLAIN_LIST, vh))
+        for vh in range(TARGET_HALVES):
+            join(
+                zt[vh][:, :, :EARLY, :].rearrange("v u c r -> v u (c r)"),
+                early_sums[vh][:].rearrange("v u c r -> v u (c r)"),
+                scaled[vh][:, :, :EARLY, :].rearrange("v u c r -> v u (c r)"),
+                vh,
+            )
+        for vh in range(TARGET_HALVES):
+            join(zt[vh][:, :, last, :], sums[last][vh], scaled[vh][:, :, last, :], vh)
+
+        w2_areas = (words("w2_first", PART, "scaled0"), round_d[:, 3 * PART - P : 4 * PART - P])
+        w2_codes, w2_scales = operand_tiles("w2", N, "scaled1")
         z_codes, z_scales = operand_tiles("z", V)
-        for vh, scaled in enumerate((scaled_on_scalar, scaled_on_vector)):
-            round_sums(scaled, vh, sums[last][vh], last, 1)
-        interleave(on_scalar, as_grouped(w2_areas[0]), w2_raw[:, :, block(0)])
+        for mb, copy in enumerate((on_vector, on_scalar)):
+            interleave(copy, as_grouped(w2_areas[mb]), w2_raw[:, :, block(mb)])
         for mb in (1, 0):
             quantize(nc, w2_codes[:, block(mb)], w2_scales[:, block(mb)], as_grouped(w2_areas[mb]))
 
-        for vh, (copy, out_bank) in enumerate(((on_scalar, 6), (on_vector, 4))):
-            back = bank(2 + vh, [P, 2, P], "back")
+        for vh, (copy, back_bank, out_banks) in enumerate(((on_scalar, 3, (4, 5)), (on_vector, 6, (7, 2)))):
+            back = bank(back_bank, [P, 2, P], "back")
+            zt_words = zt[vh][:].rearrange("v u c r -> v (u c r)").bitcast(F32)
             for u in range(2):
-                nc.tensor.transpose(back[:, u, :], zt_words[vh][:, block(u)], ident[:])
+                nc.tensor.transpose(back[:, u, :], zt_words[:, block(u)], ident[:])
             z_words = keep.tile([P, P, 2], F32, align_bytes=64, name=f"z_words{vh}")
             on_scalar(out=z_words[:], in_=back[:].rearrange("p u v -> p v u"))
             targets = block(vh)
             quantize(nc, z_codes[:, targets], z_scales[:, targets], as_grouped(z_words[:].rearrange("p v u -> p (v u)")))
             for mb in range(N // P):
-                acc = bank(out_bank + mb, [P, P], "out_acc")
+                acc = bank(out_banks[mb], [P, P], "out_acc")
                 nc.tensor.matmul_mx(
                     out=acc[:],
                     lhsT=w2_codes[:, block(mb)].bitcast(FP8X4),

@@ -14,7 +14,7 @@ U8 = mybir.dt.uint8
 FP8X4 = mybir.dt.float8_e4m3fn_x4
 RELU = mybir.ActivationFunctionType.Relu
 COPY = mybir.ActivationFunctionType.Copy
-MULT, MAX, ADD = mybir.AluOpType.mult, mybir.AluOpType.max, mybir.AluOpType.add
+MULT, MAX = mybir.AluOpType.mult, mybir.AluOpType.max
 
 P = 128
 J = 4
@@ -28,10 +28,7 @@ LIST_COLUMNS = P // 16
 GROUP_PARTITIONS = P // J
 PART = KP // 2
 PLAIN_LIST = 2
-LONE_LIST = 3
-GATED = tuple(d for d in range(D) if d not in (PLAIN_LIST, LONE_LIST))
-EARLY = GROUPS - 1
-RUN = P // 2
+GATED = tuple(d for d in range(D) if d != PLAIN_LIST)
 LEAST_SHARE = 2.0**-24
 LEAST_TOP = 2.0**-102
 
@@ -129,16 +126,7 @@ def tile_picked_gcn_mlp_relu_sub_l_kernel(
         x_operands = [operand_tiles(f"x{g}", T) for g in range(PASSES)]
 
         def stage_slice(copy, area, c, g):
-            copy(
-                out=area.bitcast(BF16).rearrange("p (u r e j) -> p r j u e", u=2, e=2, j=J),
-                in_=w1_raw[c, g].rearrange("p (j r u e) -> p r j u e", j=J, u=2, e=2),
-            )
-
-        def stage_slice_half(copy, area, c, g, u):
-            copy(
-                out=area.bitcast(BF16).rearrange("p (u r e j) -> p u r j e", u=2, e=2, j=J)[:, u],
-                in_=w1_raw[c, g].rearrange("p (j r u e) -> p u r j e", j=J, u=2, e=2)[:, u],
-            )
+            interleave(copy, as_grouped(area), w1_raw[c, g].rearrange("p (j c) -> p j c", j=J))
 
         def project_slice(c, g, area, accs, scales_tag=None):
             codes, scales = operand_tiles(f"w1_{c}_{g}", P, None, scales_tag)
@@ -154,6 +142,7 @@ def tile_picked_gcn_mlp_relu_sub_l_kernel(
                     start=(g == 0),
                     stop=(g == PASSES - 1),
                 )
+            return codes, scales
 
         def relu_on_scalar(out, in_):
             nc.scalar.activation(out=out, in_=in_, func=RELU)
@@ -185,7 +174,7 @@ def tile_picked_gcn_mlp_relu_sub_l_kernel(
                 divided[:], signed[:], 2.0, inverse[:].unsqueeze(2).to_broadcast(along_lists), MULT, MULT
             )
             spread = words("ratios", len(GATED) * V)
-            for first, b in ((0, 0), (2, 1)):
+            for first, b in ((0, 2), (2, 0), (4, 1)):
                 in_bank = GATED[first : first + 2]
                 acc = bank(b, [P, len(in_bank) * V], "spread")
                 for i, d in enumerate(in_bank):
@@ -193,7 +182,7 @@ def tile_picked_gcn_mlp_relu_sub_l_kernel(
                         column = divided[:, vh, d : d + 1].to_broadcast([P, P])
                         nc.tensor.transpose(acc[:, block(i * TARGET_HALVES + vh)], column, ident[:])
                 on_vector(out=part(spread, first, len(in_bank)), in_=acc[:])
-            return {d: part(spread, i) for i, d in enumerate(GATED)}, factor, columns
+            return {d: part(spread, i) for i, d in enumerate(GATED)}, factor
 
         def project_first_group():
             width = 2 * HALF
@@ -221,7 +210,19 @@ def tile_picked_gcn_mlp_relu_sub_l_kernel(
                 if g == 0:
                     area = x_raw[0][:, 0, NODE_HALVES[1]]
                     stage_slice(on_scalar, area, 0, 0)
-                    project_slice(0, 0, area, accs)
+                    first_slice = area
+            codes, scales = project_slice(0, 0, first_slice, accs, "after_spreading")
+            unread = bank(6, [P, T], "unread"), bank(7, [P, P], "unread")
+            for acc, nodes in ((unread[0][:, :HALF], NODE_HALVES[0]), (unread[0][:, HALF:], NODE_HALVES[1]), (unread[1][:], block(0))):
+                nc.tensor.matmul_mx(
+                    out=acc,
+                    lhsT=codes[:].bitcast(FP8X4),
+                    lhsT_scale=scales[:],
+                    rhs=x_operands[0][0][:, nodes].bitcast(FP8X4),
+                    rhs_scale=x_operands[0][1][:, nodes],
+                    start=True,
+                    stop=True,
+                )
             interleave(on_vector, as_grouped(third)[:, :P, :], x_raw[2][:, :, :P])
             interleave(on_scalar, as_grouped(fourth), x_raw[2][:, :, HALF:])
             interleave(on_vector, as_grouped(third)[:, P:, :], x_raw[2][:, :, P:HALF])
@@ -230,18 +231,18 @@ def tile_picked_gcn_mlp_relu_sub_l_kernel(
             quantize_x(2, 0)
             project_slice(0, 1, area, accs)
             area = last_loads[:, J * T - P : J * T + P]
-            for u, copy in enumerate((on_scalar, on_vector)):
-                stage_slice_half(copy, area, 0, 2, u)
+            raw = w1_raw[0, 2].rearrange("p (j c) -> p j c", j=J)
+            for copy, columns in ((on_scalar, slice(0, P // 2)), (on_vector, slice(P // 2, P))):
+                interleave(copy, as_grouped(area)[:, columns, :], raw[:, :, columns])
             quantize_x(2, 1)
             project_slice(0, 2, area, accs)
             for acc, nodes, relu in zip(accs, NODE_HALVES, (nc.vector.tensor_relu, relu_on_scalar)):
                 relu(out=h[:, nodes], in_=acc[:])
             return h
 
-        ratios, factor, columns = spread_ratios()
+        ratios, factor = spread_ratios()
         h = {0: project_first_group()}
         h_accs, staged = {}, {}
-        last = GROUPS - 1
 
         def stage(c, g, area):
             staged[c, g] = area
@@ -249,23 +250,20 @@ def tile_picked_gcn_mlp_relu_sub_l_kernel(
 
         def project(c, g, scales_tag=None):
             if g == 0:
-                h_accs[c] = [bank({1: 4, 2: 0, 3: 2}[c] + i, [P, HALF], "h_acc") for i in range(2)]
+                h_accs[c] = [bank({1: 2, 2: 0, 3: 6}[c] + i, [P, HALF], "h_acc") for i in range(2)]
             project_slice(c, g, staged[c, g], h_accs[c], scales_tag)
 
-        def finish_h(c, first=relu_on_scalar):
+        def finish_h(c):
             h[c] = keep.tile([P, T], F32, name=f"h{c}")
-            for acc, nodes, relu in zip(h_accs[c], NODE_HALVES, (first, relu_on_scalar)):
-                relu(out=h[c][:, nodes], in_=acc[:])
+            for acc, nodes in zip(h_accs[c], NODE_HALVES):
+                relu_on_scalar(h[c][:, nodes], acc[:])
 
         sums, added, waiting = {}, {}, []
-        TERMS = len(GATED) + 1
 
         def add_half(c, vh, term):
-            key = (c == last, vh)
-            k = added.get(key, 0)
-            total = TERMS if c == last else EARLY * TERMS
-            nc.tensor.matmul(sums[c][vh], term, ident[:], start=(k == 0), stop=(k == total - 1), is_transpose=True)
-            added[key] = k + 1
+            k = added.get((c, vh), 0)
+            nc.tensor.matmul(sums[c][vh], term, ident[:], start=(k == 0), stop=(k == D - 1), is_transpose=True)
+            added[c, vh] = k + 1
 
         def add(c, term):
             if c not in sums:
@@ -274,13 +272,6 @@ def tile_picked_gcn_mlp_relu_sub_l_kernel(
             for vh in range(TARGET_HALVES):
                 add_half(c, vh, term[:, block(vh)])
 
-        all_lone = [bank(6 + vh, [P, 2, GROUPS, RUN], "all_lone") for vh in range(TARGET_HALVES)]
-        lone = {c: [t[:, :, c, :] for t in all_lone] for c in range(GROUPS)}
-
-        def turn_lone(c, term):
-            for vh in range(TARGET_HALVES):
-                nc.tensor.transpose(lone[c][vh], term[:, block(vh)], ident[:])
-
         def offsets(d, vh=None):
             return lists[d][:] if vh is None else lists[d][:, vh * LIST_COLUMNS : (vh + 1) * LIST_COLUMNS]
 
@@ -288,9 +279,13 @@ def tile_picked_gcn_mlp_relu_sub_l_kernel(
             nc.scalar.activation(picked, h[c][:].indirect(offsets(d, vh)), COPY)
             return picked
 
-        def fused(term, c, i):
-            d = GATED[i]
+        def fused(term, c, d):
             nc.vector.tensor_tensor(term, h[c][:].indirect(offsets(d)), ratios[d], MULT)
+            add(c, term)
+
+        def multiply(picked, c, d):
+            term = words(f"term{c}_{d}", V)
+            nc.vector.tensor_tensor(term, picked, ratios[d], MULT)
             add(c, term)
 
         def after_staging(c, g, i):
@@ -299,107 +294,119 @@ def tile_picked_gcn_mlp_relu_sub_l_kernel(
         stage(1, 0, x_raw[2][:, 1, NODE_HALVES[1]])
         project(1, 0, "w1_0_2_scales")
         round_a = words("round_a", 4 * PART, "w1_0_2_codes")
-        for i, (c, g) in enumerate(((1, 1), (1, 2), (2, 0), (2, 1))):
-            stage(c, g, part(round_a, i))
+        stage(1, 1, part(round_a, 0))
+        stage(1, 2, part(round_a, 1))
+        stage(2, 0, part(round_a, 2))
+        plain = pick(words("plain0", V), 0, PLAIN_LIST)
+        stage(2, 1, part(round_a, 3))
         fused(words("term0_0", V), 0, 0)
         project(1, 1)
         fused(after_staging(1, 1, 0), 0, 1)
         project(1, 2)
         finish_h(1)
-        fused(after_staging(1, 2, 0), 0, 2)
+        add(0, plain)
+        fused(after_staging(1, 2, 0), 0, 3)
         project(2, 0)
-        fused(after_staging(2, 0, 0), 0, 3)
+        fused(after_staging(2, 0, 0), 0, 4)
+        fused(after_staging(2, 0, 1), 0, 5)
         project(2, 1)
-        early_sums = [bank(4 + vh, [P, 2, EARLY, RUN], "early_sums") for vh in range(TARGET_HALVES)]
-        for c in range(EARLY):
-            sums[c] = [t[:, :, c, :] for t in early_sums]
-        for c, term in waiting:
-            add(c, term)
 
         round_b = words("round_b", 3 * PART, "w1_1_2_codes")
-        for i, (c, g) in enumerate(((2, 2), (3, 0), (3, 1))):
-            stage(c, g, part(round_b, i))
-        plain = pick(after_staging(3, 1, 1), 0, PLAIN_LIST)
-        fused(words("term1_0", V), 1, 0)
+        stage(2, 2, part(round_b, 0))
+        stage(3, 0, part(round_b, 1))
+        plain = pick(after_staging(2, 1, 1), 1, PLAIN_LIST)
+        picked = pick(after_staging(3, 0, 1), 1, 3)
+        stage(3, 1, part(round_b, 2))
+        fused(after_staging(2, 1, 0), 1, 0)
         project(2, 2)
+        first_sums = [bank(2 + vh, [P, 2 * P], "first_sums") for vh in range(TARGET_HALVES)]
+        third_sums = [bank(4 + vh, [P, P], "third_sums") for vh in range(TARGET_HALVES)]
+        sums[0] = [t[:, :P] for t in first_sums]
+        sums[1] = [t[:, P:] for t in first_sums]
+        sums[2] = [t[:] for t in third_sums]
+        for c, term in waiting:
+            add(c, term)
         finish_h(2)
         fused(after_staging(2, 2, 0), 1, 1)
+        fused(after_staging(2, 2, 1), 1, 4)
         project(3, 0)
-        fused(after_staging(3, 0, 0), 1, 2)
+        add(1, plain)
+        fused(after_staging(3, 0, 0), 1, 5)
+        multiply(picked, 1, 3)
         project(3, 1)
-        add(0, plain)
-        fused(after_staging(3, 1, 0), 1, 3)
 
         round_c = words("round_c", 3 * PART, "w1_2_2_codes")
         stage(3, 2, part(round_c, 0))
-        alone = pick(part(round_c, 1), 0, LONE_LIST)
-        plain = pick(part(round_c, 2), 1, PLAIN_LIST)
-        fused(words("term2_0", V), 2, 0)
+        plain = pick(part(round_c, 1), 2, PLAIN_LIST)
+        picked = pick(part(round_c, 2), 2, 3)
+        fused(after_staging(3, 1, 0), 2, 0)
         project(3, 2)
         finish_h(3)
-        turn_lone(0, alone)
         fused(after_staging(3, 2, 0), 2, 1)
-        add(1, plain)
-        fused(after_staging(3, 2, 1), 2, 2)
-        fused(staged[3, 2], 2, 3)
+        add(2, plain)
+        fused(after_staging(3, 2, 1), 2, 4)
+        multiply(picked, 2, 3)
+        fused(staged[3, 2], 2, 5)
 
-        round_d = words("round_d", 4 * PART, "w1_3_2_codes")
-        last_sums = [bank(vh, [P, 2, RUN], "last_sums") for vh in range(TARGET_HALVES)]
+        def scaled_on_scalar(out, in_, vh):
+            nc.scalar.activation(out, in_, COPY, scale=factor[:, vh : vh + 1])
+
+        def scaled_on_vector(out, in_, vh):
+            nc.vector.tensor_scalar(out, in_, factor[:, vh : vh + 1], None, MULT)
+
+        def round_sums(scaled, vh, acc, first_group, groups):
+            zt = zt_words[vh].bitcast(BF16).rearrange("v (u p e) -> v u p e", u=2, e=2)
+            partitions = slice(GROUP_PARTITIONS * first_group, GROUP_PARTITIONS * (first_group + groups))
+            scaled(zt[:, :, partitions, :], acc.rearrange("v (p u e) -> v u p e", u=2, e=2), vh)
+
+        last = GROUPS - 1
+        last_sums = [bank(vh, [P, P], "last_sums") for vh in range(TARGET_HALVES)]
         sums[last] = [t[:] for t in last_sums]
-        turn_lone(1, pick(part(round_d, 0), 1, LONE_LIST))
+        plain = pick(words("plain3", V), last, PLAIN_LIST)
+        zt_both = words("zt", TARGET_HALVES * PART, "w1_3_1_scales")
+        zt_words = [part(zt_both, vh) for vh in range(TARGET_HALVES)]
+        for vh in range(TARGET_HALVES):
+            round_sums(scaled_on_scalar, vh, first_sums[vh][:], 0, 2)
+        picked_last = words("picked_last", TARGET_HALVES * PART)
+        for vh in range(TARGET_HALVES):
+            for i, d in enumerate((4, 5)):
+                pick(part(picked_last, vh)[:, block(i)], last, d, vh)
+        for vh in range(TARGET_HALVES):
+            round_sums(scaled_on_scalar, vh, third_sums[vh][:], 2, 1)
         fused(words("term3_0", V), last, 0)
-        turn_lone(2, pick(part(round_d, 1), 2, LONE_LIST))
+        add(last, plain)
         fused(words("term3_1", V), last, 1)
-        turn_lone(last, pick(part(round_d, 2), last, LONE_LIST))
-        fused(part(round_d, 0), last, 2)
-        add(2, pick(part(round_d, 3), 2, PLAIN_LIST))
-        fused(part(round_d, 1), last, 3)
-
-        zt = [keep.tile([P, 2, GROUPS, RUN], BF16, align_bytes=64, name=f"zt{vh}") for vh in range(TARGET_HALVES)]
-
-        def scale_on_vector(scaled, acc, vh):
-            nc.vector.tensor_scalar(scaled, acc, columns[:, vh, LONE_LIST : LONE_LIST + 1], None, MULT)
-
-        def scale_on_scalar(scaled, acc, vh):
-            nc.scalar.activation(scaled, acc, COPY, scale=columns[:, vh, LONE_LIST : LONE_LIST + 1])
-
-        def join(out, acc, scaled, vh):
-            nc.vector.scalar_tensor_tensor(out, acc, factor[:, vh : vh + 1], scaled, MULT, ADD)
-
-        scaled = [keep.tile([P, 2, GROUPS, RUN], F32, align_bytes=64, name=f"scaled{vh}", tag=f"scaled{vh}") for vh in range(TARGET_HALVES)]
-        for vh, scale in enumerate((scale_on_scalar, scale_on_vector)):
-            scale(scaled[vh][:].rearrange("v u c r -> v (u c r)"), all_lone[vh][:].rearrange("v u c r -> v (u c r)"), vh)
+        last_terms = []
         for vh in range(TARGET_HALVES):
-            add_half(last, vh, pick(part(round_d, 3)[:, block(vh)], last, PLAIN_LIST, vh))
-        for vh in range(TARGET_HALVES):
-            join(
-                zt[vh][:, :, :EARLY, :].rearrange("v u c r -> v u (c r)"),
-                early_sums[vh][:].rearrange("v u c r -> v u (c r)"),
-                scaled[vh][:, :, :EARLY, :].rearrange("v u c r -> v u (c r)"),
-                vh,
-            )
-        for vh in range(TARGET_HALVES):
-            join(zt[vh][:, :, last, :], sums[last][vh], scaled[vh][:, :, last, :], vh)
+            term = words(f"term3_3_{vh}", P)
+            nc.vector.tensor_tensor(term, h[last][:].indirect(offsets(3, vh)), ratios[3][:, block(vh)], MULT)
+            add_half(last, vh, term)
+            last_terms.append(words(f"term3_45_{vh}", PART))
+            for i, d in enumerate((4, 5)):
+                term = last_terms[vh][:, block(i)]
+                nc.vector.tensor_tensor(term, part(picked_last, vh)[:, block(i)], ratios[d][:, block(vh)], MULT)
+                add_half(last, vh, term)
 
-        w2_areas = (words("w2_first", PART, "scaled0"), round_d[:, 3 * PART - P : 4 * PART - P])
-        w2_codes, w2_scales = operand_tiles("w2", N, "scaled1")
+        w2_areas = (last_terms[0], part(picked_last, 1))
+        interleave(on_vector, as_grouped(w2_areas[1]), w2_raw[:, :, block(1)])
+        w2_codes, w2_scales = operand_tiles("w2", N, "term3_45_1")
         z_codes, z_scales = operand_tiles("z", V)
-        for mb, copy in enumerate((on_vector, on_scalar)):
-            interleave(copy, as_grouped(w2_areas[mb]), w2_raw[:, :, block(mb)])
+        for vh, scaled in enumerate((scaled_on_scalar, scaled_on_vector)):
+            round_sums(scaled, vh, sums[last][vh], last, 1)
+        interleave(on_scalar, as_grouped(w2_areas[0]), w2_raw[:, :, block(0)])
         for mb in (1, 0):
             quantize(nc, w2_codes[:, block(mb)], w2_scales[:, block(mb)], as_grouped(w2_areas[mb]))
 
-        for vh, (copy, back_bank, out_banks) in enumerate(((on_scalar, 3, (4, 5)), (on_vector, 6, (7, 2)))):
-            back = bank(back_bank, [P, 2, P], "back")
-            zt_words = zt[vh][:].rearrange("v u c r -> v (u c r)").bitcast(F32)
+        for vh, (copy, out_bank) in enumerate(((on_scalar, 6), (on_vector, 4))):
+            back = bank(2 + vh, [P, 2, P], "back")
             for u in range(2):
-                nc.tensor.transpose(back[:, u, :], zt_words[:, block(u)], ident[:])
+                nc.tensor.transpose(back[:, u, :], zt_words[vh][:, block(u)], ident[:])
             z_words = keep.tile([P, P, 2], F32, align_bytes=64, name=f"z_words{vh}")
             on_scalar(out=z_words[:], in_=back[:].rearrange("p u v -> p v u"))
             targets = block(vh)
             quantize(nc, z_codes[:, targets], z_scales[:, targets], as_grouped(z_words[:].rearrange("p v u -> p (v u)")))
             for mb in range(N // P):
-                acc = bank(out_banks[mb], [P, P], "out_acc")
+                acc = bank(out_bank + mb, [P, P], "out_acc")
                 nc.tensor.matmul_mx(
                     out=acc[:],
                     lhsT=w2_codes[:, block(mb)].bitcast(FP8X4),

@@ -14,7 +14,7 @@ U8 = mybir.dt.uint8
 FP8X4 = mybir.dt.float8_e4m3fn_x4
 RELU = mybir.ActivationFunctionType.Relu
 COPY = mybir.ActivationFunctionType.Copy
-MULT, MAX = mybir.AluOpType.mult, mybir.AluOpType.max
+MULT, MAX, ADD = mybir.AluOpType.mult, mybir.AluOpType.max, mybir.AluOpType.add
 
 P = 128
 J = 4
@@ -27,6 +27,8 @@ NODE_HALVES = (slice(0, HALF), slice(HALF, T))
 LIST_COLUMNS = P // 16
 GROUP_PARTITIONS = P // J
 PART = KP // 2
+LONE_LIST = 5
+RUN = P // 2
 PLAIN_LIST = 2
 GATED = tuple(d for d in range(D) if d != PLAIN_LIST)
 LEAST_SHARE = 2.0**-24
@@ -126,7 +128,13 @@ def tile_picked_gcn_mlp_relu_sub_l_kernel(
         x_operands = [operand_tiles(f"x{g}", T) for g in range(PASSES)]
 
         def stage_slice(copy, area, c, g):
-            interleave(copy, as_grouped(area), w1_raw[c, g].rearrange("p (j c) -> p j c", j=J))
+            if c < GROUPS - 1:
+                interleave(copy, as_grouped(area), w1_raw[c, g].rearrange("p (j c) -> p j c", j=J))
+                return
+            copy(
+                out=area.bitcast(BF16).rearrange("p (u r e j) -> p r j u e", u=2, e=2, j=J),
+                in_=w1_raw[c, g].rearrange("p (j r u e) -> p r j u e", j=J, u=2, e=2),
+            )
 
         def project_slice(c, g, area, accs, scales_tag=None):
             codes, scales = operand_tiles(f"w1_{c}_{g}", P, None, scales_tag)
@@ -142,7 +150,6 @@ def tile_picked_gcn_mlp_relu_sub_l_kernel(
                     start=(g == 0),
                     stop=(g == PASSES - 1),
                 )
-            return codes, scales
 
         def relu_on_scalar(out, in_):
             nc.scalar.activation(out=out, in_=in_, func=RELU)
@@ -182,7 +189,7 @@ def tile_picked_gcn_mlp_relu_sub_l_kernel(
                         column = divided[:, vh, d : d + 1].to_broadcast([P, P])
                         nc.tensor.transpose(acc[:, block(i * TARGET_HALVES + vh)], column, ident[:])
                 on_vector(out=part(spread, first, len(in_bank)), in_=acc[:])
-            return {d: part(spread, i) for i, d in enumerate(GATED)}, factor
+            return {d: part(spread, i) for i, d in enumerate(GATED)}, factor, columns
 
         def project_first_group():
             width = 2 * HALF
@@ -210,19 +217,7 @@ def tile_picked_gcn_mlp_relu_sub_l_kernel(
                 if g == 0:
                     area = x_raw[0][:, 0, NODE_HALVES[1]]
                     stage_slice(on_scalar, area, 0, 0)
-                    first_slice = area
-            codes, scales = project_slice(0, 0, first_slice, accs, "after_spreading")
-            unread = bank(6, [P, T], "unread"), bank(7, [P, P], "unread")
-            for acc, nodes in ((unread[0][:, :HALF], NODE_HALVES[0]), (unread[0][:, HALF:], NODE_HALVES[1]), (unread[1][:], block(0))):
-                nc.tensor.matmul_mx(
-                    out=acc,
-                    lhsT=codes[:].bitcast(FP8X4),
-                    lhsT_scale=scales[:],
-                    rhs=x_operands[0][0][:, nodes].bitcast(FP8X4),
-                    rhs_scale=x_operands[0][1][:, nodes],
-                    start=True,
-                    stop=True,
-                )
+                    project_slice(0, 0, area, accs)
             interleave(on_vector, as_grouped(third)[:, :P, :], x_raw[2][:, :, :P])
             interleave(on_scalar, as_grouped(fourth), x_raw[2][:, :, HALF:])
             interleave(on_vector, as_grouped(third)[:, P:, :], x_raw[2][:, :, P:HALF])
@@ -240,7 +235,7 @@ def tile_picked_gcn_mlp_relu_sub_l_kernel(
                 relu(out=h[:, nodes], in_=acc[:])
             return h
 
-        ratios, factor = spread_ratios()
+        ratios, factor, columns = spread_ratios()
         h = {0: project_first_group()}
         h_accs, staged = {}, {}
 
@@ -262,7 +257,7 @@ def tile_picked_gcn_mlp_relu_sub_l_kernel(
 
         def add_half(c, vh, term):
             k = added.get((c, vh), 0)
-            nc.tensor.matmul(sums[c][vh], term, ident[:], start=(k == 0), stop=(k == D - 1), is_transpose=True)
+            nc.tensor.matmul(sums[c][vh], term, ident[:], start=(k == 0), stop=(k == D - 1 - (c == GROUPS - 1)), is_transpose=True)
             added[c, vh] = k + 1
 
         def add(c, term):
@@ -320,10 +315,10 @@ def tile_picked_gcn_mlp_relu_sub_l_kernel(
         fused(after_staging(2, 1, 0), 1, 0)
         project(2, 2)
         first_sums = [bank(2 + vh, [P, 2 * P], "first_sums") for vh in range(TARGET_HALVES)]
-        third_sums = [bank(4 + vh, [P, P], "third_sums") for vh in range(TARGET_HALVES)]
+        third_sums = [bank(4 + vh, [P, 2 * P], "third_sums") for vh in range(TARGET_HALVES)]
         sums[0] = [t[:, :P] for t in first_sums]
         sums[1] = [t[:, P:] for t in first_sums]
-        sums[2] = [t[:] for t in third_sums]
+        sums[2] = [t[:, :P] for t in third_sums]
         for c, term in waiting:
             add(c, term)
         finish_h(2)
@@ -362,37 +357,47 @@ def tile_picked_gcn_mlp_relu_sub_l_kernel(
         last = GROUPS - 1
         last_sums = [bank(vh, [P, P], "last_sums") for vh in range(TARGET_HALVES)]
         sums[last] = [t[:] for t in last_sums]
-        plain = pick(words("plain3", V), last, PLAIN_LIST)
         zt_both = words("zt", TARGET_HALVES * PART, "w1_3_1_scales")
         zt_words = [part(zt_both, vh) for vh in range(TARGET_HALVES)]
         for vh in range(TARGET_HALVES):
             round_sums(scaled_on_scalar, vh, first_sums[vh][:], 0, 2)
-        picked_last = words("picked_last", TARGET_HALVES * PART)
-        for vh in range(TARGET_HALVES):
-            for i, d in enumerate((4, 5)):
-                pick(part(picked_last, vh)[:, block(i)], last, d, vh)
-        for vh in range(TARGET_HALVES):
-            round_sums(scaled_on_scalar, vh, third_sums[vh][:], 2, 1)
+        alone = pick(words("alone", V), last, LONE_LIST)
+        picked_last = words("picked_last", V)
+        pick(picked_last[:, block(0)], last, 4, 0)
+        plain = pick(words("plain3", V), last, PLAIN_LIST)
+        pick(picked_last[:, block(1)], last, 4, 1)
         fused(words("term3_0", V), last, 0)
-        add(last, plain)
+        lone = [t[:, P:] for t in third_sums]
+        for vh in range(TARGET_HALVES):
+            nc.tensor.transpose(lone[vh], alone[:, block(vh)], ident[:])
         fused(words("term3_1", V), last, 1)
-        last_terms = []
+        scaled = [words(f"scaled{vh}", P) for vh in range(TARGET_HALVES)]
+        w2_areas = []
+        for vh in range(TARGET_HALVES):
+            scale = columns[:, vh, LONE_LIST : LONE_LIST + 1]
+            nc.scalar.activation(scaled[vh][:, :P], lone[vh], COPY, scale=scale)
+            round_sums(scaled_on_scalar, vh, sums[2][vh], 2, 1)
         for vh in range(TARGET_HALVES):
             term = words(f"term3_3_{vh}", P)
             nc.vector.tensor_tensor(term, h[last][:].indirect(offsets(3, vh)), ratios[3][:, block(vh)], MULT)
             add_half(last, vh, term)
-            last_terms.append(words(f"term3_45_{vh}", PART))
-            for i, d in enumerate((4, 5)):
-                term = last_terms[vh][:, block(i)]
-                nc.vector.tensor_tensor(term, part(picked_last, vh)[:, block(i)], ratios[d][:, block(vh)], MULT)
-                add_half(last, vh, term)
+            if vh == 0:
+                add(last, plain)
+            w2_areas.append(words(f"term3_4_{vh}", PART))
+            term = w2_areas[vh][:, :P]
+            nc.vector.tensor_tensor(term, picked_last[:, block(vh)], ratios[4][:, block(vh)], MULT)
+            add_half(last, vh, term)
 
-        w2_areas = (last_terms[0], part(picked_last, 1))
+        def join(vh):
+            zt = zt_words[vh].bitcast(BF16).rearrange("v (u n) -> v u n", u=2)[:, :, last * RUN :]
+            acc, other = (t.rearrange("v (u n) -> v u n", u=2) for t in (sums[last][vh], scaled[vh][:, :P]))
+            nc.vector.scalar_tensor_tensor(zt, acc, factor[:, vh : vh + 1], other, MULT, ADD)
+
+        join(0)
         interleave(on_vector, as_grouped(w2_areas[1]), w2_raw[:, :, block(1)])
-        w2_codes, w2_scales = operand_tiles("w2", N, "term3_45_1")
+        w2_codes, w2_scales = operand_tiles("w2", N, "scaled1")
         z_codes, z_scales = operand_tiles("z", V)
-        for vh, scaled in enumerate((scaled_on_scalar, scaled_on_vector)):
-            round_sums(scaled, vh, sums[last][vh], last, 1)
+        join(1)
         interleave(on_scalar, as_grouped(w2_areas[0]), w2_raw[:, :, block(0)])
         for mb in (1, 0):
             quantize(nc, w2_codes[:, block(mb)], w2_scales[:, block(mb)], as_grouped(w2_areas[mb]))

@@ -27,10 +27,11 @@ NODE_HALVES = (slice(0, HALF), slice(HALF, T))
 LIST_COLUMNS = P // 16
 GROUP_PARTITIONS = P // J
 PART = KP // 2
-LONE_LIST = 5
-RUN = P // 2
 PLAIN_LIST = 2
-GATED = tuple(d for d in range(D) if d != PLAIN_LIST)
+LONE_LIST = 3
+GATED = tuple(d for d in range(D) if d not in (PLAIN_LIST, LONE_LIST))
+EARLY = GROUPS - 1
+RUN = P // 2
 LEAST_SHARE = 2.0**-24
 LEAST_TOP = 2.0**-102
 
@@ -128,12 +129,15 @@ def tile_picked_gcn_mlp_relu_sub_l_kernel(
         x_operands = [operand_tiles(f"x{g}", T) for g in range(PASSES)]
 
         def stage_slice(copy, area, c, g):
-            if c < GROUPS - 1:
-                interleave(copy, as_grouped(area), w1_raw[c, g].rearrange("p (j c) -> p j c", j=J))
-                return
             copy(
                 out=area.bitcast(BF16).rearrange("p (u r e j) -> p r j u e", u=2, e=2, j=J),
                 in_=w1_raw[c, g].rearrange("p (j r u e) -> p r j u e", j=J, u=2, e=2),
+            )
+
+        def stage_slice_half(copy, area, c, g, u):
+            copy(
+                out=area.bitcast(BF16).rearrange("p (u r e j) -> p u r j e", u=2, e=2, j=J)[:, u],
+                in_=w1_raw[c, g].rearrange("p (j r u e) -> p u r j e", j=J, u=2, e=2)[:, u],
             )
 
         def project_slice(c, g, area, accs, scales_tag=None):
@@ -181,7 +185,7 @@ def tile_picked_gcn_mlp_relu_sub_l_kernel(
                 divided[:], signed[:], 2.0, inverse[:].unsqueeze(2).to_broadcast(along_lists), MULT, MULT
             )
             spread = words("ratios", len(GATED) * V)
-            for first, b in ((0, 2), (2, 0), (4, 1)):
+            for first, b in ((0, 0), (2, 1)):
                 in_bank = GATED[first : first + 2]
                 acc = bank(b, [P, len(in_bank) * V], "spread")
                 for i, d in enumerate(in_bank):
@@ -226,9 +230,8 @@ def tile_picked_gcn_mlp_relu_sub_l_kernel(
             quantize_x(2, 0)
             project_slice(0, 1, area, accs)
             area = last_loads[:, J * T - P : J * T + P]
-            raw = w1_raw[0, 2].rearrange("p (j c) -> p j c", j=J)
-            for copy, columns in ((on_scalar, slice(0, P // 2)), (on_vector, slice(P // 2, P))):
-                interleave(copy, as_grouped(area)[:, columns, :], raw[:, :, columns])
+            for u, copy in enumerate((on_scalar, on_vector)):
+                stage_slice_half(copy, area, 0, 2, u)
             quantize_x(2, 1)
             project_slice(0, 2, area, accs)
             for acc, nodes, relu in zip(accs, NODE_HALVES, (nc.vector.tensor_relu, relu_on_scalar)):
@@ -238,6 +241,7 @@ def tile_picked_gcn_mlp_relu_sub_l_kernel(
         ratios, factor, columns = spread_ratios()
         h = {0: project_first_group()}
         h_accs, staged = {}, {}
+        last = GROUPS - 1
 
         def stage(c, g, area):
             staged[c, g] = area
@@ -245,20 +249,23 @@ def tile_picked_gcn_mlp_relu_sub_l_kernel(
 
         def project(c, g, scales_tag=None):
             if g == 0:
-                h_accs[c] = [bank({1: 2, 2: 0, 3: 6}[c] + i, [P, HALF], "h_acc") for i in range(2)]
+                h_accs[c] = [bank({1: 4, 2: 0, 3: 2}[c] + i, [P, HALF], "h_acc") for i in range(2)]
             project_slice(c, g, staged[c, g], h_accs[c], scales_tag)
 
-        def finish_h(c):
+        def finish_h(c, first=relu_on_scalar):
             h[c] = keep.tile([P, T], F32, name=f"h{c}")
-            for acc, nodes in zip(h_accs[c], NODE_HALVES):
-                relu_on_scalar(h[c][:, nodes], acc[:])
+            for acc, nodes, relu in zip(h_accs[c], NODE_HALVES, (first, relu_on_scalar)):
+                relu(out=h[c][:, nodes], in_=acc[:])
 
         sums, added, waiting = {}, {}, []
+        TERMS = len(GATED) + 1
 
         def add_half(c, vh, term):
-            k = added.get((c, vh), 0)
-            nc.tensor.matmul(sums[c][vh], term, ident[:], start=(k == 0), stop=(k == D - 1 - (c == GROUPS - 1)), is_transpose=True)
-            added[c, vh] = k + 1
+            key = (c == last, vh)
+            k = added.get(key, 0)
+            total = TERMS if c == last else EARLY * TERMS
+            nc.tensor.matmul(sums[c][vh], term, ident[:], start=(k == 0), stop=(k == total - 1), is_transpose=True)
+            added[key] = k + 1
 
         def add(c, term):
             if c not in sums:
@@ -267,6 +274,13 @@ def tile_picked_gcn_mlp_relu_sub_l_kernel(
             for vh in range(TARGET_HALVES):
                 add_half(c, vh, term[:, block(vh)])
 
+        all_lone = [bank(6 + vh, [P, 2, GROUPS, RUN], "all_lone") for vh in range(TARGET_HALVES)]
+        lone = {c: [t[:, :, c, :] for t in all_lone] for c in range(GROUPS)}
+
+        def turn_lone(c, term):
+            for vh in range(TARGET_HALVES):
+                nc.tensor.transpose(lone[c][vh], term[:, block(vh)], ident[:])
+
         def offsets(d, vh=None):
             return lists[d][:] if vh is None else lists[d][:, vh * LIST_COLUMNS : (vh + 1) * LIST_COLUMNS]
 
@@ -274,13 +288,9 @@ def tile_picked_gcn_mlp_relu_sub_l_kernel(
             nc.scalar.activation(picked, h[c][:].indirect(offsets(d, vh)), COPY)
             return picked
 
-        def fused(term, c, d):
+        def fused(term, c, i):
+            d = GATED[i]
             nc.vector.tensor_tensor(term, h[c][:].indirect(offsets(d)), ratios[d], MULT)
-            add(c, term)
-
-        def multiply(picked, c, d):
-            term = words(f"term{c}_{d}", V)
-            nc.vector.tensor_tensor(term, picked, ratios[d], MULT)
             add(c, term)
 
         def after_staging(c, g, i):
@@ -289,129 +299,112 @@ def tile_picked_gcn_mlp_relu_sub_l_kernel(
         stage(1, 0, x_raw[2][:, 1, NODE_HALVES[1]])
         project(1, 0, "w1_0_2_scales")
         round_a = words("round_a", 4 * PART, "w1_0_2_codes")
-        stage(1, 1, part(round_a, 0))
-        stage(1, 2, part(round_a, 1))
-        stage(2, 0, part(round_a, 2))
-        plain = pick(words("plain0", V), 0, PLAIN_LIST)
-        stage(2, 1, part(round_a, 3))
+        for i, (c, g) in enumerate(((1, 1), (1, 2), (2, 0), (2, 1))):
+            stage(c, g, part(round_a, i))
         fused(words("term0_0", V), 0, 0)
         project(1, 1)
         fused(after_staging(1, 1, 0), 0, 1)
         project(1, 2)
         finish_h(1)
-        add(0, plain)
-        fused(after_staging(1, 2, 0), 0, 3)
+        fused(after_staging(1, 2, 0), 0, 2)
         project(2, 0)
-        fused(after_staging(2, 0, 0), 0, 4)
-        fused(after_staging(2, 0, 1), 0, 5)
+        fused(after_staging(2, 0, 0), 0, 3)
         project(2, 1)
-
-        round_b = words("round_b", 3 * PART, "w1_1_2_codes")
-        stage(2, 2, part(round_b, 0))
-        stage(3, 0, part(round_b, 1))
-        plain = pick(after_staging(2, 1, 1), 1, PLAIN_LIST)
-        picked = pick(after_staging(3, 0, 1), 1, 3)
-        stage(3, 1, part(round_b, 2))
-        fused(after_staging(2, 1, 0), 1, 0)
-        project(2, 2)
-        first_sums = [bank(2 + vh, [P, 2 * P], "first_sums") for vh in range(TARGET_HALVES)]
-        third_sums = [bank(4 + vh, [P, 2 * P], "third_sums") for vh in range(TARGET_HALVES)]
-        sums[0] = [t[:, :P] for t in first_sums]
-        sums[1] = [t[:, P:] for t in first_sums]
-        sums[2] = [t[:, :P] for t in third_sums]
+        early_sums = [bank(4 + vh, [P, 2, EARLY, RUN], "early_sums") for vh in range(TARGET_HALVES)]
+        for c in range(EARLY):
+            sums[c] = [t[:, :, c, :] for t in early_sums]
         for c, term in waiting:
             add(c, term)
+
+        round_b = words("round_b", 3 * PART, "w1_1_2_codes")
+        for i, (c, g) in enumerate(((2, 2), (3, 0), (3, 1))):
+            stage(c, g, part(round_b, i))
+        fused(words("term1_0", V), 1, 0)
+        project(2, 2)
         finish_h(2)
+        alone = pick(after_staging(3, 1, 1), 0, LONE_LIST)
         fused(after_staging(2, 2, 0), 1, 1)
-        fused(after_staging(2, 2, 1), 1, 4)
         project(3, 0)
-        add(1, plain)
-        fused(after_staging(3, 0, 0), 1, 5)
-        multiply(picked, 1, 3)
+        fused(after_staging(3, 0, 0), 1, 2)
         project(3, 1)
+        turn_lone(0, alone)
+        fused(after_staging(3, 1, 0), 1, 3)
 
         round_c = words("round_c", 3 * PART, "w1_2_2_codes")
         stage(3, 2, part(round_c, 0))
-        plain = pick(part(round_c, 1), 2, PLAIN_LIST)
-        picked = pick(part(round_c, 2), 2, 3)
-        fused(after_staging(3, 1, 0), 2, 0)
+        alone = [pick(part(round_c, c), c, LONE_LIST) for c in (1, 2)]
+        fused(words("term2_0", V), 2, 0)
         project(3, 2)
         finish_h(3)
+        turn_lone(1, alone[0])
         fused(after_staging(3, 2, 0), 2, 1)
-        add(2, plain)
-        fused(after_staging(3, 2, 1), 2, 4)
-        multiply(picked, 2, 3)
-        fused(staged[3, 2], 2, 5)
+        turn_lone(2, alone[1])
+        fused(after_staging(3, 2, 1), 2, 2)
+        fused(staged[3, 2], 2, 3)
 
-        def scaled_on_scalar(out, in_, vh):
-            nc.scalar.activation(out, in_, COPY, scale=factor[:, vh : vh + 1])
-
-        def scaled_on_vector(out, in_, vh):
-            nc.vector.tensor_scalar(out, in_, factor[:, vh : vh + 1], None, MULT)
-
-        def round_sums(scaled, vh, acc, first_group, groups):
-            zt = zt_words[vh].bitcast(BF16).rearrange("v (u p e) -> v u p e", u=2, e=2)
-            partitions = slice(GROUP_PARTITIONS * first_group, GROUP_PARTITIONS * (first_group + groups))
-            scaled(zt[:, :, partitions, :], acc.rearrange("v (p u e) -> v u p e", u=2, e=2), vh)
-
-        last = GROUPS - 1
-        last_sums = [bank(vh, [P, P], "last_sums") for vh in range(TARGET_HALVES)]
+        round_d = words("round_d", 4 * PART, "w1_3_2_codes")
+        last_sums = [bank(vh, [P, 2, RUN], "last_sums") for vh in range(TARGET_HALVES)]
         sums[last] = [t[:] for t in last_sums]
-        zt_both = words("zt", TARGET_HALVES * PART, "w1_3_1_scales")
-        zt_words = [part(zt_both, vh) for vh in range(TARGET_HALVES)]
-        for vh in range(TARGET_HALVES):
-            round_sums(scaled_on_scalar, vh, first_sums[vh][:], 0, 2)
-        alone = pick(words("alone", V), last, LONE_LIST)
-        picked_last = words("picked_last", V)
-        pick(picked_last[:, block(0)], last, 4, 0)
-        plain = pick(words("plain3", V), last, PLAIN_LIST)
-        pick(picked_last[:, block(1)], last, 4, 1)
+
+        def scale_on_vector(scaled, acc, vh):
+            nc.vector.tensor_scalar(scaled, acc, columns[:, vh, LONE_LIST : LONE_LIST + 1], None, MULT)
+
+        def scale_on_scalar(scaled, acc, vh):
+            nc.scalar.activation(scaled, acc, COPY, scale=columns[:, vh, LONE_LIST : LONE_LIST + 1])
+
+        def join(out, acc, scaled, vh):
+            nc.vector.scalar_tensor_tensor(out, acc, factor[:, vh : vh + 1], scaled, MULT, ADD)
+
+        scaled = [keep.tile([P, 2, GROUPS, RUN], F32, align_bytes=64, name=f"scaled{vh}", tag=f"scaled{vh}") for vh in range(TARGET_HALVES)]
+
+        def scale_lone(scale, vh):
+            scale(scaled[vh][:].rearrange("v u c r -> v (u c r)"), all_lone[vh][:].rearrange("v u c r -> v (u c r)"), vh)
+
+        turn_lone(last, pick(part(round_d, 0), last, LONE_LIST))
         fused(words("term3_0", V), last, 0)
-        lone = [t[:, P:] for t in third_sums]
-        for vh in range(TARGET_HALVES):
-            nc.tensor.transpose(lone[vh], alone[:, block(vh)], ident[:])
+        add(0, pick(part(round_d, 1), 0, PLAIN_LIST))
         fused(words("term3_1", V), last, 1)
-        scaled = [words(f"scaled{vh}", P) for vh in range(TARGET_HALVES)]
-        w2_areas = []
+        add(1, pick(words("plain1", V, "w1_3_2_scales"), 1, PLAIN_LIST))
+        fused(words("term3_2", V), last, 2)
+        add(2, pick(part(round_d, 3), 2, PLAIN_LIST))
+        fused(words("term3_3", V), last, 3)
+        scale_lone(scale_on_vector, 0)
+        add_half(last, 0, pick(words("first_pick", P), last, PLAIN_LIST, 0))
+        scale_lone(scale_on_scalar, 1)
+        second_pick = words("second_pick", PART, "w1_3_2_scales")
+        add_half(last, 1, pick(second_pick[:, :P], last, PLAIN_LIST, 1))
+        zt = [
+            keep.tile([P, 2, GROUPS, RUN], BF16, align_bytes=64, name=f"zt{vh}", tag=("zt", "first_pick")[vh])
+            for vh in range(TARGET_HALVES)
+        ]
         for vh in range(TARGET_HALVES):
-            scale = columns[:, vh, LONE_LIST : LONE_LIST + 1]
-            nc.scalar.activation(scaled[vh][:, :P], lone[vh], COPY, scale=scale)
-            round_sums(scaled_on_scalar, vh, sums[2][vh], 2, 1)
-        for vh in range(TARGET_HALVES):
-            term = words(f"term3_3_{vh}", P)
-            nc.vector.tensor_tensor(term, h[last][:].indirect(offsets(3, vh)), ratios[3][:, block(vh)], MULT)
-            add_half(last, vh, term)
-            if vh == 0:
-                add(last, plain)
-            w2_areas.append(words(f"term3_4_{vh}", PART))
-            term = w2_areas[vh][:, :P]
-            nc.vector.tensor_tensor(term, picked_last[:, block(vh)], ratios[4][:, block(vh)], MULT)
-            add_half(last, vh, term)
+            join(
+                zt[vh][:, :, :EARLY, :].rearrange("v u c r -> v u (c r)"),
+                early_sums[vh][:].rearrange("v u c r -> v u (c r)"),
+                scaled[vh][:, :, :EARLY, :].rearrange("v u c r -> v u (c r)"),
+                vh,
+            )
+            join(zt[vh][:, :, last, :], sums[last][vh], scaled[vh][:, :, last, :], vh)
 
-        def join(vh):
-            zt = zt_words[vh].bitcast(BF16).rearrange("v (u n) -> v u n", u=2)[:, :, last * RUN :]
-            acc, other = (t.rearrange("v (u n) -> v u n", u=2) for t in (sums[last][vh], scaled[vh][:, :P]))
-            nc.vector.scalar_tensor_tensor(zt, acc, factor[:, vh : vh + 1], other, MULT, ADD)
-
-        join(0)
-        interleave(on_vector, as_grouped(w2_areas[1]), w2_raw[:, :, block(1)])
+        w2_areas = (part(round_d, 3), second_pick)
         w2_codes, w2_scales = operand_tiles("w2", N, "scaled1")
         z_codes, z_scales = operand_tiles("z", V)
-        join(1)
-        interleave(on_scalar, as_grouped(w2_areas[0]), w2_raw[:, :, block(0)])
-        for mb in (1, 0):
+        for mb in range(N // P):
+            interleave(on_scalar, as_grouped(w2_areas[mb]), w2_raw[:, :, block(mb)])
+        for mb in range(N // P):
             quantize(nc, w2_codes[:, block(mb)], w2_scales[:, block(mb)], as_grouped(w2_areas[mb]))
 
-        for vh, (copy, out_bank) in enumerate(((on_scalar, 6), (on_vector, 4))):
-            back = bank(2 + vh, [P, 2, P], "back")
+        for vh, (copy, back_bank, out_banks) in enumerate(((on_scalar, 3, (4, 5)), (on_vector, 6, (7, 2)))):
+            back = bank(back_bank, [P, 2, P], "back")
+            zt_words = zt[vh][:].rearrange("v u c r -> v (u c r)").bitcast(F32)
             for u in range(2):
-                nc.tensor.transpose(back[:, u, :], zt_words[vh][:, block(u)], ident[:])
+                nc.tensor.transpose(back[:, u, :], zt_words[:, block(u)], ident[:])
             z_words = keep.tile([P, P, 2], F32, align_bytes=64, name=f"z_words{vh}")
             on_scalar(out=z_words[:], in_=back[:].rearrange("p u v -> p v u"))
             targets = block(vh)
             quantize(nc, z_codes[:, targets], z_scales[:, targets], as_grouped(z_words[:].rearrange("p v u -> p (v u)")))
             for mb in range(N // P):
-                acc = bank(out_bank + mb, [P, P], "out_acc")
+                acc = bank(out_banks[mb], [P, P], "out_acc")
                 nc.tensor.matmul_mx(
                     out=acc[:],
                     lhsT=w2_codes[:, block(mb)].bitcast(FP8X4),

@@ -14,7 +14,7 @@ U8 = mybir.dt.uint8
 FP8X4 = mybir.dt.float8_e4m3fn_x4
 RELU = mybir.ActivationFunctionType.Relu
 COPY = mybir.ActivationFunctionType.Copy
-MULT, MAX, ADD = mybir.AluOpType.mult, mybir.AluOpType.max, mybir.AluOpType.add
+MULT, MAX = mybir.AluOpType.mult, mybir.AluOpType.max
 
 P = 128
 J = 4
@@ -27,11 +27,12 @@ NODE_HALVES = (slice(0, HALF), slice(HALF, T))
 LIST_COLUMNS = P // 16
 GROUP_PARTITIONS = P // J
 PART = KP // 2
+GATE_PARTITIONS, GATE_TURNS = 4, 3
+CLEARED = P - GATE_PARTITIONS
+GATE_STEP = P * V // 2 - P
+GATE_FIRST = 5 * V
 PLAIN_LIST = 2
-LONE_LIST = 3
-GATED = tuple(d for d in range(D) if d not in (PLAIN_LIST, LONE_LIST))
-EARLY = GROUPS - 1
-RUN = P // 2
+GATED = tuple(d for d in range(D) if d != PLAIN_LIST)
 LEAST_SHARE = 2.0**-24
 LEAST_TOP = 2.0**-102
 
@@ -103,10 +104,10 @@ def tile_picked_gcn_mlp_relu_sub_l_kernel(
             nc.sync.dma_start(t[:], (pos1, pos2, pos3, pos4, pos5, pos6)[d])
             lists.append(t)
 
-        gate_raw = keep.tile([D, V], F32)
-        gate_rows = keep.tile([P, V], F32, align_bytes=64)
-        for rows in (slice(0, 4), slice(4, D)):
-            nc.sync.dma_start(out=gate_raw[rows, :], in_=gate[rows, 0, :])
+        gate_rows = keep.tile([P, GATE_TURNS, P], F32, align_bytes=64)
+        pieces = gate.rearrange("d r v -> (d r v)")[GATE_FIRST : GATE_FIRST + D * TARGET_HALVES * GATE_STEP]
+        pieces = pieces.rearrange("(b a s) -> a b s", a=GATE_PARTITIONS, s=GATE_STEP)
+        nc.sync.dma_start(out=gate_rows[CLEARED:], in_=pieces[:, :, :P])
         load_x(0)
         load_w1(0, 0)
         load_x(1)
@@ -123,22 +124,13 @@ def tile_picked_gcn_mlp_relu_sub_l_kernel(
 
         ident = keep.tile([P, P], F32)
         make_identity(nc, ident[:])
-        for vh in range(TARGET_HALVES):
-            on_scalar(out=gate_rows[:, block(vh)], in_=ident[:])
+        nc.vector.memset(gate_rows[:CLEARED, : GATE_TURNS - 1], 0.0)
+        on_scalar(out=gate_rows[:CLEARED, GATE_TURNS - 1, :], in_=ident[:CLEARED])
 
         x_operands = [operand_tiles(f"x{g}", T) for g in range(PASSES)]
 
         def stage_slice(copy, area, c, g):
-            copy(
-                out=area.bitcast(BF16).rearrange("p (u r e j) -> p r j u e", u=2, e=2, j=J),
-                in_=w1_raw[c, g].rearrange("p (j r u e) -> p r j u e", j=J, u=2, e=2),
-            )
-
-        def stage_slice_half(copy, area, c, g, u):
-            copy(
-                out=area.bitcast(BF16).rearrange("p (u r e j) -> p u r j e", u=2, e=2, j=J)[:, u],
-                in_=w1_raw[c, g].rearrange("p (j r u e) -> p u r j e", j=J, u=2, e=2)[:, u],
-            )
+            interleave(copy, as_grouped(area), w1_raw[c, g].rearrange("p (j c) -> p j c", j=J))
 
         def project_slice(c, g, area, accs, scales_tag=None):
             codes, scales = operand_tiles(f"w1_{c}_{g}", P, None, scales_tag)
@@ -159,13 +151,15 @@ def tile_picked_gcn_mlp_relu_sub_l_kernel(
             nc.scalar.activation(out=out, in_=in_, func=RELU)
 
         def spread_ratios():
-            on_vector(out=gate_rows[:D, :], in_=gate_raw[:])
-            turned = bank(7, [P, TARGET_HALVES, P], "turned")
-            for vh in range(TARGET_HALVES):
-                nc.tensor.transpose(turned[:, vh, :], gate_rows[:, block(vh)], ident[:])
+            turned = bank(7, [P, GATE_TURNS, P], "turned")
+            for b in range(GATE_TURNS):
+                nc.tensor.transpose(turned[:, b, :], gate_rows[:, b, :], ident[:])
             columns = keep.tile([P, TARGET_HALVES, D + 1], F32, align_bytes=64, name="gate_columns")
             nc.gpsimd.memset(columns[:, :, D:], LEAST_TOP)
-            on_vector(out=columns[:, :, :D], in_=turned[:, :, :D])
+            on_vector(
+                out=columns[:, :, :D].rearrange("v h (b e) -> v h b e", e=2),
+                in_=turned[:, :, CLEARED:].rearrange("v b (e h) -> v h b e", h=TARGET_HALVES),
+            )
             own = columns[:, :, PLAIN_LIST]
             steps = keep.tile([P, 4, TARGET_HALVES], F32, name="factor_steps")
             top, size, half_sign, guarded = (steps[:, i, :] for i in range(4))
@@ -185,7 +179,7 @@ def tile_picked_gcn_mlp_relu_sub_l_kernel(
                 divided[:], signed[:], 2.0, inverse[:].unsqueeze(2).to_broadcast(along_lists), MULT, MULT
             )
             spread = words("ratios", len(GATED) * V)
-            for first, b in ((0, 0), (2, 1)):
+            for first, b in ((0, 2), (2, 0), (4, 1)):
                 in_bank = GATED[first : first + 2]
                 acc = bank(b, [P, len(in_bank) * V], "spread")
                 for i, d in enumerate(in_bank):
@@ -193,7 +187,7 @@ def tile_picked_gcn_mlp_relu_sub_l_kernel(
                         column = divided[:, vh, d : d + 1].to_broadcast([P, P])
                         nc.tensor.transpose(acc[:, block(i * TARGET_HALVES + vh)], column, ident[:])
                 on_vector(out=part(spread, first, len(in_bank)), in_=acc[:])
-            return {d: part(spread, i) for i, d in enumerate(GATED)}, factor, columns
+            return {d: part(spread, i) for i, d in enumerate(GATED)}, factor
 
         def project_first_group():
             width = 2 * HALF
@@ -230,18 +224,18 @@ def tile_picked_gcn_mlp_relu_sub_l_kernel(
             quantize_x(2, 0)
             project_slice(0, 1, area, accs)
             area = last_loads[:, J * T - P : J * T + P]
-            for u, copy in enumerate((on_scalar, on_vector)):
-                stage_slice_half(copy, area, 0, 2, u)
+            raw = w1_raw[0, 2].rearrange("p (j c) -> p j c", j=J)
+            for copy, columns in ((on_scalar, slice(0, P // 2)), (on_vector, slice(P // 2, P))):
+                interleave(copy, as_grouped(area)[:, columns, :], raw[:, :, columns])
             quantize_x(2, 1)
             project_slice(0, 2, area, accs)
             for acc, nodes, relu in zip(accs, NODE_HALVES, (nc.vector.tensor_relu, relu_on_scalar)):
                 relu(out=h[:, nodes], in_=acc[:])
             return h
 
-        ratios, factor, columns = spread_ratios()
+        ratios, factor = spread_ratios()
         h = {0: project_first_group()}
         h_accs, staged = {}, {}
-        last = GROUPS - 1
 
         def stage(c, g, area):
             staged[c, g] = area
@@ -249,23 +243,20 @@ def tile_picked_gcn_mlp_relu_sub_l_kernel(
 
         def project(c, g, scales_tag=None):
             if g == 0:
-                h_accs[c] = [bank({1: 4, 2: 0, 3: 2}[c] + i, [P, HALF], "h_acc") for i in range(2)]
+                h_accs[c] = [bank({1: 2, 2: 0, 3: 6}[c] + i, [P, HALF], "h_acc") for i in range(2)]
             project_slice(c, g, staged[c, g], h_accs[c], scales_tag)
 
-        def finish_h(c, first=relu_on_scalar):
+        def finish_h(c):
             h[c] = keep.tile([P, T], F32, name=f"h{c}")
-            for acc, nodes, relu in zip(h_accs[c], NODE_HALVES, (first, relu_on_scalar)):
-                relu(out=h[c][:, nodes], in_=acc[:])
+            for acc, nodes in zip(h_accs[c], NODE_HALVES):
+                relu_on_scalar(h[c][:, nodes], acc[:])
 
         sums, added, waiting = {}, {}, []
-        TERMS = len(GATED) + 1
 
         def add_half(c, vh, term):
-            key = (c == last, vh)
-            k = added.get(key, 0)
-            total = TERMS if c == last else EARLY * TERMS
-            nc.tensor.matmul(sums[c][vh], term, ident[:], start=(k == 0), stop=(k == total - 1), is_transpose=True)
-            added[key] = k + 1
+            k = added.get((c, vh), 0)
+            nc.tensor.matmul(sums[c][vh], term, ident[:], start=(k == 0), stop=(k == D - 1), is_transpose=True)
+            added[c, vh] = k + 1
 
         def add(c, term):
             if c not in sums:
@@ -274,13 +265,6 @@ def tile_picked_gcn_mlp_relu_sub_l_kernel(
             for vh in range(TARGET_HALVES):
                 add_half(c, vh, term[:, block(vh)])
 
-        all_lone = [bank(6 + vh, [P, 2, GROUPS, RUN], "all_lone") for vh in range(TARGET_HALVES)]
-        lone = {c: [t[:, :, c, :] for t in all_lone] for c in range(GROUPS)}
-
-        def turn_lone(c, term):
-            for vh in range(TARGET_HALVES):
-                nc.tensor.transpose(lone[c][vh], term[:, block(vh)], ident[:])
-
         def offsets(d, vh=None):
             return lists[d][:] if vh is None else lists[d][:, vh * LIST_COLUMNS : (vh + 1) * LIST_COLUMNS]
 
@@ -288,9 +272,13 @@ def tile_picked_gcn_mlp_relu_sub_l_kernel(
             nc.scalar.activation(picked, h[c][:].indirect(offsets(d, vh)), COPY)
             return picked
 
-        def fused(term, c, i):
-            d = GATED[i]
+        def fused(term, c, d):
             nc.vector.tensor_tensor(term, h[c][:].indirect(offsets(d)), ratios[d], MULT)
+            add(c, term)
+
+        def multiply(picked, c, d):
+            term = words(f"term{c}_{d}", V)
+            nc.vector.tensor_tensor(term, picked, ratios[d], MULT)
             add(c, term)
 
         def after_staging(c, g, i):
@@ -299,112 +287,119 @@ def tile_picked_gcn_mlp_relu_sub_l_kernel(
         stage(1, 0, x_raw[2][:, 1, NODE_HALVES[1]])
         project(1, 0, "w1_0_2_scales")
         round_a = words("round_a", 4 * PART, "w1_0_2_codes")
-        for i, (c, g) in enumerate(((1, 1), (1, 2), (2, 0), (2, 1))):
-            stage(c, g, part(round_a, i))
+        stage(1, 1, part(round_a, 0))
+        stage(1, 2, part(round_a, 1))
+        stage(2, 0, part(round_a, 2))
+        plain = pick(words("plain0", V), 0, PLAIN_LIST)
+        stage(2, 1, part(round_a, 3))
         fused(words("term0_0", V), 0, 0)
         project(1, 1)
         fused(after_staging(1, 1, 0), 0, 1)
         project(1, 2)
         finish_h(1)
-        fused(after_staging(1, 2, 0), 0, 2)
+        add(0, plain)
+        fused(after_staging(1, 2, 0), 0, 3)
         project(2, 0)
-        fused(after_staging(2, 0, 0), 0, 3)
+        fused(after_staging(2, 0, 0), 0, 4)
+        fused(after_staging(2, 0, 1), 0, 5)
         project(2, 1)
-        early_sums = [bank(4 + vh, [P, 2, EARLY, RUN], "early_sums") for vh in range(TARGET_HALVES)]
-        for c in range(EARLY):
-            sums[c] = [t[:, :, c, :] for t in early_sums]
-        for c, term in waiting:
-            add(c, term)
 
         round_b = words("round_b", 3 * PART, "w1_1_2_codes")
-        for i, (c, g) in enumerate(((2, 2), (3, 0), (3, 1))):
-            stage(c, g, part(round_b, i))
-        fused(words("term1_0", V), 1, 0)
+        stage(2, 2, part(round_b, 0))
+        stage(3, 0, part(round_b, 1))
+        plain = pick(after_staging(2, 1, 1), 1, PLAIN_LIST)
+        picked = pick(after_staging(3, 0, 1), 1, 3)
+        stage(3, 1, part(round_b, 2))
+        fused(after_staging(2, 1, 0), 1, 0)
         project(2, 2)
+        first_sums = [bank(2 + vh, [P, 2 * P], "first_sums") for vh in range(TARGET_HALVES)]
+        third_sums = [bank(4 + vh, [P, P], "third_sums") for vh in range(TARGET_HALVES)]
+        sums[0] = [t[:, :P] for t in first_sums]
+        sums[1] = [t[:, P:] for t in first_sums]
+        sums[2] = [t[:] for t in third_sums]
+        for c, term in waiting:
+            add(c, term)
         finish_h(2)
-        alone = pick(after_staging(3, 1, 1), 0, LONE_LIST)
         fused(after_staging(2, 2, 0), 1, 1)
+        fused(after_staging(2, 2, 1), 1, 4)
         project(3, 0)
-        fused(after_staging(3, 0, 0), 1, 2)
+        add(1, plain)
+        fused(after_staging(3, 0, 0), 1, 5)
+        multiply(picked, 1, 3)
         project(3, 1)
-        turn_lone(0, alone)
-        fused(after_staging(3, 1, 0), 1, 3)
 
         round_c = words("round_c", 3 * PART, "w1_2_2_codes")
         stage(3, 2, part(round_c, 0))
-        alone = [pick(part(round_c, c), c, LONE_LIST) for c in (1, 2)]
-        fused(words("term2_0", V), 2, 0)
+        plain = pick(part(round_c, 1), 2, PLAIN_LIST)
+        picked = pick(part(round_c, 2), 2, 3)
+        fused(after_staging(3, 1, 0), 2, 0)
         project(3, 2)
         finish_h(3)
-        turn_lone(1, alone[0])
         fused(after_staging(3, 2, 0), 2, 1)
-        turn_lone(2, alone[1])
-        fused(after_staging(3, 2, 1), 2, 2)
-        fused(staged[3, 2], 2, 3)
+        add(2, plain)
+        fused(after_staging(3, 2, 1), 2, 4)
+        multiply(picked, 2, 3)
+        fused(staged[3, 2], 2, 5)
 
-        round_d = words("round_d", 4 * PART, "w1_3_2_codes")
-        last_sums = [bank(vh, [P, 2, RUN], "last_sums") for vh in range(TARGET_HALVES)]
+        def scaled_on_scalar(out, in_, vh):
+            nc.scalar.activation(out, in_, COPY, scale=factor[:, vh : vh + 1])
+
+        def scaled_on_vector(out, in_, vh):
+            nc.vector.tensor_scalar(out, in_, factor[:, vh : vh + 1], None, MULT)
+
+        def round_sums(scaled, vh, acc, first_group, groups):
+            zt = zt_words[vh].bitcast(BF16).rearrange("v (u p e) -> v u p e", u=2, e=2)
+            partitions = slice(GROUP_PARTITIONS * first_group, GROUP_PARTITIONS * (first_group + groups))
+            scaled(zt[:, :, partitions, :], acc.rearrange("v (p u e) -> v u p e", u=2, e=2), vh)
+
+        last = GROUPS - 1
+        last_sums = [bank(vh, [P, P], "last_sums") for vh in range(TARGET_HALVES)]
         sums[last] = [t[:] for t in last_sums]
-
-        def scale_on_vector(scaled, acc, vh):
-            nc.vector.tensor_scalar(scaled, acc, columns[:, vh, LONE_LIST : LONE_LIST + 1], None, MULT)
-
-        def scale_on_scalar(scaled, acc, vh):
-            nc.scalar.activation(scaled, acc, COPY, scale=columns[:, vh, LONE_LIST : LONE_LIST + 1])
-
-        def join(out, acc, scaled, vh):
-            nc.vector.scalar_tensor_tensor(out, acc, factor[:, vh : vh + 1], scaled, MULT, ADD)
-
-        scaled = [keep.tile([P, 2, GROUPS, RUN], F32, align_bytes=64, name=f"scaled{vh}", tag=f"scaled{vh}") for vh in range(TARGET_HALVES)]
-
-        def scale_lone(scale, vh):
-            scale(scaled[vh][:].rearrange("v u c r -> v (u c r)"), all_lone[vh][:].rearrange("v u c r -> v (u c r)"), vh)
-
-        turn_lone(last, pick(part(round_d, 0), last, LONE_LIST))
-        fused(words("term3_0", V), last, 0)
-        add(0, pick(part(round_d, 1), 0, PLAIN_LIST))
-        fused(words("term3_1", V), last, 1)
-        add(1, pick(words("plain1", V, "w1_3_2_scales"), 1, PLAIN_LIST))
-        fused(words("term3_2", V), last, 2)
-        add(2, pick(part(round_d, 3), 2, PLAIN_LIST))
-        fused(words("term3_3", V), last, 3)
-        scale_lone(scale_on_vector, 0)
-        add_half(last, 0, pick(words("first_pick", P), last, PLAIN_LIST, 0))
-        scale_lone(scale_on_scalar, 1)
-        second_pick = words("second_pick", PART, "w1_3_2_scales")
-        add_half(last, 1, pick(second_pick[:, :P], last, PLAIN_LIST, 1))
-        zt = [
-            keep.tile([P, 2, GROUPS, RUN], BF16, align_bytes=64, name=f"zt{vh}", tag=("zt", "first_pick")[vh])
-            for vh in range(TARGET_HALVES)
-        ]
+        plain = pick(words("plain3", V), last, PLAIN_LIST)
+        zt_both = words("zt", TARGET_HALVES * PART, "w1_3_1_scales")
+        zt_words = [part(zt_both, vh) for vh in range(TARGET_HALVES)]
         for vh in range(TARGET_HALVES):
-            join(
-                zt[vh][:, :, :EARLY, :].rearrange("v u c r -> v u (c r)"),
-                early_sums[vh][:].rearrange("v u c r -> v u (c r)"),
-                scaled[vh][:, :, :EARLY, :].rearrange("v u c r -> v u (c r)"),
-                vh,
-            )
-            join(zt[vh][:, :, last, :], sums[last][vh], scaled[vh][:, :, last, :], vh)
+            round_sums(scaled_on_scalar, vh, first_sums[vh][:], 0, 2)
+        picked_last = words("picked_last", TARGET_HALVES * PART)
+        for vh in range(TARGET_HALVES):
+            for i, d in enumerate((4, 5)):
+                pick(part(picked_last, vh)[:, block(i)], last, d, vh)
+        for vh in range(TARGET_HALVES):
+            round_sums(scaled_on_scalar, vh, third_sums[vh][:], 2, 1)
+        fused(words("term3_0", V), last, 0)
+        add(last, plain)
+        fused(words("term3_1", V), last, 1)
+        last_terms = []
+        for vh in range(TARGET_HALVES):
+            term = words(f"term3_3_{vh}", P)
+            nc.vector.tensor_tensor(term, h[last][:].indirect(offsets(3, vh)), ratios[3][:, block(vh)], MULT)
+            add_half(last, vh, term)
+            last_terms.append(words(f"term3_45_{vh}", PART))
+            for i, d in enumerate((4, 5)):
+                term = last_terms[vh][:, block(i)]
+                nc.vector.tensor_tensor(term, part(picked_last, vh)[:, block(i)], ratios[d][:, block(vh)], MULT)
+                add_half(last, vh, term)
 
-        w2_areas = (part(round_d, 3), second_pick)
-        w2_codes, w2_scales = operand_tiles("w2", N, "scaled1")
+        w2_areas = (last_terms[0], part(picked_last, 1))
+        interleave(on_vector, as_grouped(w2_areas[1]), w2_raw[:, :, block(1)])
+        w2_codes, w2_scales = operand_tiles("w2", N, "term3_45_1")
         z_codes, z_scales = operand_tiles("z", V)
-        for mb in range(N // P):
-            interleave(on_scalar, as_grouped(w2_areas[mb]), w2_raw[:, :, block(mb)])
-        for mb in range(N // P):
+        for vh, scaled in enumerate((scaled_on_scalar, scaled_on_vector)):
+            round_sums(scaled, vh, sums[last][vh], last, 1)
+        interleave(on_scalar, as_grouped(w2_areas[0]), w2_raw[:, :, block(0)])
+        for mb in (1, 0):
             quantize(nc, w2_codes[:, block(mb)], w2_scales[:, block(mb)], as_grouped(w2_areas[mb]))
 
-        for vh, (copy, back_bank, out_banks) in enumerate(((on_scalar, 3, (4, 5)), (on_vector, 6, (7, 2)))):
-            back = bank(back_bank, [P, 2, P], "back")
-            zt_words = zt[vh][:].rearrange("v u c r -> v (u c r)").bitcast(F32)
+        for vh, (copy, out_bank) in enumerate(((on_scalar, 6), (on_vector, 4))):
+            back = bank(2 + vh, [P, 2, P], "back")
             for u in range(2):
-                nc.tensor.transpose(back[:, u, :], zt_words[:, block(u)], ident[:])
+                nc.tensor.transpose(back[:, u, :], zt_words[vh][:, block(u)], ident[:])
             z_words = keep.tile([P, P, 2], F32, align_bytes=64, name=f"z_words{vh}")
             on_scalar(out=z_words[:], in_=back[:].rearrange("p u v -> p v u"))
             targets = block(vh)
             quantize(nc, z_codes[:, targets], z_scales[:, targets], as_grouped(z_words[:].rearrange("p v u -> p (v u)")))
             for mb in range(N // P):
-                acc = bank(out_banks[mb], [P, P], "out_acc")
+                acc = bank(out_bank + mb, [P, P], "out_acc")
                 nc.tensor.matmul_mx(
                     out=acc[:],
                     lhsT=w2_codes[:, block(mb)].bitcast(FP8X4),

@@ -82,7 +82,7 @@ def tile_picked_gcn_mlp_relu_sub_l_kernel(
             scales = keep.tile([P, width], U8, align_bytes=64, name=f"{name}_scales", tag=scales_tag or f"{name}_scales")
             return codes, scales
 
-        x_raw, w1_raw, lists = {}, {}, []
+        x_raw, w1_raw, lists = {}, {}, {}
         spare_and_loads = words("last_loads", P + J * T + KP)
         last_loads = spare_and_loads[:, P:]
 
@@ -102,7 +102,7 @@ def tile_picked_gcn_mlp_relu_sub_l_kernel(
         def load_list(d):
             t = keep.tile([P, V // 16], U16, name=f"list{d}")
             nc.sync.dma_start(t[:], (pos1, pos2, pos3, pos4, pos5, pos6)[d])
-            lists.append(t)
+            lists[d] = t
 
         gate_rows = keep.tile([P, GATE_TURNS, P], F32, align_bytes=64)
         pieces = gate.rearrange("d r v -> (d r v)")[GATE_FIRST : GATE_FIRST + D * TARGET_HALVES * GATE_STEP]
@@ -114,20 +114,20 @@ def tile_picked_gcn_mlp_relu_sub_l_kernel(
         load_x(2)
         load_w1(0, 1)
         load_w1(0, 2)
-        for d in range(D):
-            load_list(d)
-            load_w1(1 + d // PASSES, d % PASSES)
-        for g in range(PASSES):
-            load_w1(GROUPS - 1, g)
+        later = [(c, g) for c in range(1, GROUPS) for g in range(PASSES)]
+        behind = {0: (0,), 1: (1,), 2: (3,), 3: (PLAIN_LIST, 4), 4: (5,)}
+        for i, (c, g) in enumerate(later):
+            load_w1(c, g)
+            for d in behind.get(i, ()):
+                load_list(d)
         w2_raw = keep.tile([P, J, N], F32)
         nc.sync.dma_start(out=w2_raw[:], in_=w2.rearrange("(p j) m -> p j m", j=J))
 
         ident = keep.tile([P, P], F32)
         make_identity(nc, ident[:])
-        nc.vector.memset(gate_rows[:CLEARED, : GATE_TURNS - 1], 0.0)
-        on_scalar(out=gate_rows[:CLEARED, GATE_TURNS - 1, :], in_=ident[:CLEARED])
+        nc.vector.memset(gate_rows[:CLEARED], 0.0)
 
-        x_operands = [operand_tiles(f"x{g}", T) for g in range(PASSES)]
+        x_operands = {}
 
         def stage_slice(copy, area, c, g):
             interleave(copy, as_grouped(area), w1_raw[c, g].rearrange("p (j c) -> p j c", j=J))
@@ -170,7 +170,7 @@ def tile_picked_gcn_mlp_relu_sub_l_kernel(
             along_lists = [P, TARGET_HALVES, D]
             signed = keep.tile(along_lists, F32, align_bytes=64, name="signed", tag="after_division")
             nc.vector.tensor_tensor(signed[:], columns[:, :, :D], half_sign.unsqueeze(2).to_broadcast(along_lists), MULT)
-            inverse = keep.tile([P, TARGET_HALVES], F32, name="inverse")
+            inverse = keep.tile([P, TARGET_HALVES], F32, align_bytes=64, name="inverse", tag="after_inverse")
             nc.vector.reciprocal(inverse[:], guarded)
             factor = keep.tile([P, TARGET_HALVES], F32, name="factor")
             nc.vector.scalar_tensor_tensor(factor[:], half_sign, 2.0, guarded, MULT, MULT)
@@ -179,23 +179,26 @@ def tile_picked_gcn_mlp_relu_sub_l_kernel(
                 divided[:], signed[:], 2.0, inverse[:].unsqueeze(2).to_broadcast(along_lists), MULT, MULT
             )
             spread = words("ratios", len(GATED) * V)
-            for first, b in ((0, 2), (2, 0), (4, 1)):
+            for first, b, copy in ((0, 2, on_scalar), (2, 3, on_scalar), (4, 4, on_vector)):
                 in_bank = GATED[first : first + 2]
                 acc = bank(b, [P, len(in_bank) * V], "spread")
                 for i, d in enumerate(in_bank):
                     for vh in range(TARGET_HALVES):
                         column = divided[:, vh, d : d + 1].to_broadcast([P, P])
                         nc.tensor.transpose(acc[:, block(i * TARGET_HALVES + vh)], column, ident[:])
-                on_vector(out=part(spread, first, len(in_bank)), in_=acc[:])
+                copy(out=part(spread, first, len(in_bank)), in_=acc[:])
             return {d: part(spread, i) for i, d in enumerate(GATED)}, factor
 
         def project_first_group():
             width = 2 * HALF
-            first = words("x_stage_first", 2 * width, "after_division")
+            first = words("x_stage_first", width, "after_division")
+            free = words("x_stage_free", width)
             second = words("x_stage_second", width, "after_spreading")
             behind_pass_1 = x_raw[1].rearrange("p j t -> p (j t)")
             third, fourth = (behind_pass_1[:, i * width : (i + 1) * width] for i in (1, 2))
-            areas = ((first[:, :width], first[:, width:]), (first[:, :width], second), (third, fourth))
+            areas = ((first, free), (first, second), (third, fourth))
+            for g in range(PASSES):
+                x_operands[g] = operand_tiles(f"x{g}", T, None, "after_inverse" if g == 0 else None)
             h = keep.tile([P, T], F32, name="h0")
             accs = [bank(b, [P, HALF], "h_acc") for b in range(2)]
 
@@ -213,8 +216,8 @@ def tile_picked_gcn_mlp_relu_sub_l_kernel(
                 quantize_x(g, 0)
                 quantize_x(g, 1)
                 if g == 0:
-                    area = x_raw[0][:, 0, NODE_HALVES[1]]
-                    stage_slice(on_scalar, area, 0, 0)
+                    area = x_raw[0][:, 0, NODE_HALVES[0]]
+                    stage_slice(on_vector, area, 0, 0)
                     project_slice(0, 0, area, accs)
             interleave(on_vector, as_grouped(third)[:, :P, :], x_raw[2][:, :, :P])
             interleave(on_scalar, as_grouped(fourth), x_raw[2][:, :, HALF:])

@@ -24,6 +24,8 @@ GROUPS = H // P
 TARGET_HALVES = V // P
 HALF = T // 2
 NODE_HALVES = (slice(0, HALF), slice(HALF, T))
+FIRST_PARTS = (slice(0, HALF), slice(HALF, HALF + P), slice(HALF + P, T))
+SCALAR_COLUMNS = 32
 LIST_COLUMNS = P // 16
 GROUP_PARTITIONS = P // J
 PART = KP // 2
@@ -132,11 +134,13 @@ def tile_picked_gcn_mlp_relu_sub_l_kernel(
         def stage_slice(copy, area, c, g):
             interleave(copy, as_grouped(area), w1_raw[c, g].rearrange("p (j c) -> p j c", j=J))
 
-        def project_slice(c, g, area, accs, scales_tag=None):
+        def project_slice(c, g, area, accs, scales_tag=None, between=None):
             codes, scales = operand_tiles(f"w1_{c}_{g}", P, None, scales_tag)
             quantize(nc, codes[:], scales[:], as_grouped(area))
+            if between:
+                between()
             x_codes, x_scales = x_operands[g]
-            for acc, nodes in zip(accs, NODE_HALVES):
+            for acc, nodes in zip(accs, FIRST_PARTS if c == 0 else NODE_HALVES):
                 nc.tensor.matmul_mx(
                     out=acc[:],
                     lhsT=codes[:].bitcast(FP8X4),
@@ -200,7 +204,7 @@ def tile_picked_gcn_mlp_relu_sub_l_kernel(
             for g in range(PASSES):
                 x_operands[g] = operand_tiles(f"x{g}", T, None, "after_inverse" if g == 0 else None)
             h = keep.tile([P, T], F32, name="h0")
-            accs = [bank(b, [P, HALF], "h_acc") for b in range(2)]
+            accs = [bank(b, [P, n.stop - n.start], "h_acc") for b, n in zip((0, 1, 5), FIRST_PARTS)]
 
             def stage_x(g):
                 for area, nodes, copy in zip(areas[g], NODE_HALVES, (on_vector, on_scalar)):
@@ -226,13 +230,15 @@ def tile_picked_gcn_mlp_relu_sub_l_kernel(
             stage_slice(on_vector, area, 0, 1)
             quantize_x(2, 0)
             project_slice(0, 1, area, accs)
-            area = last_loads[:, J * T - P : J * T + P]
+            area = last_loads[:, J * T - 2 * SCALAR_COLUMNS : J * T - 2 * SCALAR_COLUMNS + PART]
             raw = w1_raw[0, 2].rearrange("p (j c) -> p j c", j=J)
-            for copy, columns in ((on_scalar, slice(0, P // 2)), (on_vector, slice(P // 2, P))):
+            for copy, columns in ((on_scalar, slice(0, SCALAR_COLUMNS)), (on_vector, slice(SCALAR_COLUMNS, P))):
                 interleave(copy, as_grouped(area)[:, columns, :], raw[:, :, columns])
-            quantize_x(2, 1)
-            project_slice(0, 2, area, accs)
-            for acc, nodes, relu in zip(accs, NODE_HALVES, (nc.vector.tensor_relu, relu_on_scalar)):
+            x_codes, x_scales = x_operands[2]
+            second_part, last_part = FIRST_PARTS[1:]
+            quantize(nc, x_codes[:, second_part], x_scales[:, second_part], as_grouped(part(fourth, 0)))
+            project_slice(0, 2, area, accs, None, lambda: quantize(nc, x_codes[:, last_part], x_scales[:, last_part], as_grouped(part(fourth, 1))))
+            for acc, nodes, relu in zip(accs, FIRST_PARTS, (nc.vector.tensor_relu, relu_on_scalar, relu_on_scalar)):
                 relu(out=h[:, nodes], in_=acc[:])
             return h
 
@@ -350,10 +356,10 @@ def tile_picked_gcn_mlp_relu_sub_l_kernel(
         def scaled_on_vector(out, in_, vh):
             nc.vector.tensor_scalar(out, in_, factor[:, vh : vh + 1], None, MULT)
 
-        def round_sums(scaled, vh, acc, first_group, groups):
+        def round_sums(scaled, vh, acc, first_group, groups, us=slice(0, 2)):
             zt = zt_words[vh].bitcast(BF16).rearrange("v (u p e) -> v u p e", u=2, e=2)
             partitions = slice(GROUP_PARTITIONS * first_group, GROUP_PARTITIONS * (first_group + groups))
-            scaled(zt[:, :, partitions, :], acc.rearrange("v (p u e) -> v u p e", u=2, e=2), vh)
+            scaled(zt[:, us, partitions, :], acc.rearrange("v (p u e) -> v u p e", u=2, e=2)[:, us], vh)
 
         last = GROUPS - 1
         last_sums = [bank(vh, [P, P], "last_sums") for vh in range(TARGET_HALVES)]
@@ -387,8 +393,9 @@ def tile_picked_gcn_mlp_relu_sub_l_kernel(
         interleave(on_vector, as_grouped(w2_areas[1]), w2_raw[:, :, block(1)])
         w2_codes, w2_scales = operand_tiles("w2", N, "term3_45_1")
         z_codes, z_scales = operand_tiles("z", V)
-        for vh, scaled in enumerate((scaled_on_scalar, scaled_on_vector)):
-            round_sums(scaled, vh, sums[last][vh], last, 1)
+        round_sums(scaled_on_scalar, 0, sums[last][0], last, 1)
+        for u in range(2):
+            round_sums(scaled_on_vector, 1, sums[last][1], last, 1, slice(u, u + 1))
         interleave(on_scalar, as_grouped(w2_areas[0]), w2_raw[:, :, block(0)])
         for mb in (1, 0):
             quantize(nc, w2_codes[:, block(mb)], w2_scales[:, block(mb)], as_grouped(w2_areas[mb]))

from contextlib import ExitStack

import concourse.mybir as mybir
from concourse.masks import make_identity

K, T, D, V, H, N = 1536, 512, 6, 256, 512, 256
FLOPS = 2 * K * H * T + 2 * H * N * V

F32 = mybir.dt.float32
BF16 = mybir.dt.bfloat16
U32 = mybir.dt.uint32
U16 = mybir.dt.uint16
U8 = mybir.dt.uint8
FP8X4 = mybir.dt.float8_e4m3fn_x4
RELU = mybir.ActivationFunctionType.Relu
COPY = mybir.ActivationFunctionType.Copy
MULT, MAX = mybir.AluOpType.mult, mybir.AluOpType.max

P = 128
J = 4
KP = P * J
PASSES = K // KP
GROUPS = H // P
TARGET_HALVES = V // P
HALF = T // 2
NODE_HALVES = (slice(0, HALF), slice(HALF, T))
FIRST_PARTS = (slice(0, HALF), slice(HALF, HALF + P), slice(HALF + P, T))
SCALAR_COLUMNS = 32
LIST_COLUMNS = P // 16
GROUP_PARTITIONS = P // J
PART = KP // 2
GATE_PARTITIONS, GATE_TURNS = 4, 3
CLEARED = P - GATE_PARTITIONS
GATE_STEP = P * V // 2 - P
GATE_FIRST = 5 * V
PLAIN_LIST = 2
GATED = tuple(d for d in range(D) if d != PLAIN_LIST)
LEAST_SHARE = 2.0**-24
LEAST_TOP = 2.0**-102


def interleave(copy, grouped, raw):
    copy(
        out=grouped.rearrange("p (c i) j -> p c j i", i=4),
        in_=raw.rearrange("p j (c i) -> p c j i", i=4),
    )


def quantize(nc, codes, scales, grouped):
    nc.vector.quantize_mx(out=codes.bitcast(FP8X4), scales=scales, in_=grouped.rearrange("p c j -> p (c j)"))


def as_grouped(area):
    return area.bitcast(BF16).rearrange("p (c j) -> p c j", j=J)


def part(area, i, n=1):
    return area[:, i * PART : (i + n) * PART]


def block(i):
    return slice(i * P, (i + 1) * P)


def tile_picked_gcn_mlp_relu_sub_l_kernel(
    tc, xT, w1, w2, gate, pos1, pos2, pos3, pos4, pos5, pos6, out
):
    nc = tc.nc
    with ExitStack() as ctx:
        keep = ctx.enter_context(tc.tile_pool(name="keep", bufs=1))
        psum = ctx.enter_context(tc.psum_pool(name="psum", bufs=1))
        on_scalar, on_vector = nc.scalar.copy, nc.vector.tensor_copy

        def bank(b, shape, name):
            t = psum.tile(shape, F32, name=name, tag=f"bank{b}")
            return t

        def words(name, width, tag=None):
            t = keep.tile([P, width], F32, align_bytes=64, name=name, tag=tag or name)
            return t[:]

        def operand_tiles(name, width, codes_tag=None, scales_tag=None):
            codes = keep.tile([P, width], U32, align_bytes=64, name=f"{name}_codes", tag=codes_tag or f"{name}_codes")
            scales = keep.tile([P, width], U8, align_bytes=64, name=f"{name}_scales", tag=scales_tag or f"{name}_scales")
            return codes, scales

        x_raw, w1_raw, lists = {}, {}, {}
        spare_and_loads = words("last_loads", P + J * T + KP)
        last_loads = spare_and_loads[:, P:]

        def load_x(g):
            t = last_loads[:, : J * T] if g == PASSES - 1 else words(f"x_raw{g}", J * T)
            t = t.rearrange("p (j t) -> p j t", j=J)
            nc.sync.dma_start(out=t, in_=xT[g * KP : (g + 1) * KP, :].rearrange("(p j) t -> p j t", j=J))
            x_raw[g] = t

        def load_w1(c, g):
            w1_raw[c, g] = last_loads[:, J * T :] if (c, g) == (0, 1) else words(f"w1_raw{c}_{g}", KP)
            rows = w1[g * KP : (g + 1) * KP, block(c)]
            nc.sync.dma_start(
                out=w1_raw[c, g].rearrange("p (j c) -> p j c", j=J), in_=rows.rearrange("(p j) c -> p j c", j=J)
            )

        def load_list(d):
            t = keep.tile([P, V // 16], U16, name=f"list{d}")
            nc.sync.dma_start(t[:], (pos1, pos2, pos3, pos4, pos5, pos6)[d])
            lists[d] = t

        gate_rows = keep.tile([P, GATE_TURNS, P], F32, align_bytes=64)
        pieces = gate.rearrange("d r v -> (d r v)")[GATE_FIRST : GATE_FIRST + D * TARGET_HALVES * GATE_STEP]
        pieces = pieces.rearrange("(b a s) -> a b s", a=GATE_PARTITIONS, s=GATE_STEP)
        nc.sync.dma_start(out=gate_rows[CLEARED:], in_=pieces[:, :, :P])
        load_x(0)
        load_w1(0, 0)
        load_x(1)
        load_x(2)
        load_w1(0, 1)
        load_w1(0, 2)
        later = [(c, g) for c in range(1, GROUPS) for g in range(PASSES)]
        behind = {0: (0,), 1: (1,), 2: (3,), 3: (PLAIN_LIST, 4), 4: (5,)}
        for i, (c, g) in enumerate(later):
            load_w1(c, g)
            for d in behind.get(i, ()):
                load_list(d)
        w2_raw = keep.tile([P, J, N], F32)
        nc.sync.dma_start(out=w2_raw[:], in_=w2.rearrange("(p j) m -> p j m", j=J))

        ident = keep.tile([P, P], F32)
        make_identity(nc, ident[:])
        nc.vector.memset(gate_rows[:CLEARED], 0.0)

        x_operands = {}

        def stage_slice(copy, area, c, g):
            interleave(copy, as_grouped(area), w1_raw[c, g].rearrange("p (j c) -> p j c", j=J))

        def project_slice(c, g, area, accs, scales_tag=None, between=None):
            codes, scales = operand_tiles(f"w1_{c}_{g}", P, None, scales_tag)
            quantize(nc, codes[:], scales[:], as_grouped(area))
            if between:
                between()
            x_codes, x_scales = x_operands[g]
            for acc, nodes in zip(accs, FIRST_PARTS if c == 0 else NODE_HALVES):
                nc.tensor.matmul_mx(
                    out=acc[:],
                    lhsT=codes[:].bitcast(FP8X4),
                    lhsT_scale=scales[:],
                    rhs=x_codes[:, nodes].bitcast(FP8X4),
                    rhs_scale=x_scales[:, nodes],
                    start=(g == 0),
                    stop=(g == PASSES - 1),
                )

        def relu_on_scalar(out, in_):
            nc.scalar.activation(out=out, in_=in_, func=RELU)

        def spread_ratios():
            turned = bank(7, [P, GATE_TURNS, P], "turned")
            for b in range(GATE_TURNS):
                nc.tensor.transpose(turned[:, b, :], gate_rows[:, b, :], ident[:])
            columns = keep.tile([P, TARGET_HALVES, D + 1], F32, align_bytes=64, name="gate_columns")
            nc.gpsimd.memset(columns[:, :, D:], LEAST_TOP)
            on_vector(
                out=columns[:, :, :D].rearrange("v h (b e) -> v h b e", e=2),
                in_=turned[:, :, CLEARED:].rearrange("v b (e h) -> v h b e", h=TARGET_HALVES),
            )
            own = columns[:, :, PLAIN_LIST]
            steps = keep.tile([P, 4, TARGET_HALVES], F32, name="factor_steps")
            top, size, half_sign, guarded = (steps[:, i, :] for i in range(4))
            nc.vector.tensor_reduce(top, columns[:], mybir.AxisListType.X, MAX, apply_absolute_value=True)
            nc.vector.scalar_tensor_tensor(size, own, -1.0, own, MULT, MAX)
            nc.vector.tensor_scalar(half_sign, own, 0.0, 0.5, mybir.AluOpType.is_ge, mybir.AluOpType.subtract)
            nc.vector.scalar_tensor_tensor(guarded, top, LEAST_SHARE, size, MULT, MAX)
            along_lists = [P, TARGET_HALVES, D]
            signed = keep.tile(along_lists, F32, align_bytes=64, name="signed", tag="after_division")
            nc.vector.tensor_tensor(signed[:], columns[:, :, :D], half_sign.unsqueeze(2).to_broadcast(along_lists), MULT)
            inverse = keep.tile([P, TARGET_HALVES], F32, align_bytes=64, name="inverse", tag="after_inverse")
            nc.vector.reciprocal(inverse[:], guarded)
            factor = keep.tile([P, TARGET_HALVES], F32, name="factor")
            nc.vector.scalar_tensor_tensor(factor[:], half_sign, 2.0, guarded, MULT, MULT)
            divided = keep.tile(along_lists, F32, align_bytes=64, name="divided", tag="after_spreading")
            nc.vector.scalar_tensor_tensor(
                divided[:], signed[:], 2.0, inverse[:].unsqueeze(2).to_broadcast(along_lists), MULT, MULT
            )
            spread = words("ratios", len(GATED) * V)
            for first, b, copy in ((0, 2, on_scalar), (2, 3, on_scalar), (4, 4, on_vector)):
                in_bank = GATED[first : first + 2]
                acc = bank(b, [P, len(in_bank) * V], "spread")
                for i, d in enumerate(in_bank):
                    for vh in range(TARGET_HALVES):
                        column = divided[:, vh, d : d + 1].to_broadcast([P, P])
                        nc.tensor.transpose(acc[:, block(i * TARGET_HALVES + vh)], column, ident[:])
                copy(out=part(spread, first, len(in_bank)), in_=acc[:])
            return {d: part(spread, i) for i, d in enumerate(GATED)}, factor

        def project_first_group():
            width = 2 * HALF
            first = words("x_stage_first", width, "after_division")
            free = words("x_stage_free", width)
            second = words("x_stage_second", width, "after_spreading")
            behind_pass_1 = x_raw[1].rearrange("p j t -> p (j t)")
            third, fourth = (behind_pass_1[:, i * width : (i + 1) * width] for i in (1, 2))
            areas = ((first, free), (first, second), (third, fourth))
            for g in range(PASSES):
                x_operands[g] = operand_tiles(f"x{g}", T, None, "after_inverse" if g == 0 else None)
            h = keep.tile([P, T], F32, name="h0")
            accs = [bank(b, [P, n.stop - n.start], "h_acc") for b, n in zip((0, 1, 5), FIRST_PARTS)]

            def stage_x(g):
                for area, nodes, copy in zip(areas[g], NODE_HALVES, (on_vector, on_scalar)):
                    interleave(copy, as_grouped(area), x_raw[g][:, :, nodes])

            def quantize_x(g, half):
                codes, scales = x_operands[g]
                nodes = NODE_HALVES[half]
                quantize(nc, codes[:, nodes], scales[:, nodes], as_grouped(areas[g][half]))

            for g in range(PASSES - 1):
                stage_x(g)
                quantize_x(g, 0)
                quantize_x(g, 1)
                if g == 0:
                    area = x_raw[0][:, 0, NODE_HALVES[0]]
                    stage_slice(on_vector, area, 0, 0)
                    project_slice(0, 0, area, accs)
            interleave(on_vector, as_grouped(third)[:, :P, :], x_raw[2][:, :, :P])
            interleave(on_scalar, as_grouped(fourth), x_raw[2][:, :, HALF:])
            interleave(on_vector, as_grouped(third)[:, P:, :], x_raw[2][:, :, P:HALF])
            area = spare_and_loads[:, :PART]
            stage_slice(on_vector, area, 0, 1)
            quantize_x(2, 0)
            project_slice(0, 1, area, accs)
            area = last_loads[:, J * T - 2 * SCALAR_COLUMNS : J * T - 2 * SCALAR_COLUMNS + PART]
            raw = w1_raw[0, 2].rearrange("p (j c) -> p j c", j=J)
            for copy, columns in ((on_scalar, slice(0, SCALAR_COLUMNS)), (on_vector, slice(SCALAR_COLUMNS, P))):
                interleave(copy, as_grouped(area)[:, columns, :], raw[:, :, columns])
            x_codes, x_scales = x_operands[2]
            second_part, last_part = FIRST_PARTS[1:]
            quantize(nc, x_codes[:, second_part], x_scales[:, second_part], as_grouped(part(fourth, 0)))
            project_slice(0, 2, area, accs, None, lambda: quantize(nc, x_codes[:, last_part], x_scales[:, last_part], as_grouped(part(fourth, 1))))
            for acc, nodes, relu in zip(accs, FIRST_PARTS, (nc.vector.tensor_relu, relu_on_scalar, relu_on_scalar)):
                relu(out=h[:, nodes], in_=acc[:])
            return h

        ratios, factor = spread_ratios()
        h = {0: project_first_group()}
        h_accs, staged = {}, {}

        def stage(c, g, area):
            staged[c, g] = area
            stage_slice(on_scalar, area, c, g)

        def project(c, g, scales_tag=None):
            if g == 0:
                h_accs[c] = [bank({1: 2, 2: 0, 3: 6}[c] + i, [P, HALF], "h_acc") for i in range(2)]
            project_slice(c, g, staged[c, g], h_accs[c], scales_tag)

        def finish_h(c):
            h[c] = keep.tile([P, T], F32, name=f"h{c}")
            for acc, nodes in zip(h_accs[c], NODE_HALVES):
                relu_on_scalar(h[c][:, nodes], acc[:])

        sums, added, waiting = {}, {}, []

        def add_half(c, vh, term):
            k = added.get((c, vh), 0)
            nc.tensor.matmul(sums[c][vh], term, ident[:], start=(k == 0), stop=(k == D - 1), is_transpose=True)
            added[c, vh] = k + 1

        def add(c, term):
            if c not in sums:
                waiting.append((c, term))
                return
            for vh in range(TARGET_HALVES):
                add_half(c, vh, term[:, block(vh)])

        def offsets(d, vh=None):
            return lists[d][:] if vh is None else lists[d][:, vh * LIST_COLUMNS : (vh + 1) * LIST_COLUMNS]

        def pick(picked, c, d, vh=None):
            nc.scalar.activation(picked, h[c][:].indirect(offsets(d, vh)), COPY)
            return picked

        def fused(term, c, d):
            nc.vector.tensor_tensor(term, h[c][:].indirect(offsets(d)), ratios[d], MULT)
            add(c, term)

        def multiply(picked, c, d):
            term = words(f"term{c}_{d}", V)
            nc.vector.tensor_tensor(term, picked, ratios[d], MULT)
            add(c, term)

        def after_staging(c, g, i):
            return part(w1_raw[c, g], i)

        stage(1, 0, x_raw[2][:, 1, NODE_HALVES[1]])
        project(1, 0, "w1_0_2_scales")
        round_a = words("round_a", 4 * PART, "w1_0_2_codes")
        stage(1, 1, part(round_a, 0))
        stage(1, 2, part(round_a, 1))
        stage(2, 0, part(round_a, 2))
        plain = pick(words("plain0", V), 0, PLAIN_LIST)
        stage(2, 1, part(round_a, 3))
        fused(words("term0_0", V), 0, 0)
        project(1, 1)
        fused(after_staging(1, 1, 0), 0, 1)
        project(1, 2)
        finish_h(1)
        add(0, plain)
        fused(after_staging(1, 2, 0), 0, 3)
        project(2, 0)
        fused(after_staging(2, 0, 0), 0, 4)
        fused(after_staging(2, 0, 1), 0, 5)
        project(2, 1)

        round_b = words("round_b", 3 * PART, "w1_1_2_codes")
        stage(2, 2, part(round_b, 0))
        stage(3, 0, part(round_b, 1))
        plain = pick(after_staging(2, 1, 1), 1, PLAIN_LIST)
        picked = pick(after_staging(3, 0, 1), 1, 3)
        stage(3, 1, part(round_b, 2))
        fused(after_staging(2, 1, 0), 1, 0)
        project(2, 2)
        first_sums = [bank(2 + vh, [P, 2 * P], "first_sums") for vh in range(TARGET_HALVES)]
        third_sums = [bank(4 + vh, [P, P], "third_sums") for vh in range(TARGET_HALVES)]
        sums[0] = [t[:, :P] for t in first_sums]
        sums[1] = [t[:, P:] for t in first_sums]
        sums[2] = [t[:] for t in third_sums]
        for c, term in waiting:
            add(c, term)
        finish_h(2)
        fused(after_staging(2, 2, 0), 1, 1)
        fused(after_staging(2, 2, 1), 1, 4)
        project(3, 0)
        add(1, plain)
        fused(after_staging(3, 0, 0), 1, 5)
        multiply(picked, 1, 3)
        project(3, 1)

        round_c = words("round_c", 3 * PART, "w1_2_2_codes")
        stage(3, 2, part(round_c, 0))
        plain = pick(part(round_c, 1), 2, PLAIN_LIST)
        picked = pick(part(round_c, 2), 2, 3)
        fused(after_staging(3, 1, 0), 2, 0)
        project(3, 2)
        finish_h(3)
        fused(after_staging(3, 2, 0), 2, 1)
        add(2, plain)
        fused(after_staging(3, 2, 1), 2, 4)
        multiply(picked, 2, 3)
        fused(staged[3, 2], 2, 5)

        def scaled_on_scalar(out, in_, vh):
            nc.scalar.activation(out, in_, COPY, scale=factor[:, vh : vh + 1])

        def scaled_on_vector(out, in_, vh):
            nc.vector.tensor_scalar(out, in_, factor[:, vh : vh + 1], None, MULT)

        def round_sums(scaled, vh, acc, first_group, groups, us=slice(0, 2)):
            zt = zt_words[vh].bitcast(BF16).rearrange("v (u p e) -> v u p e", u=2, e=2)
            partitions = slice(GROUP_PARTITIONS * first_group, GROUP_PARTITIONS * (first_group + groups))
            scaled(zt[:, us, partitions, :], acc.rearrange("v (p u e) -> v u p e", u=2, e=2)[:, us], vh)

        last = GROUPS - 1
        last_sums = [bank(vh, [P, P], "last_sums") for vh in range(TARGET_HALVES)]
        sums[last] = [t[:] for t in last_sums]
        plain = pick(words("plain3", V), last, PLAIN_LIST)
        zt_both = words("zt", TARGET_HALVES * PART, "w1_3_1_scales")
        zt_words = [part(zt_both, vh) for vh in range(TARGET_HALVES)]
        for vh in range(TARGET_HALVES):
            round_sums(scaled_on_scalar, vh, first_sums[vh][:], 0, 2)
        picked_last = words("picked_last", TARGET_HALVES * PART)
        for vh in range(TARGET_HALVES):
            for i, d in enumerate((4, 5)):
                pick(part(picked_last, vh)[:, block(i)], last, d, vh)
        for vh in range(TARGET_HALVES):
            round_sums(scaled_on_scalar, vh, third_sums[vh][:], 2, 1)
        fused(words("term3_0", V), last, 0)
        add(last, plain)
        fused(words("term3_1", V), last, 1)
        last_terms = []
        for vh in range(TARGET_HALVES):
            term = words(f"term3_3_{vh}", P)
            nc.vector.tensor_tensor(term, h[last][:].indirect(offsets(3, vh)), ratios[3][:, block(vh)], MULT)
            add_half(last, vh, term)
            last_terms.append(words(f"term3_45_{vh}", PART))
            for i, d in enumerate((4, 5)):
                term = last_terms[vh][:, block(i)]
                nc.vector.tensor_tensor(term, part(picked_last, vh)[:, block(i)], ratios[d][:, block(vh)], MULT)
                add_half(last, vh, term)

        w2_areas = (last_terms[0], part(picked_last, 1))
        interleave(on_vector, as_grouped(w2_areas[1]), w2_raw[:, :, block(1)])
        w2_codes, w2_scales = operand_tiles("w2", N, "term3_45_1")
        z_codes, z_scales = operand_tiles("z", V)
        round_sums(scaled_on_scalar, 0, sums[last][0], last, 1)
        for u in range(2):
            round_sums(scaled_on_vector, 1, sums[last][1], last, 1, slice(u, u + 1))
        interleave(on_scalar, as_grouped(w2_areas[0]), w2_raw[:, :, block(0)])
        for mb in (1, 0):
            quantize(nc, w2_codes[:, block(mb)], w2_scales[:, block(mb)], as_grouped(w2_areas[mb]))

        for vh, (copy, out_bank) in enumerate(((on_scalar, 6), (on_vector, 4))):
            back = bank(2 + vh, [P, 2, P], "back")
            for u in range(2):
                nc.tensor.transpose(back[:, u, :], zt_words[vh][:, block(u)], ident[:])
            z_words = keep.tile([P, P, 2], F32, align_bytes=64, name=f"z_words{vh}")
            on_scalar(out=z_words[:], in_=back[:].rearrange("p u v -> p v u"))
            targets = block(vh)
            quantize(nc, z_codes[:, targets], z_scales[:, targets], as_grouped(z_words[:].rearrange("p v u -> p (v u)")))
            for mb in range(N // P):
                acc = bank(out_bank + mb, [P, P], "out_acc")
                nc.tensor.matmul_mx(
                    out=acc[:],
                    lhsT=w2_codes[:, block(mb)].bitcast(FP8X4),
                    lhsT_scale=w2_scales[:, block(mb)],
                    rhs=z_codes[:, targets].bitcast(FP8X4),
                    rhs_scale=z_scales[:, targets],
                    start=True,
                    stop=True,
                )
                res = keep.tile([P, P], F32, name=f"res{vh}_{mb}")
                (on_scalar, copy)[mb](out=res[:], in_=acc[:])
                nc.sync.dma_start(out=out[block(mb), targets], in_=res[:])
